import numpy as np, ml_dtypes
CORES = [35,38,43,46]
N = 4
import mx_ref
BF = ml_dtypes.bfloat16
def gentries(a):
    return np.ascontiguousarray(a.reshape(8, 16, -1).transpose(0, 2, 1)).reshape(8, -1)
def gtable(e):
    e = np.asarray(e); return np.ascontiguousarray(e.reshape(8, -1, 16).transpose(0, 2, 1)).reshape(128, -1).astype(np.int32)
def gcols(t, e):
    v = np.concatenate([t.reshape(8, 16, -1, 4), np.zeros((8, 16, 1, 4), BF)], axis=2)
    return np.ascontiguousarray(np.stack([v[g][:, e[g]] for g in range(8)])).reshape(128, -1)
def tile(rs):
    return np.stack(rs, axis=2).reshape(128, -1).astype(BF)
def pick(q, e):
    c = np.concatenate([q[0].reshape(128, -1, 4), np.zeros((128, 1, 4), np.uint8)], axis=1); s = np.concatenate([q[1], np.ones((16, 1), np.uint8)], axis=1)
    return (np.ascontiguousarray(c[:, e].reshape(128, -1)), np.ascontiguousarray(s[:, e]))
def join(*qs):
    return (np.concatenate([q[0] for q in qs], axis=1), np.concatenate([q[1] for q in qs], axis=1))
def put(q, e, v):
    c, s = q[0].reshape(128, -1, 4).copy(), q[1].copy(); c[:, e] = v[0].reshape(128, -1, 4); s[:, e] = v[1]
    return (c.reshape(128, -1), s)
def pk(c, s):
    return (np.ascontiguousarray(c), mx_ref.live(s))
def emit(q):
    return q[0], q[1]
def packed(v, rng):
    q = [mx_ref.quantize(np.ascontiguousarray(v[r])) for r in range(N)]
    return np.stack([a for a, b in q]), np.stack([mx_ref.plane(b, rng) for a, b in q])
def values_of_codes():
    e, c = np.zeros((128, 128, 4), np.float32), np.zeros((128, 2, 4), np.uint8)
    e[np.arange(128), np.arange(128), 0] = 1
    c[:127, :, 0] = np.arange(256).reshape(2, 128).T[:127]
    return mx_ref.matmul(mx_ref.quantize(e.reshape(128, 512).astype(BF)), (c.reshape(128, 8), np.full((16, 2), 127, np.uint8))).T.reshape(-1).astype(np.float64)
CODE_VALUE, SCALE_VALUE = values_of_codes(), 2.0 ** (np.arange(256) - 127.0)
def decode(q):
    return (CODE_VALUE[q[0]].reshape(16, 8, -1, 4) * SCALE_VALUE[q[1]][:, None, :, None] + 0.0).reshape(128, -1).astype(np.float32)
def f(rng, *shape):
    return mx_ref.flush((rng.standard_normal(shape, dtype=np.float32) * np.exp2(rng.integers(-2, 3, shape[:-1] + (1,)))).astype(BF))
def wide(rng, *shape, cols=0):
    v = rng.standard_normal(shape, dtype=np.float32) * np.exp2(rng.integers(-12, 13, shape)).astype(np.float32)
    if cols: v *= np.repeat(np.exp2(rng.integers(-cols, cols + 1, shape[:-2] + (1, shape[-1] // 4))) * (rng.random(shape[:-2] + (1, shape[-1] // 4)) > 0.0625), 4, axis=-1).astype(np.float32)
    return mx_ref.flush(v.astype(BF))
C, H = 384, 192
MASK = [1, 2, 3]
def numbers_of(rng):
    return {"x": np.array(f(rng, N, 128, 4 * C)), "u": np.array(f(rng, N, 128, 512)), "v": np.array(f(rng, N, 128, 512))}
def stored(l, k):
    return {"gl": np.stack([gtable(l[r]) for r in range(N)]), "gk": np.stack([gtable(k[r]) for r in range(N)])}
def lists(rng):
    e = np.tile(np.arange(C), (N, 8, 1))
    return stored(rng.permuted(e, axis=2), rng.permuted(e, axis=2))
def layers(rng, still=[]):
    w = np.array(f(rng, N, 128, 2048)).reshape(N, 8, 16, 4, 8, 16, 4)
    for i in still:
        w[:, :, i] = 0
        w[:, :, :, :, :, i] = 0
    return w
def weights(rng, w):
    c, p = packed(np.ascontiguousarray(w).reshape(N, 128, 2048), rng)
    return {"wc": c, "ws": p}
def setup_inputs(rng):
    return {**numbers_of(rng), **lists(rng), **weights(rng, layers(rng))}
def setup_inputs_ties(rng):
    d = numbers_of(rng)
    o = rng.permutation(N)
    k = rng.integers(-1, 2, (N, 8, C, 2)).astype(np.float32)
    k[o[1]] = 1
    k[o[2]] = -1
    x = d["x"].reshape(N, 8, 16, C, 4)
    x[:, :, 0] = 0
    x[:, :, 0, :, :2] = k.astype(BF)
    a = np.exp2(rng.integers(-3, 4, 8).astype(np.float32))[None, :, None]
    x[:, :, 8:] = 0
    x[:, :, 8, :, 0] = (-1.125 * a).astype(BF)
    x[:, :, 10, :, 0] = (-0.0703125 * a).astype(BF)
    c = np.ones(N, np.float32)
    c[o[0]] = 0
    u = d["u"].reshape(N, 128, 128, 4)
    for t in range(2):
        u[:, :, t::16] = 0
        for h in range(0, 128, 16): u[:, h, h + t, t] = c.astype(BF)
    w = layers(rng, [0])
    w[:, :, :, :, :, 8:] = 0
    for g in range(8):
        w[:, g, 8, 0, g, 8, 0] = -28.0
        for b in range(4): w[:, g, 10, b, g, 9, 0] = -2.0 ** (b - 5)
    return {"x": x.reshape(N, 128, 4 * C), "u": u.reshape(N, 128, 512), "v": d["v"], **stored(rng.integers(0, C, (N, 8, C)), rng.integers(0, C, (N, 8, C))), **weights(rng, w)}
def setup_inputs_near(rng):
    d = numbers_of(rng)
    o = rng.permutation(N) % 2
    k = np.where(o == 0, 2.0 ** -30, 1.0).astype(np.float32)
    x = d["x"].astype(np.float32).reshape(N, 8, 16, C, 4)
    x[:, :, :8] = 0
    s = rng.integers(-1, 2, (N, 8, C, 2)) * k[:, None, None, None]
    x[:, :, 0, :, :2] = 1.125 * s
    x[:, :, 1, :, :2] = -1.25 * s
    x[:, :, 3, :, :2] = rng.choice([-1.0, 1.0], (N, 8, C, 2)) * 2.0 ** -30
    x[:, :, 5] = 2.0 ** -30
    for r in range(N):
        for g in rng.permutation(8)[:4]: x[r, g, 0, rng.integers(C), 0] = 2.0 ** 30 * rng.choice([-1.0, 1.0])
    u = d["u"].reshape(N, 128, 128, 4)
    w = layers(rng, range(8))
    for t in range(2):
        u[:, :, t::16] = 0
        for h in range(0, 128, 16):
            u[:, h, h + t, t] = (1.125 * k).astype(BF)
            u[:, h + 1, h + t, t] = k.astype(BF)
            u[:, h + 2, h + t, t] = k.astype(BF)
        for g in range(8):
            w[:, g, 3, t, g, 2, t] = 2.0 ** -8
            w[:, g, 3, t, g, 4, t] = 32.0
    return {"x": x.reshape(N, 128, 4 * C).astype(BF), "u": u.reshape(N, 128, 512), "v": d["v"], **lists(rng), **weights(rng, w)}
def setup_inputs_odd(rng):
    d = numbers_of(rng)
    x = (1.0 + (2 * rng.integers(0, 64, (N, 16, 8, C, 4)) + 1) * 2.0 ** -7) * np.exp2(-rng.integers(0, 7, (N, 16, 8, C, 4)).astype(np.float64)) * rng.choice([-1.0, 1.0], (N, 16, 8, C, 4))
    x[:, :, 0, :, 0] = 1.96875 * 2.0 ** 8 * rng.choice([-1.0, 1.0], (N, 16, C))
    x[:, ::2, 1, :, :2] = rng.integers(7, 10, (N, 8, C, 2)) * 2.0 ** -8
    x[:, ::2, 2, :, :2] = 2.0 ** -5
    u = d["u"].reshape(N, 16, 8, 128, 4)
    for t in range(2):
        u[:, :, :, t::16] = 0
        for g in range(8):
            u[:, 2 * g, 1, 16 * g + t, t] = 1.0
            u[:, 2 * g, 2, 16 * g + t, t] = -1.0
    return {"x": x.astype(np.float32).reshape(N, 128, 4 * C).astype(BF), "u": u.reshape(N, 128, 512), "v": d["v"], **lists(rng), **weights(rng, layers(rng, [0, 1, 2, 8]))}
def setup_inputs_ends(rng):
    d = numbers_of(rng)
    x = np.zeros((N, 128, C, 4))
    u = d["u"].astype(np.float32).reshape(N, 128, 128, 4)
    v = d["v"].astype(np.float32)
    w = np.zeros((N, 128, 4, 128, 4), np.float32)
    o, e = rng.permutation(N) % 4, rng.permutation(N) % 4
    i = np.arange(128)
    def amount(large, *n):
        return (0.9 + 0.1 * rng.random(n)) * 2.0 ** 30 if large else (1.0 + 0.125 * rng.integers(0, 8, n)) * 2.0 ** -30
    for r in range(N):
        large = o[r] < 2
        if o[r] == 3: x[r] = d["x"][r].astype(np.float32).reshape(128, C, 4)[:, :1]
        else: x[r] = -amount(large, 128, C, 4) * (0.5 if large else 1.0)
        if o[r] == 1: x[r] *= rng.choice([-1.0, 1.0], (1, C, 1))
        x[r, 7::8] = 2.0 ** -30
        for t in range(2):
            h = rng.permutation(8)
            c = np.where(h < 2, 0.0, h % 2 * 2.0 - 1.0)[None, :, None]
            if o[r] == 3: u[r, :, t::16] *= np.abs(c).astype(np.float32)
            else: u[r, :, t::16] = c * amount(large, 128, 8, 4)
        v[r] = rng.choice([-1.0, 1.0], (128, 512)) * amount(large, 128, 512)
        k = np.array([1.0, 2.0, 4.0])[rng.permutation(8) % 3][i // 16]
        k[7::8] = 0
        if o[r] == 2: k = np.where(i % 8 == 7, 2.0 ** 8, 2.0 ** -8)
        for b in range(4): w[r, i, b, i, b] = k
    both = []
    for z in (e, (e + rng.integers(1, 4)) % 4):
        a = rng.integers(0, C, (N, 8, C))
        a[z == 0] = C - 1
        a[z == 1] = 0
        a[z == 2] = rng.integers(0, 2, a[z == 2].shape) * (C - 1)
        both.append(a)
    return {"x": x.astype(np.float32).reshape(N, 128, 4 * C).astype(BF), "u": u.reshape(N, 128, 512).astype(BF), "v": v.astype(BF), **stored(*both), **weights(rng, w.astype(BF))}
def setup_inputs_spread(rng):
    d = setup_inputs(rng)
    d["x"] = wide(rng, N, 128, 4 * C, cols=6)
    return d
def check_inputs(d):
    b = []
    for k in ("x", "u", "v"):
        a = np.abs(d[k].astype(np.float32))
        if not (np.isfinite(a).all() and ((a == 0) | (a >= 2.0 ** -30) & (a <= 2.0 ** 30)).all()): b.append("a value of " + k)
    for k in ("gl", "gk"):
        if not ((d[k] >= 0) & (d[k] < C)).all(): b.append("an entry of " + k)
    none, least, most = [emit(mx_ref.quantize(np.full((128, 16), k, np.float32).astype(BF)))[1][0, 0] for k in (0.0, 2.0 ** -8, 2.0 ** 8)]
    for r in range(N):
        if ((d["wc"][r] == 0x7F) | (d["wc"][r] == 0xFF)).any(): b.append("wc: a code that is no number")
        s = mx_ref.live(d["ws"][r])
        if ((s != none) & ((s < least) | (s > most))).any(): b.append("ws: a scale out of range")
        if (((d["wc"][r].reshape(16, 8, 512, 4) & 0x7F) != 0) & (s == none)[:, None, :, None]).any(): b.append("wc: a code other than zero under the scale of zeros")
    return b
def at(t, e):
    return np.take_along_axis(t, e, axis=1)
def reference(x, u, v, gl, gk, wc, ws):
    qu = [mx_ref.quantize(u[r]) for r in range(N)]
    lay = [pk(wc[r], ws[r]) for r in range(N)]
    left, right = [gentries(gl[r]) for r in range(N)], [gentries(gk[r]) for r in range(N)]
    now = [x[r] for r in range(N)]
    for mask in MASK:
        point, made, sent, turn = [], [], [], []
        for r in range(N):
            l, k = left[r], right[r]
            s = mx_ref.matmul(qu[r], mx_ref.quantize(now[r]))
            b = s[::16] > 0
            turn.append(s[1::16][:, :H] < 0)
            state, down = b, []
            for t in range(3):
                a, c = at(state, l), at(state, k)
                down.append(np.where(a, l, np.where(c, k, np.arange(C))))
                state = b ^ (a & ~c)
            o = at(down[0], at(down[1], down[2]))
            z = (gcols(now[r], o).astype(np.float32) + gcols(now[r], at(l, o)).astype(np.float32)) * np.float32(0.5)
            q = mx_ref.quantize(z.astype(BF))
            h = tile([mx_ref.matmul(pick(lay[r], np.arange(128 * b, 128 * b + 128)), q) * np.float32(0.03125) for b in range(4)])
            point.append(o)
            made.append(h)
            sent.append(decode(mx_ref.quantize(h)).astype(BF))
        for r in range(N):
            p = r ^ mask
            l, k = left[r], right[r]
            m = at(point[p], k)
            add = np.concatenate([gcols(sent[p], m[:, :H]), gcols(made[r], m[:, H:])], axis=1)
            now[r] = (now[r].astype(np.float32) + add.astype(np.float32)).astype(BF)
            t = np.concatenate([turn[r], turn[r]], axis=1)
            left[r] = np.where(t, np.roll(k, H, axis=1), l)
            right[r] = np.where(t, np.roll(l, H, axis=1), k)
    y, lr = np.zeros((N, 128, C), np.float32), np.zeros((N, 8, 2 * C), np.float32)
    oc, osc = np.zeros((N, 128, 4 * C), np.uint8), np.zeros((N, 16, C), np.uint8)
    for r in range(N):
        q = mx_ref.quantize(now[r])
        y[r] = mx_ref.matmul(mx_ref.quantize(v[r]), q)
        lr[r] = np.concatenate([left[r], right[r]], axis=1)
        oc[r], osc[r] = emit(q)
    return {"y": y, "lr": lr, "oc": oc, "osc": osc}

@@ -1,0 +1,474 @@
+from concourse.bass import DstId, RemoteDMATransfer
+from concourse.mybir import dt, AluOpType, ActivationFunctionType
+
+OP = AluOpType
+AF = ActivationFunctionType
+C, HC, K24, K12 = 384, 192, 24, 12
+MASK = [1, 2, 3]
+ROUNDS = 3
+WGT = 1024.0
+CYCLE, WAKE, LOOK = 0.00083, 0.12, 0.5
+BOOST = (3.0, 0.0)
+
+BF, F32, I32, U16, COD, PLN = "bfloat16", "float32", "int32", "uint16", "float8_e4m3fn_x4", "uint8"
+
+
+def _buffers():
+    s = {}
+
+    def sb(dtype, n, *names):
+        for name in names:
+            s[name] = ("sbuf", [128, n], dtype)
+    sb(BF, 4 * C, "x0", "x1", "x2", "x3", "pp", "zt")
+    sb(BF, C, "h0", "h1", "h2", "h3")
+    sb(BF, 4 * HC, "ht")
+    sb(COD, C, "xq", "zq")
+    sb(PLN, C, "xs", "zs")
+    sb(COD, HC, "hq", "dq1", "dq2", "dq3")
+    sb(PLN, HC, "hs", "ds1", "ds2", "ds3")
+    sb(BF, 512, "ut", "vt")
+    sb(COD, 128, "uq", "vq")
+    sb(PLN, 128, "us", "vs")
+    sb(COD, 256, "uq2")
+    sb(PLN, 256, "us2")
+    sb(COD, 512, "wq", "eq")
+    sb(PLN, 512, "wp", "es")
+    sb(BF, 128, "one", "eye")
+    sb(BF, 2048, "et")
+    sb(I32, 16, "ulist", "ddi", "ddm")
+    sb(U16, 16, "ulist16")
+    sb(BF, 16, "wga", "wgb")
+    sb(BF, C, "wgt")
+    sb(F32, C, "sel", "jj", "rst", "nat")
+    sb(I32, K24, "pi", "pm", "q16")
+    sb(F32, K24, "cw")
+    sb(F32, 4, "last", "fac")
+    sb(I32, 2 * K24, "gin")
+    sb(F32, 2 * K24, "lk0", "lk1", "lk2", "lk3")
+    sb(U16, 2 * K24, "lu0", "lu1", "lu2", "lu3")
+    sb(U16, K24, "la0", "la1", "la2", "la3")
+    sb(F32, 3 * K24, "pr")
+    sb(F32, K24, "dif", "tt", "ud", "xd")
+    sb(BF, C, "b", "ga", "c0", "c3", "c1", "yy", "gb", "xx", "raw0", "raw1", "raw2")
+    sb(BF, 2 * C, "tx")
+    sb(F32, 9 * K24, "sm0", "sm1", "sm2")
+    sb(U16, K24, "d0", "d1", "d2", "of0", "of1", "of2", "of3", "mu", "kin1", "kin2", "kin3")
+    sb(U16, K12, "min1", "min2", "min3")
+    sb(F32, C, "dn", "qn", "on", "om", "ow", "mn", "mw", "yo")
+    sb(BF, HC, "ts", "tw")
+    sb(F32, 2 * C, "lro")
+    for i in range(8):
+        s["ps%d" % i] = ("psum", [128, 512], F32)
+    return s
+
+
+SCRATCH = _buffers()
+SEMAPHORES = ["cv", "cs", "ct", "cg"]
+SEMAPHORES += ["i%d" % i for i in range(7)]
+SEMAPHORES += ["pa%d_%d" % (r, h) for r in (1, 2, 3) for h in (0, 1)]
+SEMAPHORES += [n + "%d" % r for r in (1, 2, 3) for n in ("rk", "rm", "rc", "rs", "lk", "lm", "lc", "ls")]
+SEMAPHORES += ["o%d" % i for i in range(20)]
+
+COMPUTE = {"v": "cv", "s": "cs", "t": "ct", "g": "cg"}
+
+
+def rank_program(g, core, T, topo):
+    rank = T.rank_of(core)
+    if rank is None:
+        return
+    queue = {"v": g.vector, "s": g.scalar, "t": g.tensor, "y": g.sync, "g": g}
+    seen = {}
+
+    def A(name, lo=0, hi=None, step=1):
+        t = T[name]
+        n = t.shape[1]
+        hi = n if hi is None else hi
+        ap = t[:, lo:hi] if step == 1 else t[:, lo:hi:step]
+        return (ap, [(name, lo, hi, step)])
+
+    def U8(name, lo, hi):
+        return (T[name][:, lo:hi].bitcast(dt.uint8), [(name, lo, hi, 1)])
+
+    def IND(win, off, a, b):
+        n = T[win].shape[1]
+        return (T[win][:, 0:n].indirect(T[off][:, a:b]), [(win, 0, n, 1), (off, a, b, 1)])
+
+    nodes = []
+    boost = [0.0]
+
+    def clash(p, q):
+        if p[0] >= q[1] or q[0] >= p[1]:
+            return False
+        return not (p[2] == 4 and q[2] == 4 and (p[0] - q[0]) % 4)
+
+    def add(q, call, outs, ins, sem, inc, busy, late, slow, after=()):
+        reads = [r for _, regs in ins for r in regs]
+        writes = [r for _, regs in outs for r in regs]
+        me = len(nodes)
+        deps = {n: True for n in after}
+        for w, regs in ((False, reads), (True, writes)):
+            for name, lo, hi, step in regs:
+                bank = name[:2] == "ps"
+                for (reg, rw, n) in seen.get(name, ()):
+                    other = nodes[n]
+                    if not (w or rw or (bank and other["q"] != q)):
+                        continue
+                    if bank or clash(reg, (lo, hi, step)):
+                        strong = other["q"] != q or other["slow"] or rw
+                        deps[n] = deps.get(n, False) or strong
+        for w, regs in ((False, reads), (True, writes)):
+            for name, lo, hi, step in regs:
+                seen.setdefault(name, []).append(((lo, hi, step), w, me))
+        nodes.append({"q": q, "call": call, "deps": deps, "sem": sem, "inc": inc, "busy": busy, "late": late, "slow": slow,
+                      "boost": boost[0]})
+        return me
+
+    def width(regs):
+        name, lo, hi, step = regs[0]
+        return (hi - lo + step - 1) // step
+
+    def narrow(regs):
+        return SCRATCH[regs[0][0]][2] == BF
+
+    def op(q, call, outs, ins, pairs=False, flat=False, product=False):
+        n = width(outs[0][1])
+        if product:
+            busy = (n + 16) * CYCLE * 1.4
+        elif flat:
+            busy = 0.012 + 0.00022 * 1.25 * width(ins[0][1])
+        elif any(len(a[1]) > 1 for a in ins):
+            busy = 0.06 + n * CYCLE * 1.6
+        elif q == "s":
+            busy = 0.08 + n * CYCLE * 1.25
+        elif q == "g":
+            busy = 0.15 + 2 * n * CYCLE * 1.25
+        else:
+            both = all(narrow(a[1]) for a in ins + outs)
+            per = 2.0 if pairs and ins[0][1][0][0][:2] != "ps" else 0.5 if both and not pairs else 1.0
+            busy = max(64, n * per) * CYCLE * 1.25
+        add(q, lambda: call().then_inc(T.sem[COMPUTE[q]], 1), outs, ins, COMPUTE[q], 1, busy, 0.0, False)
+
+    def load(q, out, in_, sem, **kw):
+        add(q, lambda: queue[q].dma_start(out[0], in_[0], **kw).then_inc(T.sem[sem], 16), [out], [in_], sem, 16,
+            0.6 if q == "g" else 0.06, 2.3, True)
+
+    def X(ap):
+        return (ap, [])
+
+    def send(out, in_, dst, rsem, lsem, late):
+        rid, pid = topo.addr(dst)[:2]
+        n = len(topo.engines(core, dst))
+        me = add("g", lambda: g.remote_dma(out_ap=out[0], in_ap=in_[0], remote_sem=T.sem[rsem], local_sem=T.sem[lsem],
+                                           pid=pid, routing_id=rid, dma_engine_mask=topo.mask(core, dst)),
+                 [], [in_], lsem, n, 0.6, late, True)
+        add("far", None, [out], [], rsem, len(topo.engines(dst, core)), 0.0, 0.0, True, (me,))
+
+    def plan():
+        after = [[] for _ in nodes]
+        for i, n in enumerate(nodes):
+            for d, strong in n["deps"].items():
+                after[d].append((i, strong))
+        way = [0.0] * len(nodes)
+        for i in range(len(nodes) - 1, -1, -1):
+            own = nodes[i]["busy"] + nodes[i]["late"]
+            way[i] = max([own] + [(own + WAKE if strong else 0.0) + way[j] for j, strong in after[i]])
+        way = [w + n["boost"] for w, n in zip(way, nodes)]
+        left = [len(n["deps"]) for n in nodes]
+        ready = [0.0] * len(nodes)
+        free = {q: 0.0 for q in list(queue) + ["far"]}
+        avail = {q: [] for q in free}
+        for i, n in enumerate(nodes):
+            if not left[i]:
+                avail[n["q"]].append(i)
+        done = []
+        while len(done) < len(nodes):
+            best = None
+            for q, c in avail.items():
+                if not c:
+                    continue
+                now = min(ready[i] for i in c)
+                if q != "far":
+                    now = max(free[q], now)
+                i = max((i for i in c if ready[i] <= now + 1e-9), key=lambda i: (way[i], -i))
+                for j in sorted((j for j in c if ready[j] > now and way[j] > way[i]), key=lambda j: -way[j]):
+                    if ready[j] - now < LOOK * (now + nodes[i]["busy"] - ready[j]):
+                        i, now = j, ready[j]
+                        break
+                if best is None or now < best[0]:
+                    best = (now, q, i)
+            now, q, i = best
+            avail[q].remove(i)
+            free[q] = now + nodes[i]["busy"]
+            done.append(i)
+            end = now + nodes[i]["busy"] + nodes[i]["late"]
+            for j, strong in after[i]:
+                ready[j] = max(ready[j], end + WAKE if strong else now)
+                left[j] -= 1
+                if not left[j]:
+                    avail[nodes[j]["q"]].append(j)
+        return done
+
+    def issue(sequence):
+        known = {q: {} for q in list(queue) + ["far"]}
+        total, value, clock = {}, {}, {}
+        for i in sequence:
+            n = nodes[i]
+            best = {}
+            for d, strong in n["deps"].items():
+                sem = nodes[d]["sem"]
+                if strong and known[n["q"]].get(sem, 0) < value[d] and (sem not in best or value[best[sem]] < value[d]):
+                    best[sem] = d
+            if n["call"] is not None:
+                for sem, d in best.items():
+                    if any(s2 != sem and clock[d2].get(sem, 0) >= value[d] for s2, d2 in best.items()):
+                        continue
+                    queue[n["q"]].wait_ge(T.sem[sem], value[d])
+                    k = known[n["q"]]
+                    for s, v in list(clock[d].items()) + [(sem, value[d])]:
+                        if v > k.get(s, 0):
+                            k[s] = v
+                n["call"]()
+            total[n["sem"]] = total.get(n["sem"], 0) + n["inc"]
+            value[i] = total[n["sem"]]
+            clock[i] = dict(known[n["q"]]) if n["call"] is not None else {}
+        for sem in sorted(total):
+            if known["g"].get(sem, 0) < total[sem]:
+                g.wait_ge(T.sem[sem], total[sem])
+
+    def ts(out, a, s1, o1, s2=None, o2=None):
+        k1 = s1[0] if isinstance(s1, tuple) else s1
+        ins = [a] + ([s1] if isinstance(s1, tuple) else [])
+        if o2 is None:
+            op("v", lambda: g.vector.tensor_scalar(out[0], a[0], k1, None, o1), [out], ins)
+        else:
+            op("v", lambda: g.vector.tensor_scalar(out[0], a[0], k1, s2, o1, o2), [out], ins)
+
+    def tt(out, a, b, o):
+        op("v", lambda: g.vector.tensor_tensor(out[0], a[0], b[0], o), [out], [a, b], pairs=True)
+
+    def vcopy(out, a):
+        op("v", lambda: g.vector.tensor_copy(out[0], a[0]), [out], [a])
+
+    def fill(out, value):
+        op("v", lambda: g.vector.memset(out[0], value), [out], [])
+
+    def act(out, a, func=AF.Copy, scale=1.0, bias=0.0):
+        more = {k: v for k, v, d in (("bias", bias, 0.0), ("scale", scale, 1.0)) if v != d}
+        op("s", lambda: g.scalar.activation(out[0], a[0], func, **more), [out], [a])
+
+    def scan(out, d0, d1):
+        op("v", lambda: g.vector.tensor_tensor_scan(out[0], d0[0], d1[0], 0.0, OP.mult, OP.add), [out], [d0, d1])
+
+    def quant(code, plane, a):
+        op("v", lambda: g.vector.quantize_mx(code[0], plane[0], a[0]), [code, plane], [a], flat=True)
+
+    def mm(bank, lhs, lhs_s, a, rhs, rhs_s, lo, hi):
+        out, w, ws_ = A(bank, 0, hi - lo), A(lhs, a, a + 128), A(lhs_s, a, a + 128)
+        x, xs_ = A(rhs, lo, hi), A(rhs_s, lo, hi)
+        op("t", lambda: g.tensor.matmul_mx(out[0], w[0], ws_[0], x[0], xs_[0], True, True), [out], [w, ws_, x, xs_], product=True)
+
+    def iota(out, pattern, cm, base=0, small=False):
+        if small:
+            op("g", lambda: g.iota(out[0], pattern, base, cm, allow_small_or_imprecise_dtypes=True), [out], [])
+        else:
+            op("g", lambda: g.iota(out[0], pattern, base, cm), [out], [])
+
+    VIEW24, VIEW12 = (15, C, 16), (15, HC, 16)
+
+    load("y", A("ut"), X(T.u[:]), "i0")
+    load("s", A("gin", K24, 2 * K24), X(T.gk[:]), "i1")
+    load("y", A("x0"), X(T.x[:]), "i2")
+    iota(A("ulist"), [[1, 2], [16, 8]], 0)
+    iota(A("ddi"), [[1, 16]], -1, base=128)
+    iota(A("pi"), [[0, K24]], 1)
+    iota(A("q16"), [[16, K24]], 0)
+    load("g", A("gin", 0, K24), X(T.gl[:]), "i3")
+    load("y", U8("wq", 0, 512), X(T.wc[:]), "i4")
+    load("y", A("wp"), X(T.ws[:]), "i5")
+    load("y", A("vt"), X(T.v[:]), "i6")
+
+    vcopy(A("ulist16"), A("ulist"))
+    ts(A("ddm"), A("ddi"), 15, OP.bitwise_and)
+    ts(A("wga"), A("ddm"), 1, OP.is_equal, WGT, OP.mult)
+    ts(A("wgb"), A("ddm"), 1, OP.is_gt)
+    tt(A("wgt", 0, 16), A("wga"), A("wgb"), OP.add)
+    ts(A("sel", 0, 16), A("ddm"), 0, OP.is_equal)
+    ts(A("pm"), A("pi"), 15, OP.bitwise_and)
+    tt(A("cw"), A("pm"), A("q16"), OP.add)
+    ts(A("last", 0, 1), A("pm", 0, 1), 15, OP.is_equal)
+    ts(A("fac", 0, 1), A("last", 0, 1), 1.0 - 1.0 / WGT, OP.mult, 1.0 / WGT, OP.add)
+    ts(A("fac", 1, 2), A("last", 0, 1), 1.0 - WGT ** -2, OP.mult, WGT ** -2, OP.add)
+    fill(A("one"), 1.0)
+    fill(A("et"), 0.0)
+    for name in ("wgt", "sel"):
+        have = 16
+        while have < C:
+            more = min(have, C - have)
+            act(A(name, have, have + more), A(name, 0, more))
+            have += more
+    vcopy(A("lu0", K24, 2 * K24), A("gin", K24, 2 * K24))
+
+    def partner(r):
+        return T.cores[rank ^ MASK[r - 1]]
+
+    def send_children(r):
+        send(A("kin%d" % r), A("lu%d" % (r - 1), K24, 2 * K24), partner(r), "rk%d" % r, "lk%d" % r, 2.0)
+
+    def lists_of(n, first):
+        L = "lk%d" % n
+        if first:
+            vcopy(A("lu%d" % n, 0, K24), A("gin", 0, K24))
+            vcopy(A(L), A("gin"))
+        else:
+            vcopy(A("lu%d" % n), A(L))
+        for t in range(4):
+            ts(A("la%d" % t), A(L, 0, K24), 4.0, OP.mult, float(t), OP.add)
+
+    def pairs_of(n):
+        L = "lk%d" % n
+        tt(A("pr", 0, K24), A(L, K24, 2 * K24), A(L, 0, K24), OP.subtract)
+        tt(A("pr", K24, 2 * K24), A("cw"), A(L, K24, 2 * K24), OP.subtract)
+        tt(A("pr", 2 * K24, 3 * K24), A(L, K24, 2 * K24), A("cw"), OP.subtract)
+        tt(A("dif", 0, K12), A(L, 3 * K12, 4 * K12), A(L, 0, K12), OP.subtract)
+        tt(A("dif", K12, K24), A(L, 2 * K12, 3 * K12), A(L, K12, 2 * K12), OP.subtract)
+
+    quant(A("uq"), A("us"), A("ut"))
+    src = (T.uq[:, 0:128].bitcast(dt.uint32).indirect(T.ulist16[:, 0:16]), [("uq", 0, 128, 1), ("ulist16", 0, 16, 1)])
+    vcopy((T.uq2[:, 0:256].bitcast(dt.uint32), [("uq2", 0, 256, 1)]), src)
+    act(A("us2"), (T.us[:, 0:128].indirect(T.ulist16[:, 0:16]), [("us", 0, 128, 1), ("ulist16", 0, 16, 1)]))
+    iota(A("jj"), [[0, K24], [1, 16]], 0, small=True)
+    iota(A("nat"), [[1, C]], 0, small=True)
+    send_children(1)
+    op("g", lambda: g.affine_select(T.eye[:], T.one[:], [[-1, 128]], OP.is_equal, 0.0, 0, 1), [A("eye")], [A("one")])
+
+    def signs(x, h):
+        lo, hi = HC * h, HC * (h + 1)
+        quant(A("xq", lo, hi), A("xs", lo, hi), A(x, 4 * lo, 4 * hi))
+        mm("ps%d" % (5 - h), "uq2", "us2", 0, "xq", "xs", lo, hi)
+        if h == 0:
+            mm("ps6", "uq2", "us2", 128, "xq", "xs", lo, hi)
+        ts(A("b", lo, hi), A("ps%d" % (5 - h), 0, HC), 0.0, OP.is_gt)
+
+    act(A("rst"), A("jj"), AF.Sign)
+    lists_of(0, True)
+    signs("x0", 1)
+
+    def select(s, raw, L):
+        def B(i, n=1):
+            return A("sm" + s, K24 * i, K24 * (i + n))
+        tt(B(0), raw, raw, OP.mult)
+        for i, least in enumerate((2.3, 6.2, 12.2)):
+            ts(B(1 + i), B(0), A("fac", 1, 2), OP.mult, least, OP.is_gt)
+        tt(B(4, 3), B(1, 3), A("pr"), OP.mult)
+        tt(B(7), B(4), B(5), OP.add)
+        tt(B(8), B(6), A(L, 0, K24), OP.add)
+        tt(A("d" + s), B(7), B(8), OP.add)
+
+    for r in range(1, ROUNDS + 1):
+        x, xn = "x%d" % (r - 1), "x%d" % r
+        lu, L, Ln = "lu%d" % (r - 1), "lk%d" % (r - 1), "lk%d" % r
+        fl = (lu, 0, K24)
+        fk = (lu, K24, 2 * K24)
+
+        signs(x, 0)
+        pairs_of(r - 1)
+        for h in (0, 1):
+            for t in range(4):
+                act(A("pp", 4 * HC * h + t, 4 * HC * (h + 1), 4), IND(x, "la%d" % t, K12 * h, K12 * (h + 1)))
+            load("g", A("pp", 4 * HC * h, 4 * HC * (h + 1)), A(x, 4 * HC * h, 4 * HC * (h + 1)), "pa%d_%d" % (r, h), accum_op=OP.add)
+        act(A("ga", 0, HC), IND("b", lu, 0, K12), AF.Identity, scale=-3.0, bias=3.0)
+        ts(A("ga", HC, C), IND("b", lu, K12, K24), -3.0, OP.mult, 3.0, OP.add)
+        tt(A("tx", HC, C), IND("b", lu, K24 + K12, 2 * K24), A("ga", HC, C), OP.add)
+        tt(A("tx", 0, HC), IND("b", lu, K24, K24 + K12), A("ga", 0, HC), OP.add)
+        act(A("c3"), A("tx", 0, C), AF.Relu, scale=-3.0, bias=3.0)
+        ts(A("c0"), A("tx", 0, C), 0.0, OP.is_equal)
+        tt(A("yy"), IND("c0", *fk), A("tx", 0, C), OP.subtract)
+        tt(A("tx", C, 2 * C), IND("c3", *fl), A("yy"), OP.add)
+        ts(A("c1"), A("tx", C, 2 * C), 0.0, OP.is_equal)
+        act(A("gb"), IND("c1", *fl), AF.Copy, scale=3.0)
+        tt(A("xx"), IND("c1", *fk), A("gb"), OP.add)
+        if r == 1:
+            for b in range(4):
+                act(A("et", 512 * b + b, 512 * (b + 1), 4), A("eye"))
+            quant(A("eq"), A("es"), A("et"))
+        act(A("ts"), A("ps6", 0, HC), AF.Sign, scale=-1.0)
+        scan(A("raw0"), A("wgt"), A("tx", 0, C))
+        select("0", A("raw0", *VIEW24), L)
+        act(A("dn"), IND("nat", "d0", 0, K24))
+        scan(A("raw1"), A("wgt"), A("tx", C, 2 * C))
+        select("1", A("raw1", *VIEW24), L)
+        act(A("qn"), IND("dn", "d1", 0, K24))
+        scan(A("raw2"), A("wgt"), A("xx"))
+        tt(A("xd"), A("raw2", *VIEW24), A("raw0", *VIEW24), OP.subtract)
+        select("2", A("xd"), L)
+        tt(A("om"), IND("qn", "d2", 0, K24), A("sel"), OP.mult)
+        act(A("on"), IND("qn", "d2", 0, K24))
+        scan(A("ow"), A("rst"), A("om"))
+        for t in (2, 3, 0, 1):
+            ts(A("of%d" % t), A("ow", *VIEW24), 4.0, OP.mult, float(t), OP.add)
+        for h in (0, 1):
+            boost[0] = BOOST[h]
+            for t in range(4):
+                z, p = A("zt", 4 * HC * h + t, 4 * HC * (h + 1), 4), IND("pp", "of%d" % t, K12 * h, K12 * (h + 1))
+                if t < 2 - h:
+                    ts(z, p, 0.5, OP.mult)
+                else:
+                    act(z, p, AF.Copy, scale=0.5)
+            quant(A("zq", HC * h, HC * (h + 1)), A("zs", HC * h, HC * (h + 1)), A("zt", 4 * HC * h, 4 * HC * (h + 1)))
+            for b in range(4):
+                mm("ps%d" % (4 * h + b), "wq", "wp", 128 * b, "zq", "zs", HC * h, HC * (h + 1))
+        boost[0] = 0.0
+        tt(A("mn"), IND("on", "kin%d" % r, 0, K24), A("sel"), OP.mult)
+        scan(A("mw"), A("rst"), A("mn"))
+        vcopy(A("mu"), A("mw", *VIEW24))
+        send(A("min%d" % r), A("mu", K12, K24), partner(r), "rm%d" % r, "lm%d" % r, 2.0)
+        for b in range(4):
+            act(A("h%d" % b, 0, HC), A("ps%d" % b, 0, HC), scale=0.03125)
+        for b in (0, 2):
+            ts(A("h%d" % b, HC, C), A("ps%d" % (4 + b), 0, HC), 0.03125, OP.mult)
+            act(A("h%d" % (b + 1), HC, C), A("ps%d" % (5 + b), 0, HC), scale=0.03125)
+            vcopy(A("ht", b, 4 * HC, 4), IND("h%d" % b, "mu", 0, K12))
+            act(A("ht", b + 1, 4 * HC, 4), IND("h%d" % (b + 1), "mu", 0, K12))
+        quant(A("hq"), A("hs"), A("ht"))
+        send(U8("dq%d" % r, 0, HC), U8("hq", 0, HC), partner(r), "rc%d" % r, "lc%d" % r, 3.0)
+        send(A("ds%d" % r), A("hs"), partner(r), "rs%d" % r, "ls%d" % r, 2.7)
+        for b in range(4):
+            tt(A(xn, 4 * HC + b, 8 * HC, 4), IND("h%d" % b, "min%d" % r, 0, K12), A(x, 4 * HC + b, 8 * HC, 4), OP.add)
+        if r < ROUNDS:
+            signs(xn, 1)
+        else:
+            quant(A("xq", HC, C), A("xs", HC, C), A(xn, 4 * HC, 8 * HC))
+        scan(A("tw"), A("wgt", 0, HC), A("ts"))
+        for i in range(2):
+            ts(A("tt", K12 * i, K12 * (i + 1)), A("tw", *VIEW12), A("fac", 0, 1), OP.mult, 0.5, OP.is_gt)
+        tt(A("ud"), A("tt"), A("dif"), OP.mult)
+        tt(A(Ln, 0, K24), A(L, 0, K24), A("ud"), OP.add)
+        tt(A(Ln, 3 * K12, 4 * K12), A(L, 3 * K12, 4 * K12), A("ud", 0, K12), OP.subtract)
+        tt(A(Ln, 2 * K12, 3 * K12), A(L, 2 * K12, 3 * K12), A("ud", K12, K24), OP.subtract)
+        if r < ROUNDS:
+            lists_of(r, False)
+            send_children(r + 1)
+        else:
+            quant(A("vq"), A("vs"), A("vt"))
+            mm("ps4", "vq", "vs", 0, "xq", "xs", HC, C)
+            act(A("yo", HC, C), A("ps4", 0, HC))
+            vcopy(A("lu%d" % r), A(Ln))
+            act(A("lro"), IND("nat", "lu%d" % r, 0, 2 * K24))
+            load("y", X(T.oc[:, 4 * HC:4 * C]), U8("xq", HC, C), "o0")
+            for k in range(4):
+                load("y", X(T.osc[4 * k:4 * k + 4, HC:C]), (T.xs[32 * k:32 * k + 4, HC:C], [("xs", HC, C, 1)]), "o%d" % (1 + k))
+            load("y", X(T.y[:, HC:C]), A("yo", HC, C), "o5")
+            for k in range(8):
+                load("y", X(T.lr[k:k + 1, :]), (T.lro[16 * k:16 * k + 1, :], [("lro", 0, 2 * C, 1)]), "o%d" % (6 + k))
+        for b in range(4):
+            mm("ps%d" % b, "eq", "es", 128 * b, "dq%d" % r, "ds%d" % r, 0, HC)
+            tt(A(xn, b, 4 * HC, 4), A("ps%d" % b, 0, HC), A(x, b, 4 * HC, 4), OP.add)
+
+    quant(A("xq", 0, HC), A("xs", 0, HC), A("x3", 0, 4 * HC))
+    mm("ps5", "vq", "vs", 0, "xq", "xs", 0, HC)
+    load("s", X(T.oc[:, 0:4 * HC]), U8("xq", 0, HC), "o14")
+    for k in range(4):
+        load("y" if k < 2 else "s", X(T.osc[4 * k:4 * k + 4, 0:HC]), (T.xs[32 * k:32 * k + 4, 0:HC], [("xs", 0, HC, 1)]), "o%d" % (15 + k))
+    vcopy(A("yo", 0, HC), A("ps5", 0, HC))
+    load("y", X(T.y[:, 0:HC]), A("yo", 0, HC), "o19")
+    issue(plan())

@@ -6,11 +6,22 @@ AF = ActivationFunctionType
 C, HC, K24, K12 = 384, 192, 24, 12
 MASK = [1, 2, 3]
 ROUNDS = 3
-WGT = 1024.0
-CYCLE, WAKE, LOOK = 0.00083, 0.12, 0.5
-BOOST = (3.0, 0.0)
+BIG = 512.0
+LOW = -4096.0
+CYCLE, FACTOR, GATHER, PRODUCT, WAKE, LOOK = 0.00083, 1.25, 1.56, 1.5, 0.1, 0.5
+LOCAL, ADDING, SMALL, CODES, PLANE = 1.6, 3.8, 1.6, 2.2, 2.0
+PIECES = ((0, 128, 64), (128, 256, 192), (256, 384, 320))
+MEANS = ((0, 96, 192, 240),)
+VMEANS = (240, 312, 384)
+OWN = 384
+POINT = 128
+COPIES = "vsvs" "vsvs" "vsvs"
+PARTS = "vsvs"
+BOOST = 2.0
+PASSES = 4
 
-BF, F32, I32, U16, COD, PLN = "bfloat16", "float32", "int32", "uint16", "float8_e4m3fn_x4", "uint8"
+BF, F16, F32, I32, U16, COD, PLN = "bfloat16", "float16", "float32", "int32", "uint16", "float8_e4m3fn_x4", "uint8"
+WRAP = F16
 
 
 def _buffers():
@@ -19,8 +30,7 @@ def _buffers():
     def sb(dtype, n, *names):
         for name in names:
             s[name] = ("sbuf", [128, n], dtype)
-    sb(BF, 4 * C, "x0", "x1", "x2", "x3", "pp", "zt")
-    sb(BF, C, "h0", "h1", "h2", "h3")
+    sb(BF, 4 * C, "x0", "x1", "x2", "x3", "xc", "pp", "zt", "h")
     sb(BF, 4 * HC, "ht")
     sb(COD, C, "xq", "zq")
     sb(PLN, C, "xs", "zs")
@@ -33,29 +43,32 @@ def _buffers():
     sb(PLN, 256, "us2")
     sb(COD, 512, "wq", "eq")
     sb(PLN, 512, "wp", "es")
-    sb(BF, 128, "one", "eye")
+    sb(BF, 128, "one")
     sb(BF, 2048, "et")
-    sb(I32, 16, "ulist", "ddi", "ddm")
+    sb(I32, 16, "ulist")
     sb(U16, 16, "ulist16")
-    sb(BF, 16, "wga", "wgb")
-    sb(BF, C, "wgt")
-    sb(F32, C, "sel", "jj", "rst", "nat")
     sb(I32, K24, "pi", "pm", "q16")
+    sb(I32, 3, "pq")
+    sb(U16, K24, "pm16")
+    sb(F32, 32, "pos", "pa", "pb")
+    sb(BF, 32, "pat")
+    sb(BF, C, "w16", "w4", "nat")
     sb(F32, K24, "cw")
-    sb(F32, 4, "last", "fac")
+    sb(F32, 8, "col")
     sb(I32, 2 * K24, "gin")
     sb(F32, 2 * K24, "lk0", "lk1", "lk2", "lk3")
     sb(U16, 2 * K24, "lu0", "lu1", "lu2", "lu3")
-    sb(U16, K24, "la0", "la1", "la2", "la3")
-    sb(F32, 3 * K24, "pr")
-    sb(F32, K24, "dif", "tt", "ud", "xd")
-    sb(BF, C, "b", "ga", "c0", "c3", "c1", "yy", "gb", "xx", "raw0", "raw1", "raw2")
-    sb(BF, 2 * C, "tx")
-    sb(F32, 9 * K24, "sm0", "sm1", "sm2")
-    sb(U16, K24, "d0", "d1", "d2", "of0", "of1", "of2", "of3", "mu", "kin1", "kin2", "kin3")
-    sb(U16, K12, "min1", "min2", "min3")
-    sb(F32, C, "dn", "qn", "on", "om", "ow", "mn", "mw", "yo")
-    sb(BF, HC, "ts", "tw")
+    sb(U16, 4 * K24, "la", "of")
+    sb(F32, 3 * K24, "hd", "hm0", "hm1", "hm2", "ho0", "ho1", "ho2")
+    sb(F32, K24, "dif", "tt", "ud", "thr", "ref1", "m2", "ref2", "cl", "e2")
+    sb(BF, C, "b", "ga", "gb", "t0", "c0", "gc", "yy", "t1", "ge", "gf", "ln", "dn", "qn", "on", "mn")
+    sb(WRAP, C, "t0w", "t1w", "gew", "gfw", "lw", "ow", "mw")
+    sb(U16, K24, "d0", "d1", "d2", "kin1", "kin2", "kin3")
+    sb(U16, K12, "mu")
+    sb(U16, 4 * K12, "mo", "min1", "min2", "min3")
+    sb(F32, C, "yo")
+    sb(BF, HC, "ts")
+    sb(WRAP, HC, "tw")
     sb(F32, 2 * C, "lro")
     for i in range(8):
         s["ps%d" % i] = ("psum", [128, 512], F32)
@@ -64,8 +77,8 @@ def _buffers():
 
 SCRATCH = _buffers()
 SEMAPHORES = ["cv", "cs", "ct", "cg"]
-SEMAPHORES += ["i%d" % i for i in range(7)]
-SEMAPHORES += ["pa%d_%d" % (r, h) for r in (1, 2, 3) for h in (0, 1)]
+SEMAPHORES += ["i%d" % i for i in range(8)]
+SEMAPHORES += ["pa%d_%d" % (r, h) for r in (1, 2, 3) for h in range(5)]
 SEMAPHORES += [n + "%d" % r for r in (1, 2, 3) for n in ("rk", "rm", "rc", "rs", "lk", "lm", "lc", "ls")]
 SEMAPHORES += ["o%d" % i for i in range(20)]
 
@@ -89,23 +102,27 @@ def rank_program(g, core, T, topo):
     def U8(name, lo, hi):
         return (T[name][:, lo:hi].bitcast(dt.uint8), [(name, lo, hi, 1)])
 
-    def IND(win, off, a, b):
-        n = T[win].shape[1]
-        return (T[win][:, 0:n].indirect(T[off][:, a:b]), [(win, 0, n, 1), (off, a, b, 1)])
+    def IND(win, off, a, b, lo=0, hi=None):
+        hi = T[win].shape[1] if hi is None else hi
+        return (T[win][:, lo:hi].indirect(T[off][:, a:b]), [(win, lo, hi, 1), (off, a, b, 1)])
 
     nodes = []
     boost = [0.0]
+    early = [True]
+    behind = []
 
     def clash(p, q):
         if p[0] >= q[1] or q[0] >= p[1]:
             return False
-        return not (p[2] == 4 and q[2] == 4 and (p[0] - q[0]) % 4)
+        return not (p[2] == q[2] > 1 and (p[0] - q[0]) % p[2])
 
     def add(q, call, outs, ins, sem, inc, busy, late, slow, after=()):
         reads = [r for _, regs in ins for r in regs]
         writes = [r for _, regs in outs for r in regs]
         me = len(nodes)
         deps = {n: True for n in after}
+        while behind:
+            deps[behind.pop()] = False
         for w, regs in ((False, reads), (True, writes)):
             for name, lo, hi, step in regs:
                 bank = name[:2] == "ps"
@@ -120,7 +137,7 @@ def rank_program(g, core, T, topo):
             for name, lo, hi, step in regs:
                 seen.setdefault(name, []).append(((lo, hi, step), w, me))
         nodes.append({"q": q, "call": call, "deps": deps, "sem": sem, "inc": inc, "busy": busy, "late": late, "slow": slow,
-                      "boost": boost[0]})
+                      "boost": boost[0], "early": early[0]})
         return me
 
     def width(regs):
@@ -128,29 +145,29 @@ def rank_program(g, core, T, topo):
         return (hi - lo + step - 1) // step
 
     def narrow(regs):
-        return SCRATCH[regs[0][0]][2] == BF
+        return SCRATCH[regs[0][0]][2] in (BF, F16, U16)
 
     def op(q, call, outs, ins, pairs=False, flat=False, product=False):
         n = width(outs[0][1])
         if product:
-            busy = (n + 16) * CYCLE * 1.4
+            busy = (n + 16) * CYCLE * PRODUCT
         elif flat:
-            busy = 0.012 + 0.00022 * 1.25 * width(ins[0][1])
+            busy = 0.012 + 0.00022 * FACTOR * width(ins[0][1])
         elif any(len(a[1]) > 1 for a in ins):
-            busy = 0.06 + n * CYCLE * 1.6
+            busy = 0.06 + n * CYCLE * GATHER
         elif q == "s":
-            busy = 0.08 + n * CYCLE * 1.25
+            busy = 0.06 + n * CYCLE * FACTOR
         elif q == "g":
-            busy = 0.15 + 2 * n * CYCLE * 1.25
+            busy = 0.15 + 2 * n * CYCLE * FACTOR
         else:
-            both = all(narrow(a[1]) for a in ins + outs)
+            both = all(narrow(a[1]) for a in ins + outs if width(a[1]) > 1)
             per = 2.0 if pairs and ins[0][1][0][0][:2] != "ps" else 0.5 if both and not pairs else 1.0
-            busy = max(64, n * per) * CYCLE * 1.25
+            busy = max(64, n * per) * CYCLE * FACTOR
         add(q, lambda: call().then_inc(T.sem[COMPUTE[q]], 1), outs, ins, COMPUTE[q], 1, busy, 0.0, False)
 
-    def load(q, out, in_, sem, **kw):
-        add(q, lambda: queue[q].dma_start(out[0], in_[0], **kw).then_inc(T.sem[sem], 16), [out], [in_], sem, 16,
-            0.6 if q == "g" else 0.06, 2.3, True)
+    def load(q, out, in_, sem, late=LOCAL, after=(), **kw):
+        return add(q, lambda: queue[q].dma_start(out[0], in_[0], **kw).then_inc(T.sem[sem], 16), [out], [in_], sem, 16,
+                   0.5 if q == "g" else 0.06, late, True, after)
 
     def X(ap):
         return (ap, [])
@@ -160,53 +177,52 @@ def rank_program(g, core, T, topo):
         n = len(topo.engines(core, dst))
         me = add("g", lambda: g.remote_dma(out_ap=out[0], in_ap=in_[0], remote_sem=T.sem[rsem], local_sem=T.sem[lsem],
                                            pid=pid, routing_id=rid, dma_engine_mask=topo.mask(core, dst)),
-                 [], [in_], lsem, n, 0.6, late, True)
+                 [], [in_], lsem, n, 0.4, late, True)
         add("far", None, [out], [], rsem, len(topo.engines(dst, core)), 0.0, 0.0, True, (me,))
 
     def plan():
+        count = len(nodes)
+        before = [[(d, nodes[d]["late"] + WAKE if strong else 0.0) for d, strong in n["deps"].items()] for n in nodes]
         after = [[] for _ in nodes]
-        for i, n in enumerate(nodes):
-            for d, strong in n["deps"].items():
-                after[d].append((i, strong))
-        way = [0.0] * len(nodes)
-        for i in range(len(nodes) - 1, -1, -1):
-            own = nodes[i]["busy"] + nodes[i]["late"]
-            way[i] = max([own] + [(own + WAKE if strong else 0.0) + way[j] for j, strong in after[i]])
-        way = [w + n["boost"] for w, n in zip(way, nodes)]
-        left = [len(n["deps"]) for n in nodes]
-        ready = [0.0] * len(nodes)
-        free = {q: 0.0 for q in list(queue) + ["far"]}
-        avail = {q: [] for q in free}
-        for i, n in enumerate(nodes):
-            if not left[i]:
-                avail[n["q"]].append(i)
-        done = []
-        while len(done) < len(nodes):
-            best = None
-            for q, c in avail.items():
-                if not c:
-                    continue
-                now = min(ready[i] for i in c)
-                if q != "far":
-                    now = max(free[q], now)
-                i = max((i for i in c if ready[i] <= now + 1e-9), key=lambda i: (way[i], -i))
-                for j in sorted((j for j in c if ready[j] > now and way[j] > way[i]), key=lambda j: -way[j]):
-                    if ready[j] - now < LOOK * (now + nodes[i]["busy"] - ready[j]):
-                        i, now = j, ready[j]
-                        break
-                if best is None or now < best[0]:
-                    best = (now, q, i)
-            now, q, i = best
-            avail[q].remove(i)
-            free[q] = now + nodes[i]["busy"]
-            done.append(i)
-            end = now + nodes[i]["busy"] + nodes[i]["late"]
-            for j, strong in after[i]:
-                ready[j] = max(ready[j], end + WAKE if strong else now)
-                left[j] -= 1
-                if not left[j]:
-                    avail[nodes[j]["q"]].append(j)
-        return done
+        for i in range(count):
+            for d, wait in before[i]:
+                after[d].append((i, wait))
+
+        def lay(urgency, needs, feeds, tail):
+            start, left = [0.0] * count, [len(n) for n in needs]
+            ready = list(tail)
+            taken = {q: [] for q in list(queue) + ["far"]}
+            free = [i for i in range(count) if not left[i]]
+            while free:
+                i = min(free, key=lambda i: (urgency[i], i))
+                free.remove(i)
+                busy, at, slots = nodes[i]["busy"], ready[i], taken[nodes[i]["q"]]
+                k = 0
+                while k < len(slots) and slots[k][0] < at + busy - 1e-9:
+                    at = max(at, slots[k][1])
+                    k += 1
+                if busy:
+                    slots.insert(k, (at, at + busy))
+                start[i] = at
+                for j, wait in feeds[i]:
+                    ready[j] = max(ready[j], at + busy + wait)
+                    left[j] -= 1
+                    if not left[j]:
+                        free.append(j)
+            return start
+        way = [0.0] * count
+        for i in range(count - 1, -1, -1):
+            way[i] = nodes[i]["busy"] + max([nodes[i]["late"]] + [wait + way[j] for j, wait in after[i]])
+        urgency, best = [-w - n["boost"] for w, n in zip(way, nodes)], None
+        for _ in range(PASSES):
+            urgency = [i - 1e6 if n["early"] else u for i, (u, n) in enumerate(zip(urgency, nodes))]
+            start = lay(urgency, before, after, [0.0] * count)
+            end = max(t + n["busy"] + n["late"] for t, n in zip(start, nodes))
+            if best is None or end < best[0]:
+                best = (end, start)
+            back = lay([-t - n["busy"] for t, n in zip(start, nodes)], after, before, [n["late"] for n in nodes])
+            urgency = [-t - n["busy"] for t, n in zip(back, nodes)]
+        return sorted(range(count), key=lambda i: (best[1][i], i))
 
     def issue(sequence):
         known = {q: {} for q in list(queue) + ["far"]}
@@ -236,12 +252,12 @@ def rank_program(g, core, T, topo):
                 g.wait_ge(T.sem[sem], total[sem])
 
     def ts(out, a, s1, o1, s2=None, o2=None):
-        k1 = s1[0] if isinstance(s1, tuple) else s1
-        ins = [a] + ([s1] if isinstance(s1, tuple) else [])
+        k1, k2 = (s[0] if isinstance(s, tuple) else s for s in (s1, s2))
+        ins = [a] + [s for s in (s1, s2) if isinstance(s, tuple)]
         if o2 is None:
             op("v", lambda: g.vector.tensor_scalar(out[0], a[0], k1, None, o1), [out], ins)
         else:
-            op("v", lambda: g.vector.tensor_scalar(out[0], a[0], k1, s2, o1, o2), [out], ins)
+            op("v", lambda: g.vector.tensor_scalar(out[0], a[0], k1, k2, o1, o2), [out], ins)
 
     def tt(out, a, b, o):
         op("v", lambda: g.vector.tensor_tensor(out[0], a[0], b[0], o), [out], [a, b], pairs=True)
@@ -256,8 +272,19 @@ def rank_program(g, core, T, topo):
         more = {k: v for k, v, d in (("bias", bias, 0.0), ("scale", scale, 1.0)) if v != d}
         op("s", lambda: g.scalar.activation(out[0], a[0], func, **more), [out], [a])
 
-    def scan(out, d0, d1):
-        op("v", lambda: g.vector.tensor_tensor_scan(out[0], d0[0], d1[0], 0.0, OP.mult, OP.add), [out], [d0, d1])
+    def times(q, out, a, factor=1.0):
+        if q == "s":
+            act(out, a, scale=factor)
+        elif factor == 1.0:
+            vcopy(out, a)
+        else:
+            ts(out, a, factor, OP.mult)
+
+    def scan(out, d0, d1, first, o0, o1):
+        op("v", lambda: g.vector.tensor_tensor_scan(out[0], d0[0], d1[0], first, o0, o1), [out], [d0, d1])
+
+    def wrap(out, data, lift, lo, hi):
+        scan(A(out, lo, hi), A(data, lo, hi), A(lift, lo, hi), LOW, OP.max, OP.add)
 
     def quant(code, plane, a):
         op("v", lambda: g.vector.quantize_mx(code[0], plane[0], a[0]), [code, plane], [a], flat=True)
@@ -273,96 +300,105 @@ def rank_program(g, core, T, topo):
         else:
             op("g", lambda: g.iota(out[0], pattern, base, cm), [out], [])
 
-    VIEW24, VIEW12 = (15, C, 16), (15, HC, 16)
+    def W16(name, lo=0, hi=C):
+        return A(name, lo + 15, hi, 16)
+
+    def W4(name, lo=0, hi=C):
+        return A(name, lo + 3, hi, 4)
+
+    def SLOT(name, i):
+        return A(name, i, 3 * K24, 3)
 
     load("y", A("ut"), X(T.u[:]), "i0")
     load("s", A("gin", K24, 2 * K24), X(T.gk[:]), "i1")
-    load("y", A("x0"), X(T.x[:]), "i2")
-    iota(A("ulist"), [[1, 2], [16, 8]], 0)
-    iota(A("ddi"), [[1, 16]], -1, base=128)
-    iota(A("pi"), [[0, K24]], 1)
-    iota(A("q16"), [[16, K24]], 0)
-    load("g", A("gin", 0, K24), X(T.gl[:]), "i3")
-    load("y", U8("wq", 0, 512), X(T.wc[:]), "i4")
-    load("y", A("wp"), X(T.ws[:]), "i5")
-    load("y", A("vt"), X(T.v[:]), "i6")
+    load("s", A("gin", 0, K24), X(T.gl[:]), "i3")
+    load("y", A("x0", 4 * HC, 4 * C), X(T.x[:, 4 * HC:4 * C]), "i2", late=LOCAL + 0.4)
+    first = load("y", A("x0", 0, 4 * HC), X(T.x[:, 0:4 * HC]), "i7", late=LOCAL + 0.8)
+    load("y", U8("wq", 0, 512), X(T.wc[:]), "i4", after=(first,))
+    load("y", A("wp"), X(T.ws[:]), "i5", after=(first,))
 
-    vcopy(A("ulist16"), A("ulist"))
-    ts(A("ddm"), A("ddi"), 15, OP.bitwise_and)
-    ts(A("wga"), A("ddm"), 1, OP.is_equal, WGT, OP.mult)
-    ts(A("wgb"), A("ddm"), 1, OP.is_gt)
-    tt(A("wgt", 0, 16), A("wga"), A("wgb"), OP.add)
-    ts(A("sel", 0, 16), A("ddm"), 0, OP.is_equal)
+    iota(A("pi"), [[0, K24]], 1)
+    iota(A("pos", 0, 16), [[1, 16]], 0, small=True)
+    iota(A("pos", 16, 32), [[0, 4], [1, 4]], 0, small=True)
+    iota(A("ulist"), [[1, 2], [16, 8]], 0)
+    iota(A("nat"), [[1, C]], 0, base=-HC, small=True)
+    iota(A("q16"), [[16, K24]], 0)
     ts(A("pm"), A("pi"), 15, OP.bitwise_and)
-    tt(A("cw"), A("pm"), A("q16"), OP.add)
-    ts(A("last", 0, 1), A("pm", 0, 1), 15, OP.is_equal)
-    ts(A("fac", 0, 1), A("last", 0, 1), 1.0 - 1.0 / WGT, OP.mult, 1.0 / WGT, OP.add)
-    ts(A("fac", 1, 2), A("last", 0, 1), 1.0 - WGT ** -2, OP.mult, WGT ** -2, OP.add)
+    ts(A("pq", 0, 1), A("pi", 0, 1), 15, OP.bitwise_and)
+    ts(A("pq", 1, 2), A("pi", 0, 1), 2, OP.logical_shift_right, 3, OP.bitwise_and)
+    ts(A("pq", 2, 3), A("pi", 0, 1), 3, OP.bitwise_and)
+    vcopy(A("col", 0, 3), A("pq"))
+    vcopy(A("pm16"), A("pm"))
+    for i in (1, 0):
+        ts(A("pa", 16 * i, 16 * i + 16), A("pos", 16 * i, 16 * i + 16), A("col", i, i + 1), OP.is_equal, 2 * BIG, OP.mult)
+        ts(A("pb", 16 * i, 16 * i + 16), A("pos", 16 * i, 16 * i + 16), A("col", i, i + 1), OP.is_le, -BIG, OP.mult)
+    tt(A("pat"), A("pa"), A("pb"), OP.add)
+    ts(A("pat", 15, 32, 4), A("pat", 15, 32, 4), -2 * BIG, OP.add)
+    act(A("w4"), IND("pat", "pm16", 0, K24, 16, 32))
+    act(A("w16"), IND("pat", "pm16", 0, K24, 0, 16))
+    vcopy(A("ulist16"), A("ulist"))
     fill(A("one"), 1.0)
-    fill(A("et"), 0.0)
-    for name in ("wgt", "sel"):
-        have = 16
-        while have < C:
-            more = min(have, C - have)
-            act(A(name, have, have + more), A(name, 0, more))
-            have += more
+    for b in range(4):
+        fill(A("et", 512 * b, 512 * (b + 1)), 0.0)
+    ts(A("col", 3, 4), A("pq", 2, 3), 4 * (BIG + HC), OP.add)
+    ts(A("col", 4, 5), A("pq", 2, 3), float(C), OP.mult, BIG + HC, OP.add)
+    tt(A("cw"), A("pm"), A("q16"), OP.add)
+    for name in ("hm0", "hm1", "hm2"):
+        fill(A(name), 0.0)
+    for b in range(4):
+        out = A("et", 512 * b + b, 512 * (b + 1), 4)
+        op("g", lambda out=out: g.affine_select(out[0], T.one[:], [[-1, 128]], OP.is_equal, 0.0, 0, 1), [out], [A("one")])
+    early[0] = False
     vcopy(A("lu0", K24, 2 * K24), A("gin", K24, 2 * K24))
+    vcopy(A("lu0", 0, K24), A("gin", 0, K24))
+    vcopy(A("lk0"), A("gin"))
 
     def partner(r):
         return T.cores[rank ^ MASK[r - 1]]
 
     def send_children(r):
-        send(A("kin%d" % r), A("lu%d" % (r - 1), K24, 2 * K24), partner(r), "rk%d" % r, "lk%d" % r, 2.0)
+        send(A("kin%d" % r), A("lu%d" % (r - 1), K24, 2 * K24), partner(r), "rk%d" % r, "lk%d" % r, SMALL)
 
-    def lists_of(n, first):
+    def lists_of(n):
         L = "lk%d" % n
-        if first:
-            vcopy(A("lu%d" % n, 0, K24), A("gin", 0, K24))
-            vcopy(A(L), A("gin"))
-        else:
-            vcopy(A("lu%d" % n), A(L))
-        for t in range(4):
-            ts(A("la%d" % t), A(L, 0, K24), 4.0, OP.mult, float(t), OP.add)
-
-    def pairs_of(n):
-        L = "lk%d" % n
-        tt(A("pr", 0, K24), A(L, K24, 2 * K24), A(L, 0, K24), OP.subtract)
-        tt(A("pr", K24, 2 * K24), A("cw"), A(L, K24, 2 * K24), OP.subtract)
-        tt(A("pr", 2 * K24, 3 * K24), A(L, K24, 2 * K24), A("cw"), OP.subtract)
+        act(A("ln"), IND("nat", "lu%d" % n, 0, K24))
+        wrap("lw", "ln", "w4", 0, C)
+        ts(A("la"), W4("lw"), 4.0, OP.mult, A("col", 3, 4), OP.add)
+        tt(SLOT("hd", 0), A(L, K24, 2 * K24), A("cw"), OP.subtract)
+        tt(SLOT("hd", 1), A("cw"), A(L, 0, K24), OP.subtract)
+        vcopy(SLOT("hd", 2), A(L, 0, K24))
         tt(A("dif", 0, K12), A(L, 3 * K12, 4 * K12), A(L, 0, K12), OP.subtract)
         tt(A("dif", K12, K24), A(L, 2 * K12, 3 * K12), A(L, K12, 2 * K12), OP.subtract)
 
     quant(A("uq"), A("us"), A("ut"))
-    src = (T.uq[:, 0:128].bitcast(dt.uint32).indirect(T.ulist16[:, 0:16]), [("uq", 0, 128, 1), ("ulist16", 0, 16, 1)])
-    vcopy((T.uq2[:, 0:256].bitcast(dt.uint32), [("uq2", 0, 256, 1)]), src)
-    act(A("us2"), (T.us[:, 0:128].indirect(T.ulist16[:, 0:16]), [("us", 0, 128, 1), ("ulist16", 0, 16, 1)]))
-    iota(A("jj"), [[0, K24], [1, 16]], 0, small=True)
-    iota(A("nat"), [[1, C]], 0, small=True)
+    for h in (0, 1):
+        src = (T.uq[:, 0:128].bitcast(dt.uint32).indirect(T.ulist16[:, 8 * h:8 * h + 8]), [("uq", 0, 128, 1), ("ulist16", 0, 16, 1)])
+        vcopy((T.uq2[:, 128 * h:128 * h + 128].bitcast(dt.uint32), [("uq2", 128 * h, 128 * h + 128, 1)]), src)
+        act(A("us2", 128 * h, 128 * h + 128),
+            (T.us[:, 0:128].indirect(T.ulist16[:, 8 * h:8 * h + 8]), [("us", 0, 128, 1), ("ulist16", 0, 16, 1)]))
+    early[0] = True
     send_children(1)
-    op("g", lambda: g.affine_select(T.eye[:], T.one[:], [[-1, 128]], OP.is_equal, 0.0, 0, 1), [A("eye")], [A("one")])
+    load("g", A("vt"), X(T.v[:]), "i6", after=(first,))
+    early[0] = False
 
     def signs(x, h):
         lo, hi = HC * h, HC * (h + 1)
         quant(A("xq", lo, hi), A("xs", lo, hi), A(x, 4 * lo, 4 * hi))
         mm("ps%d" % (5 - h), "uq2", "us2", 0, "xq", "xs", lo, hi)
         if h == 0:
+            ts(A("b", lo, hi), A("ps5", 0, HC), 0.0, OP.is_gt)
             mm("ps6", "uq2", "us2", 128, "xq", "xs", lo, hi)
-        ts(A("b", lo, hi), A("ps%d" % (5 - h), 0, HC), 0.0, OP.is_gt)
+        else:
+            act(A("b", lo, hi), A("ps4", 0, HC), AF.Sign)
 
-    act(A("rst"), A("jj"), AF.Sign)
-    lists_of(0, True)
+    def choose(s):
+        scan(A("ho" + s), A("hm" + s), A("hd"), 0.0, OP.mult, OP.add)
+        vcopy(A("d" + s), SLOT("ho" + s, 2))
+
+    lists_of(0)
     signs("x0", 1)
-
-    def select(s, raw, L):
-        def B(i, n=1):
-            return A("sm" + s, K24 * i, K24 * (i + n))
-        tt(B(0), raw, raw, OP.mult)
-        for i, least in enumerate((2.3, 6.2, 12.2)):
-            ts(B(1 + i), B(0), A("fac", 1, 2), OP.mult, least, OP.is_gt)
-        tt(B(4, 3), B(1, 3), A("pr"), OP.mult)
-        tt(B(7), B(4), B(5), OP.add)
-        tt(B(8), B(6), A(L, 0, K24), OP.add)
-        tt(A("d" + s), B(7), B(8), OP.add)
+    for b in range(4):
+        quant(A("eq", 128 * b, 128 * b + 128), A("es", 128 * b, 128 * b + 128), A("et", 512 * b, 512 * b + 512))
 
     for r in range(1, ROUNDS + 1):
         x, xn = "x%d" % (r - 1), "x%d" % r
@@ -371,89 +407,100 @@ def rank_program(g, core, T, topo):
         fk = (lu, K24, 2 * K24)
 
         signs(x, 0)
-        pairs_of(r - 1)
-        for h in (0, 1):
-            for t in range(4):
-                act(A("pp", 4 * HC * h + t, 4 * HC * (h + 1), 4), IND(x, "la%d" % t, K12 * h, K12 * (h + 1)))
-            load("g", A("pp", 4 * HC * h, 4 * HC * (h + 1)), A(x, 4 * HC * h, 4 * HC * (h + 1)), "pa%d_%d" % (r, h), accum_op=OP.add)
-        act(A("ga", 0, HC), IND("b", lu, 0, K12), AF.Identity, scale=-3.0, bias=3.0)
-        ts(A("ga", HC, C), IND("b", lu, K12, K24), -3.0, OP.mult, 3.0, OP.add)
-        tt(A("tx", HC, C), IND("b", lu, K24 + K12, 2 * K24), A("ga", HC, C), OP.add)
-        tt(A("tx", 0, HC), IND("b", lu, K24, K24 + K12), A("ga", 0, HC), OP.add)
-        act(A("c3"), A("tx", 0, C), AF.Relu, scale=-3.0, bias=3.0)
-        ts(A("c0"), A("tx", 0, C), 0.0, OP.is_equal)
-        tt(A("yy"), IND("c0", *fk), A("tx", 0, C), OP.subtract)
-        tt(A("tx", C, 2 * C), IND("c3", *fl), A("yy"), OP.add)
-        ts(A("c1"), A("tx", C, 2 * C), 0.0, OP.is_equal)
-        act(A("gb"), IND("c1", *fl), AF.Copy, scale=3.0)
-        tt(A("xx"), IND("c1", *fk), A("gb"), OP.add)
-        if r == 1:
-            for b in range(4):
-                act(A("et", 512 * b + b, 512 * (b + 1), 4), A("eye"))
-            quant(A("eq"), A("es"), A("et"))
+        for h, cuts in enumerate(MEANS):
+            for c, d in zip(cuts, cuts[1:]):
+                act(A("pp", 4 * c, 4 * d), IND(x, "la", c // 4, d // 4))
+            lo, hi = 4 * cuts[0], 4 * cuts[-1]
+            load("g", A("pp", lo, hi), A(x, lo, hi), "pa%d_%d" % (r, h), late=ADDING, accum_op=OP.add)
+        times("v" if r == 1 else "s", A("xc", 4 * VMEANS[0], 4 * C), A(x, 4 * VMEANS[0], 4 * C))
+        for c, d in zip(VMEANS, VMEANS[1:]):
+            tt(A("pp", 4 * c, 4 * d), IND(x, "la", c // 4, d // 4), A("xc", 4 * c, 4 * d), OP.add)
+        act(A("ga"), IND("b", *fl), AF.Relu, scale=2.0)
+        ts(A("gb"), IND("b", *fk), 0.5, OP.is_gt, 2.0, OP.add)
+        scan(A("t0"), A("ga"), A("gb"), 0.0, OP.max, OP.subtract)
+        act(A("gc"), IND("t0", *fl), AF.Relu, scale=2.0, bias=2.0)
+        ts(A("c0"), A("t0"), 0.0, OP.is_equal, -3.0, OP.add)
+        tt(A("yy"), IND("c0", *fk), A("t0"), OP.add)
+        scan(A("t1"), A("gc"), A("yy"), 0.0, OP.max, OP.add)
+        act(A("ge"), IND("t1", *fl))
+        ts(A("gf"), IND("t1", *fk), -3.0, OP.is_equal, -1.0, OP.mult)
         act(A("ts"), A("ps6", 0, HC), AF.Sign, scale=-1.0)
-        scan(A("raw0"), A("wgt"), A("tx", 0, C))
-        select("0", A("raw0", *VIEW24), L)
+        wrap("t0w", "t0", "w16", 0, C)
+        ts(SLOT("hm0", 2), W16("t0w"), -BIG - 1.5, OP.is_lt)
+        ts(SLOT("hm0", 1), W16("t0w"), -BIG - 2.5, OP.is_lt)
+        choose("0")
         act(A("dn"), IND("nat", "d0", 0, K24))
-        scan(A("raw1"), A("wgt"), A("tx", C, 2 * C))
-        select("1", A("raw1", *VIEW24), L)
+        ts(A("thr"), W16("t0w"), -1.5, OP.add)
+        ts(A("ref1"), SLOT("hm0", 2), -4.0, OP.mult, -BIG - 1.0, OP.add)
+        ts(A("m2"), W16("t0w"), -BIG - 1.5, OP.is_lt, 2.0, OP.mult)
+        tt(A("ref2"), W16("t0w"), A("m2"), OP.add)
+        wrap("t1w", "t1", "w16", 0, C)
+        tt(A("cl"), W16("t1w"), A("thr"), OP.is_gt)
+        tt(SLOT("hm1", 1), W16("t1w"), A("ref1"), OP.not_equal)
+        tt(SLOT("hm1", 2), A("cl"), SLOT("hm0", 2), OP.not_equal)
+        choose("1")
         act(A("qn"), IND("dn", "d1", 0, K24))
-        scan(A("raw2"), A("wgt"), A("xx"))
-        tt(A("xd"), A("raw2", *VIEW24), A("raw0", *VIEW24), OP.subtract)
-        select("2", A("xd"), L)
-        tt(A("om"), IND("qn", "d2", 0, K24), A("sel"), OP.mult)
-        act(A("on"), IND("qn", "d2", 0, K24))
-        scan(A("ow"), A("rst"), A("om"))
-        for t in (2, 3, 0, 1):
-            ts(A("of%d" % t), A("ow", *VIEW24), 4.0, OP.mult, float(t), OP.add)
-        for h in (0, 1):
-            boost[0] = BOOST[h]
-            for t in range(4):
-                z, p = A("zt", 4 * HC * h + t, 4 * HC * (h + 1), 4), IND("pp", "of%d" % t, K12 * h, K12 * (h + 1))
-                if t < 2 - h:
-                    ts(z, p, 0.5, OP.mult)
-                else:
-                    act(z, p, AF.Copy, scale=0.5)
-            quant(A("zq", HC * h, HC * (h + 1)), A("zs", HC * h, HC * (h + 1)), A("zt", 4 * HC * h, 4 * HC * (h + 1)))
+        wrap("gfw", "gf", "w16", 0, C)
+        wrap("gew", "ge", "w16", 0, C)
+        tt(SLOT("hm2", 1), W16("gfw"), A("ref2"), OP.not_equal)
+        ts(A("e2"), W16("gew"), -BIG - 3.0, OP.is_equal)
+        tt(SLOT("hm2", 2), A("e2"), SLOT("hm0", 2), OP.not_equal)
+        choose("2")
+        vcopy(A("on", 0, POINT), IND("qn", "d2", 0, POINT // 16))
+        act(A("on", POINT, C), IND("qn", "d2", POINT // 16, K24))
+        for lo, hi in ((0, POINT), (POINT, C)):
+            wrap("ow", "on", "w4", lo, hi)
+            ts(A("of", lo // 4, hi // 4), W4("ow", lo, hi), 4.0, OP.mult, A("col", 3, 4), OP.add)
+        for h, (lo, hi, mid) in enumerate(PIECES):
+            boost[0] = BOOST * (len(PIECES) - 1 - h)
+            for q, a, e in (("v", lo, mid), ("s", mid, hi)):
+                if e > a:
+                    times(q, A("zt", 4 * a, 4 * e), IND("pp", "of", a // 4, e // 4), 0.5)
+            quant(A("zq", lo, hi), A("zs", lo, hi), A("zt", 4 * lo, 4 * hi))
             for b in range(4):
-                mm("ps%d" % (4 * h + b), "wq", "wp", 128 * b, "zq", "zs", HC * h, HC * (h + 1))
-        boost[0] = 0.0
-        tt(A("mn"), IND("on", "kin%d" % r, 0, K24), A("sel"), OP.mult)
-        scan(A("mw"), A("rst"), A("mn"))
-        vcopy(A("mu"), A("mw", *VIEW24))
-        send(A("min%d" % r), A("mu", K12, K24), partner(r), "rm%d" % r, "lm%d" % r, 2.0)
+                mm("ps%d" % (4 * (h % 2) + b), "wq", "wp", 128 * b, "zq", "zs", lo, hi)
+            boost[0] = 0.0
+            for b in range(4):
+                times(COPIES[4 * h + b], A("h", C * b + lo, C * b + hi), A("ps%d" % (4 * (h % 2) + b), 0, hi - lo), 0.03125)
+        act(A("mn", 0, HC), IND("on", "kin%d" % r, 0, K12))
+        wrap("mw", "mn", "w16", 0, HC)
+        ts(A("mu"), W16("mw", 0, HC), BIG + HC, OP.add)
+        act(A("mn", HC, C), IND("on", "kin%d" % r, K12, K24))
+        wrap("mw", "mn", "w4", HC, C)
+        ts(A("mo"), W4("mw", HC, C), A("col", 4, 5), OP.add)
+        send(A("min%d" % r), A("mo"), partner(r), "rm%d" % r, "lm%d" % r, SMALL)
         for b in range(4):
-            act(A("h%d" % b, 0, HC), A("ps%d" % b, 0, HC), scale=0.03125)
-        for b in (0, 2):
-            ts(A("h%d" % b, HC, C), A("ps%d" % (4 + b), 0, HC), 0.03125, OP.mult)
-            act(A("h%d" % (b + 1), HC, C), A("ps%d" % (5 + b), 0, HC), scale=0.03125)
-            vcopy(A("ht", b, 4 * HC, 4), IND("h%d" % b, "mu", 0, K12))
-            act(A("ht", b + 1, 4 * HC, 4), IND("h%d" % (b + 1), "mu", 0, K12))
+            times(PARTS[b], A("ht", b, 4 * HC, 4), IND("h", "mu", 0, K12, C * b, C * (b + 1)))
         quant(A("hq"), A("hs"), A("ht"))
-        send(U8("dq%d" % r, 0, HC), U8("hq", 0, HC), partner(r), "rc%d" % r, "lc%d" % r, 3.0)
-        send(A("ds%d" % r), A("hs"), partner(r), "rs%d" % r, "ls%d" % r, 2.7)
-        for b in range(4):
-            tt(A(xn, 4 * HC + b, 8 * HC, 4), IND("h%d" % b, "min%d" % r, 0, K12), A(x, 4 * HC + b, 8 * HC, 4), OP.add)
+        if r == 2:
+            behind.append(len(nodes) - 1)
+            quant(A("vq"), A("vs"), A("vt"))
+        send(U8("dq%d" % r, 0, HC), U8("hq", 0, HC), partner(r), "rc%d" % r, "lc%d" % r, CODES)
+        send(A("ds%d" % r), A("hs"), partner(r), "rs%d" % r, "ls%d" % r, PLANE)
+        if OWN > HC:
+            tt(A(xn, 4 * HC, 4 * OWN), IND("h", "min%d" % r, 0, (OWN - HC) // 4), A(x, 4 * HC, 4 * OWN), OP.add)
+        if OWN < C:
+            act(A(xn, 4 * OWN, 4 * C), IND("h", "min%d" % r, (OWN - HC) // 4, 4 * K12))
+            load("g", A(xn, 4 * OWN, 4 * C), A(x, 4 * OWN, 4 * C), "pa%d_4" % r, late=ADDING, accum_op=OP.add)
         if r < ROUNDS:
             signs(xn, 1)
         else:
             quant(A("xq", HC, C), A("xs", HC, C), A(xn, 4 * HC, 8 * HC))
-        scan(A("tw"), A("wgt", 0, HC), A("ts"))
+        wrap("tw", "ts", "w16", 0, HC)
         for i in range(2):
-            ts(A("tt", K12 * i, K12 * (i + 1)), A("tw", *VIEW12), A("fac", 0, 1), OP.mult, 0.5, OP.is_gt)
+            ts(A("tt", K12 * i, K12 * (i + 1)), W16("tw", 0, HC), 0.5 - BIG, OP.is_gt)
         tt(A("ud"), A("tt"), A("dif"), OP.mult)
         tt(A(Ln, 0, K24), A(L, 0, K24), A("ud"), OP.add)
         tt(A(Ln, 3 * K12, 4 * K12), A(L, 3 * K12, 4 * K12), A("ud", 0, K12), OP.subtract)
         tt(A(Ln, 2 * K12, 3 * K12), A(L, 2 * K12, 3 * K12), A("ud", K12, K24), OP.subtract)
+        vcopy(A("lu%d" % r), A(Ln))
         if r < ROUNDS:
-            lists_of(r, False)
+            lists_of(r)
             send_children(r + 1)
         else:
-            quant(A("vq"), A("vs"), A("vt"))
             mm("ps4", "vq", "vs", 0, "xq", "xs", HC, C)
             act(A("yo", HC, C), A("ps4", 0, HC))
-            vcopy(A("lu%d" % r), A(Ln))
-            act(A("lro"), IND("nat", "lu%d" % r, 0, 2 * K24))
+            act(A("lro"), IND("nat", "lu%d" % r, 0, 2 * K24), AF.Identity, bias=float(HC))
             load("y", X(T.oc[:, 4 * HC:4 * C]), U8("xq", HC, C), "o0")
             for k in range(4):
                 load("y", X(T.osc[4 * k:4 * k + 4, HC:C]), (T.xs[32 * k:32 * k + 4, HC:C], [("xs", HC, C, 1)]), "o%d" % (1 + k))

@@ -8,8 +8,8 @@ MASK = [1, 2, 3]
 ROUNDS = 3
 BIG = 512.0
 LOW = -4096.0
-CYCLE, FACTOR, GATHER, PRODUCT, WAKE, LOOK = 0.00083, 1.25, 1.56, 1.5, 0.1, 0.5
-LOCAL, ADDING, SMALL, CODES, PLANE = 1.6, 3.8, 1.6, 2.2, 2.0
+CYCLE, FACTOR, GATHER, PRODUCT, WAKE, OWNWAKE, ISSUE = 0.00083, 1.25, 1.56, 1.5, 0.22, 0.22, 0.8
+LOCAL, ADDING, SMALL, CODES, PLANE = 1.6, 3.0, 1.0, 1.6, 1.2
 PIECES = ((0, 128, 64), (128, 256, 192), (256, 384, 320))
 MEANS = ((0, 96, 192, 240),)
 VMEANS = (240, 312, 384)
@@ -177,12 +177,13 @@ def rank_program(g, core, T, topo):
         n = len(topo.engines(core, dst))
         me = add("g", lambda: g.remote_dma(out_ap=out[0], in_ap=in_[0], remote_sem=T.sem[rsem], local_sem=T.sem[lsem],
                                            pid=pid, routing_id=rid, dma_engine_mask=topo.mask(core, dst)),
-                 [], [in_], lsem, n, 0.4, late, True)
+                 [], [in_], lsem, n, ISSUE, late, True)
         add("far", None, [out], [], rsem, len(topo.engines(dst, core)), 0.0, 0.0, True, (me,))
 
     def plan():
         count = len(nodes)
-        before = [[(d, nodes[d]["late"] + WAKE if strong else 0.0) for d, strong in n["deps"].items()] for n in nodes]
+        before = [[(d, nodes[d]["late"] + (OWNWAKE if nodes[d]["q"] == n["q"] else WAKE) if strong else 0.0)
+                   for d, strong in n["deps"].items()] for n in nodes]
         after = [[] for _ in nodes]
         for i in range(count):
             for d, wait in before[i]:

@@ -8,17 +8,22 @@ MASK = [1, 2, 3]
 ROUNDS = 3
 BIG = 512.0
 LOW = -4096.0
-CYCLE, FACTOR, GATHER, PRODUCT, WAKE, OWNWAKE, ISSUE = 0.00083, 1.25, 1.56, 1.5, 0.22, 0.22, 0.8
-LOCAL, ADDING, SMALL, CODES, PLANE = 1.6, 3.0, 1.0, 1.6, 1.2
-PIECES = ((0, 128, 64), (128, 256, 192), (256, 384, 320))
-MEANS = ((0, 96, 192, 240),)
-VMEANS = (240, 312, 384)
+CYCLE, FACTOR, GATHER, PRODUCT, WAKE, OWNWAKE, ISSUE = 0.00083, 1.1, 1.3, 1.2, 0.22, 0.22, 0.4
+LOCAL, ADDING, SMALL, CODES, PLANE = 1.1, 2.6, 1.3, 0.5, 0.3
+PIECES = ((0, 128, 64), (128, 256, 160), (256, 384, 288))
+MEANS = (0, 352)
 OWN = 384
-POINT = 128
-COPIES = "vsvs" "vsvs" "vsvs"
-PARTS = "vsvs"
-BOOST = 2.0
-PASSES = 4
+LISTS = (0, 128, 384)
+POINT = (("v", 0, 128), ("s", 128, 384))
+COPIES = "svvv" "svvv" "svvv"
+PARTS = (0, 0, 192, 96)
+CLIMB = (("s", 0, 320), ("s", 320, 576), ("v", 576, 768))
+FOLLOW = (("s", 0, 192), ("v", 192, 384))
+READS = (("s", 0, 192), ("s", 192, 384))
+LATE, EARLY, SIDE = True, False, False
+BOOST = 1.0
+PASSES, SWAPS, HEAT = 4, 0, 0.1
+KEPT = []
 
 BF, F16, F32, I32, U16, COD, PLN = "bfloat16", "float16", "float32", "int32", "uint16", "float8_e4m3fn_x4", "uint8"
 WRAP = F16
@@ -44,7 +49,7 @@ def _buffers():
     sb(COD, 512, "wq", "eq")
     sb(PLN, 512, "wp", "es")
     sb(BF, 128, "one")
-    sb(BF, 2048, "et")
+    sb(BF, 516, "et")
     sb(I32, 16, "ulist")
     sb(U16, 16, "ulist16")
     sb(I32, K24, "pi", "pm", "q16")
@@ -55,14 +60,19 @@ def _buffers():
     sb(BF, C, "w16", "w4", "nat")
     sb(F32, K24, "cw")
     sb(F32, 8, "col")
-    sb(I32, 2 * K24, "gin")
-    sb(F32, 2 * K24, "lk0", "lk1", "lk2", "lk3")
+    sb(I32, 2 * K24, "lk0")
+    sb(F32, 2 * K24, "lk1", "lk2", "lk3")
     sb(U16, 2 * K24, "lu0", "lu1", "lu2", "lu3")
     sb(U16, 4 * K24, "la", "of")
     sb(F32, 3 * K24, "hd", "hm0", "hm1", "hm2", "ho0", "ho1", "ho2")
-    sb(F32, K24, "dif", "tt", "ud", "thr", "ref1", "m2", "ref2", "cl", "e2")
-    sb(BF, C, "b", "ga", "gb", "t0", "c0", "gc", "yy", "t1", "ge", "gf", "ln", "dn", "qn", "on", "mn")
-    sb(WRAP, C, "t0w", "t1w", "gew", "gfw", "lw", "ow", "mw")
+    sb(F32, K24, "dif", "tt", "ud", "thr", "ref1", "m2", "ref2", "cl")
+    sb(BF, C, "b", "ga", "gb", "ln", "dn", "qn", "on", "mn")
+    sb(BF, 2 * C, "t0", "gc", "ge")
+    sb(BF, 2 * C + 16, "t1")
+    sb(WRAP, 2 * C, "gew")
+    sb(WRAP, C, "t0w", "t1w", "t2w", "lw", "ow", "mw")
+    sb(F32, 2 * K24, "e2")
+    sb(U16, 2 * K24, "lv")
     sb(U16, K24, "d0", "d1", "d2", "kin1", "kin2", "kin3")
     sb(U16, K12, "mu")
     sb(U16, 4 * K12, "mo", "min1", "min2", "min3")
@@ -77,7 +87,7 @@ def _buffers():
 
 SCRATCH = _buffers()
 SEMAPHORES = ["cv", "cs", "ct", "cg"]
-SEMAPHORES += ["i%d" % i for i in range(8)]
+SEMAPHORES += ["i%d" % i for i in range(9)]
 SEMAPHORES += ["pa%d_%d" % (r, h) for r in (1, 2, 3) for h in range(5)]
 SEMAPHORES += [n + "%d" % r for r in (1, 2, 3) for n in ("rk", "rm", "rc", "rs", "lk", "lm", "lc", "ls")]
 SEMAPHORES += ["o%d" % i for i in range(20)]
@@ -179,9 +189,12 @@ def rank_program(g, core, T, topo):
                                            pid=pid, routing_id=rid, dma_engine_mask=topo.mask(core, dst)),
                  [], [in_], lsem, n, ISSUE, late, True)
         add("far", None, [out], [], rsem, len(topo.engines(dst, core)), 0.0, 0.0, True, (me,))
+        return me
 
     def plan():
         count = len(nodes)
+        if KEPT:
+            return KEPT
         before = [[(d, nodes[d]["late"] + (OWNWAKE if nodes[d]["q"] == n["q"] else WAKE) if strong else 0.0)
                    for d, strong in n["deps"].items()] for n in nodes]
         after = [[] for _ in nodes]
@@ -223,7 +236,8 @@ def rank_program(g, core, T, topo):
                 best = (end, start)
             back = lay([-t - n["busy"] for t, n in zip(start, nodes)], after, before, [n["late"] for n in nodes])
             urgency = [-t - n["busy"] for t, n in zip(back, nodes)]
-        return sorted(range(count), key=lambda i: (best[1][i], i))
+        KEPT.extend(sorted(range(count), key=lambda i: (best[1][i], i)))
+        return KEPT
 
     def issue(sequence):
         known = {q: {} for q in list(queue) + ["far"]}
@@ -311,10 +325,12 @@ def rank_program(g, core, T, topo):
         return A(name, i, 3 * K24, 3)
 
     load("y", A("ut"), X(T.u[:]), "i0")
-    load("s", A("gin", K24, 2 * K24), X(T.gk[:]), "i1")
-    load("s", A("gin", 0, K24), X(T.gl[:]), "i3")
-    load("y", A("x0", 4 * HC, 4 * C), X(T.x[:, 4 * HC:4 * C]), "i2", late=LOCAL + 0.4)
-    first = load("y", A("x0", 0, 4 * HC), X(T.x[:, 0:4 * HC]), "i7", late=LOCAL + 0.8)
+    load("s", A("lk0", 0, K24), X(T.gl[:]), "i3")
+    load("s", A("lk0", K24, 2 * K24), X(T.gk[:]), "i1")
+    load("y", A("x0", 4 * HC, 4 * C), X(T.x[:, 4 * HC:4 * C]), "i2", late=LOCAL + 0.6)
+    first = load("y", A("x0", 0, 4 * HC), X(T.x[:, 0:4 * HC]), "i7", late=LOCAL + 1.0)
+    if MEANS[-1] < C:
+        load("y", A("xc", 4 * MEANS[-1], 4 * C), X(T.x[:, 4 * MEANS[-1]:4 * C]), "i8", late=LOCAL + 1.5, after=(first,))
     load("y", U8("wq", 0, 512), X(T.wc[:]), "i4", after=(first,))
     load("y", A("wp"), X(T.ws[:]), "i5", after=(first,))
 
@@ -322,8 +338,12 @@ def rank_program(g, core, T, topo):
     iota(A("pos", 0, 16), [[1, 16]], 0, small=True)
     iota(A("pos", 16, 32), [[0, 4], [1, 4]], 0, small=True)
     iota(A("ulist"), [[1, 2], [16, 8]], 0)
-    iota(A("nat"), [[1, C]], 0, base=-HC, small=True)
+    fill(A("one"), 1.0)
+    fill(A("et"), 0.0)
+    eye = A("et", 3, 515, 4)
+    op("g", lambda: g.affine_select(eye[0], T.one[:], [[-1, 128]], OP.is_equal, 0.0, 0, 1), [eye], [A("one")])
     iota(A("q16"), [[16, K24]], 0)
+    iota(A("nat"), [[1, C]], 0, base=-HC, small=True)
     ts(A("pm"), A("pi"), 15, OP.bitwise_and)
     ts(A("pq", 0, 1), A("pi", 0, 1), 15, OP.bitwise_and)
     ts(A("pq", 1, 2), A("pi", 0, 1), 2, OP.logical_shift_right, 3, OP.bitwise_and)
@@ -335,24 +355,17 @@ def rank_program(g, core, T, topo):
         ts(A("pb", 16 * i, 16 * i + 16), A("pos", 16 * i, 16 * i + 16), A("col", i, i + 1), OP.is_le, -BIG, OP.mult)
     tt(A("pat"), A("pa"), A("pb"), OP.add)
     ts(A("pat", 15, 32, 4), A("pat", 15, 32, 4), -2 * BIG, OP.add)
-    act(A("w4"), IND("pat", "pm16", 0, K24, 16, 32))
-    act(A("w16"), IND("pat", "pm16", 0, K24, 0, 16))
     vcopy(A("ulist16"), A("ulist"))
-    fill(A("one"), 1.0)
-    for b in range(4):
-        fill(A("et", 512 * b, 512 * (b + 1)), 0.0)
+    early[0] = EARLY
+    act(A("w16"), IND("pat", "pm16", 0, K24, 0, 16))
+    act(A("w4"), IND("pat", "pm16", 0, K24, 16, 32))
+    fill(A("t0", 1, 2 * C, 2), -64.0)
     ts(A("col", 3, 4), A("pq", 2, 3), 4 * (BIG + HC), OP.add)
     ts(A("col", 4, 5), A("pq", 2, 3), float(C), OP.mult, BIG + HC, OP.add)
     tt(A("cw"), A("pm"), A("q16"), OP.add)
     for name in ("hm0", "hm1", "hm2"):
         fill(A(name), 0.0)
-    for b in range(4):
-        out = A("et", 512 * b + b, 512 * (b + 1), 4)
-        op("g", lambda out=out: g.affine_select(out[0], T.one[:], [[-1, 128]], OP.is_equal, 0.0, 0, 1), [out], [A("one")])
     early[0] = False
-    vcopy(A("lu0", K24, 2 * K24), A("gin", K24, 2 * K24))
-    vcopy(A("lu0", 0, K24), A("gin", 0, K24))
-    vcopy(A("lk0"), A("gin"))
 
     def partner(r):
         return T.cores[rank ^ MASK[r - 1]]
@@ -362,21 +375,27 @@ def rank_program(g, core, T, topo):
 
     def lists_of(n):
         L = "lk%d" % n
-        act(A("ln"), IND("nat", "lu%d" % n, 0, K24))
-        wrap("lw", "ln", "w4", 0, C)
-        ts(A("la"), W4("lw"), 4.0, OP.mult, A("col", 3, 4), OP.add)
+        early[0] = n == 0
+        vcopy(A("lu%d" % n), A(L))
+        for t in range(4):
+            ts(A("la", K24 * t, K24 * (t + 1)), A(L, 0, K24), 4.0, OP.mult, float(t), OP.add)
+        early[0] = False
+        ts(A("lv"), A(L), 2.0, OP.mult)
         tt(SLOT("hd", 0), A(L, K24, 2 * K24), A("cw"), OP.subtract)
         tt(SLOT("hd", 1), A("cw"), A(L, 0, K24), OP.subtract)
         vcopy(SLOT("hd", 2), A(L, 0, K24))
         tt(A("dif", 0, K12), A(L, 3 * K12, 4 * K12), A(L, 0, K12), OP.subtract)
         tt(A("dif", K12, K24), A(L, 2 * K12, 3 * K12), A(L, K12, 2 * K12), OP.subtract)
 
+    early[0] = True
     quant(A("uq"), A("us"), A("ut"))
     for h in (0, 1):
+        early[0] = h == 0
         src = (T.uq[:, 0:128].bitcast(dt.uint32).indirect(T.ulist16[:, 8 * h:8 * h + 8]), [("uq", 0, 128, 1), ("ulist16", 0, 16, 1)])
         vcopy((T.uq2[:, 128 * h:128 * h + 128].bitcast(dt.uint32), [("uq2", 128 * h, 128 * h + 128, 1)]), src)
         act(A("us2", 128 * h, 128 * h + 128),
             (T.us[:, 0:128].indirect(T.ulist16[:, 8 * h:8 * h + 8]), [("us", 0, 128, 1), ("ulist16", 0, 16, 1)]))
+    lists_of(0)
     early[0] = True
     send_children(1)
     load("g", A("vt"), X(T.v[:]), "i6", after=(first,))
@@ -386,70 +405,79 @@ def rank_program(g, core, T, topo):
         lo, hi = HC * h, HC * (h + 1)
         quant(A("xq", lo, hi), A("xs", lo, hi), A(x, 4 * lo, 4 * hi))
         mm("ps%d" % (5 - h), "uq2", "us2", 0, "xq", "xs", lo, hi)
-        if h == 0:
-            ts(A("b", lo, hi), A("ps5", 0, HC), 0.0, OP.is_gt)
-            mm("ps6", "uq2", "us2", 128, "xq", "xs", lo, hi)
+        if h == 0 or x == "x0":
+            ts(A("b", lo, hi), A("ps%d" % (5 - h), 0, HC), 0.0, OP.is_gt)
         else:
             act(A("b", lo, hi), A("ps4", 0, HC), AF.Sign)
+
+    def turns():
+        mm("ps6", "uq2", "us2", 128, "xq", "xs", 0, HC)
+        act(A("ts"), A("ps6", 0, HC), AF.Sign, scale=-1.0)
 
     def choose(s):
         scan(A("ho" + s), A("hm" + s), A("hd"), 0.0, OP.mult, OP.add)
         vcopy(A("d" + s), SLOT("ho" + s, 2))
 
-    lists_of(0)
     signs("x0", 1)
     for b in range(4):
-        quant(A("eq", 128 * b, 128 * b + 128), A("es", 128 * b, 128 * b + 128), A("et", 512 * b, 512 * b + 512))
+        quant(A("eq", 128 * b, 128 * b + 128), A("es", 128 * b, 128 * b + 128), A("et", 3 - b, 515 - b))
 
     for r in range(1, ROUNDS + 1):
         x, xn = "x%d" % (r - 1), "x%d" % r
         lu, L, Ln = "lu%d" % (r - 1), "lk%d" % (r - 1), "lk%d" % r
-        fl = (lu, 0, K24)
-        fk = (lu, K24, 2 * K24)
-
         signs(x, 0)
-        for h, cuts in enumerate(MEANS):
-            for c, d in zip(cuts, cuts[1:]):
-                act(A("pp", 4 * c, 4 * d), IND(x, "la", c // 4, d // 4))
-            lo, hi = 4 * cuts[0], 4 * cuts[-1]
-            load("g", A("pp", lo, hi), A(x, lo, hi), "pa%d_%d" % (r, h), late=ADDING, accum_op=OP.add)
-        times("v" if r == 1 else "s", A("xc", 4 * VMEANS[0], 4 * C), A(x, 4 * VMEANS[0], 4 * C))
-        for c, d in zip(VMEANS, VMEANS[1:]):
-            tt(A("pp", 4 * c, 4 * d), IND(x, "la", c // 4, d // 4), A("xc", 4 * c, 4 * d), OP.add)
-        act(A("ga"), IND("b", *fl), AF.Relu, scale=2.0)
-        ts(A("gb"), IND("b", *fk), 0.5, OP.is_gt, 2.0, OP.add)
-        scan(A("t0"), A("ga"), A("gb"), 0.0, OP.max, OP.subtract)
-        act(A("gc"), IND("t0", *fl), AF.Relu, scale=2.0, bias=2.0)
-        ts(A("c0"), A("t0"), 0.0, OP.is_equal, -3.0, OP.add)
-        tt(A("yy"), IND("c0", *fk), A("t0"), OP.add)
-        scan(A("t1"), A("gc"), A("yy"), 0.0, OP.max, OP.add)
-        act(A("ge"), IND("t1", *fl))
-        ts(A("gf"), IND("t1", *fk), -3.0, OP.is_equal, -1.0, OP.mult)
-        act(A("ts"), A("ps6", 0, HC), AF.Sign, scale=-1.0)
-        wrap("t0w", "t0", "w16", 0, C)
+        if not LATE:
+            turns()
+        for h, (lo, hi) in enumerate(zip(MEANS, MEANS[1:])):
+            for t in range(4):
+                act(A("pp", 4 * lo + t, 4 * hi, 4), IND(x, "la", K24 * t + lo // 16, K24 * t + hi // 16))
+            load("g", A("pp", 4 * lo, 4 * hi), A(x, 4 * lo, 4 * hi), "pa%d_%d" % (r, h), late=ADDING, accum_op=OP.add)
+        lo = MEANS[-1]
+        if lo < C:
+            if r > 1:
+                act(A("xc", 4 * lo, 4 * C), A(x, 4 * lo, 4 * C))
+            for t in range(4):
+                tt(A("pp", 4 * lo + t, 4 * C, 4), IND(x, "la", K24 * t + lo // 16, K24 * (t + 1)), A("xc", 4 * lo + t, 4 * C, 4), OP.add)
+        act(A("ga"), IND("b", lu, 0, K24), AF.Relu, scale=2.0)
+        ts(A("gb"), IND("b", lu, K24, 2 * K24), 0.5, OP.is_gt, 2.0, OP.add)
+        scan(A("t0", 0, 2 * C, 2), A("ga"), A("gb"), 0.0, OP.max, OP.subtract)
+        ts(A("gc", 0, 2 * C, 2), IND("t0", "lv", K24, 2 * K24), 0.0, OP.is_equal, -6.0, OP.add)
+        act(A("gc", 1, 2 * C, 2), IND("t0", "lv", 0, K24), AF.Relu, scale=2.0, bias=2.0)
+        scan(A("t1", 15, 15 + 2 * C), A("t0"), A("gc"), LOW, OP.max, OP.add)
+        for q, lo, hi in CLIMB:
+            times(q, A("ge", lo, hi), IND("t1", "lv", lo // 16, hi // 16, 16, 15 + 2 * C))
+            scan(A("gew", lo, hi), A("ge", lo, hi), A("w16", 0, hi - lo), LOW, OP.max, OP.add)
+        scan(A("t0w"), A("t0", 0, 2 * C, 2), A("w16"), LOW, OP.max, OP.add)
         ts(SLOT("hm0", 2), W16("t0w"), -BIG - 1.5, OP.is_lt)
         ts(SLOT("hm0", 1), W16("t0w"), -BIG - 2.5, OP.is_lt)
         choose("0")
         act(A("dn"), IND("nat", "d0", 0, K24))
-        ts(A("thr"), W16("t0w"), -1.5, OP.add)
-        ts(A("ref1"), SLOT("hm0", 2), -4.0, OP.mult, -BIG - 1.0, OP.add)
-        ts(A("m2"), W16("t0w"), -BIG - 1.5, OP.is_lt, 2.0, OP.mult)
-        tt(A("ref2"), W16("t0w"), A("m2"), OP.add)
-        wrap("t1w", "t1", "w16", 0, C)
-        tt(A("cl"), W16("t1w"), A("thr"), OP.is_gt)
-        tt(SLOT("hm1", 1), W16("t1w"), A("ref1"), OP.not_equal)
-        tt(SLOT("hm1", 2), A("cl"), SLOT("hm0", 2), OP.not_equal)
+        ts(A("m2"), SLOT("hm0", 2), -2.0, OP.mult, -BIG, OP.add)
+        tt(A("ref2"), A("m2"), W16("t0w"), OP.subtract)
+        if SIDE:
+            ts(A("thr"), A("ref2"), -BIG - 6.0, OP.add)
+            ts(A("ref1"), SLOT("hm0", 2), 2.0, OP.mult, -BIG, OP.add)
+            scan(A("t1w"), A("gc", 0, 2 * C, 2), A("w16"), LOW, OP.max, OP.add)
+            scan(A("t2w"), A("gc", 1, 2 * C, 2), A("w16"), LOW, OP.max, OP.add)
+            tt(SLOT("hm1", 1), W16("t1w"), A("thr"), OP.not_equal)
+            tt(SLOT("hm1", 2), W16("t2w"), A("ref1"), OP.not_equal)
+        else:
+            ts(A("thr"), W16("t0w"), -4.5, OP.add)
+            ts(A("ref1"), SLOT("hm0", 2), -4.0, OP.mult, -BIG - 4.0, OP.add)
+            scan(A("t1w"), A("t1", 16, 15 + 2 * C, 2), A("w16"), LOW, OP.max, OP.add)
+            tt(A("cl"), W16("t1w"), A("thr"), OP.is_gt)
+            tt(SLOT("hm1", 1), W16("t1w"), A("ref1"), OP.not_equal)
+            tt(SLOT("hm1", 2), A("cl"), SLOT("hm0", 2), OP.not_equal)
         choose("1")
-        act(A("qn"), IND("dn", "d1", 0, K24))
-        wrap("gfw", "gf", "w16", 0, C)
-        wrap("gew", "ge", "w16", 0, C)
-        tt(SLOT("hm2", 1), W16("gfw"), A("ref2"), OP.not_equal)
-        ts(A("e2"), W16("gew"), -BIG - 3.0, OP.is_equal)
-        tt(SLOT("hm2", 2), A("e2"), SLOT("hm0", 2), OP.not_equal)
+        for q, lo, hi in FOLLOW:
+            times(q, A("qn", lo, hi), IND("dn", "d1", lo // 16, hi // 16))
+        ts(A("e2"), W16("gew", 0, 2 * C), -BIG - 6.0, OP.is_equal)
+        tt(SLOT("hm2", 1), A("e2", K24, 2 * K24), A("ref2"), OP.not_equal)
+        tt(SLOT("hm2", 2), A("e2", 0, K24), SLOT("hm0", 2), OP.not_equal)
         choose("2")
-        vcopy(A("on", 0, POINT), IND("qn", "d2", 0, POINT // 16))
-        act(A("on", POINT, C), IND("qn", "d2", POINT // 16, K24))
-        for lo, hi in ((0, POINT), (POINT, C)):
+        for q, lo, hi in POINT:
+            times(q, A("on", lo, hi), IND("qn", "d2", lo // 16, hi // 16))
+        for lo, hi in zip(LISTS, LISTS[1:]):
             wrap("ow", "on", "w4", lo, hi)
             ts(A("of", lo // 4, hi // 4), W4("ow", lo, hi), 4.0, OP.mult, A("col", 3, 4), OP.add)
         for h, (lo, hi, mid) in enumerate(PIECES):
@@ -463,21 +491,24 @@ def rank_program(g, core, T, topo):
             boost[0] = 0.0
             for b in range(4):
                 times(COPIES[4 * h + b], A("h", C * b + lo, C * b + hi), A("ps%d" % (4 * (h % 2) + b), 0, hi - lo), 0.03125)
-        act(A("mn", 0, HC), IND("on", "kin%d" % r, 0, K12))
+        for q, lo, hi in READS:
+            times(q, A("mn", lo, hi), IND("on", "kin%d" % r, lo // 16, hi // 16))
         wrap("mw", "mn", "w16", 0, HC)
         ts(A("mu"), W16("mw", 0, HC), BIG + HC, OP.add)
-        act(A("mn", HC, C), IND("on", "kin%d" % r, K12, K24))
         wrap("mw", "mn", "w4", HC, C)
         ts(A("mo"), W4("mw", HC, C), A("col", 4, 5), OP.add)
-        send(A("min%d" % r), A("mo"), partner(r), "rm%d" % r, "lm%d" % r, SMALL)
+        places = send(A("min%d" % r), A("mo"), partner(r), "rm%d" % r, "lm%d" % r, SMALL)
         for b in range(4):
-            times(PARTS[b], A("ht", b, 4 * HC, 4), IND("h", "mu", 0, K12, C * b, C * (b + 1)))
+            for q, lo, hi in (("v", 0, PARTS[b]), ("s", PARTS[b], HC)):
+                if hi > lo:
+                    times(q, A("ht", 4 * lo + b, 4 * hi, 4), IND("h", "mu", lo // 16, hi // 16, C * b, C * (b + 1)))
         quant(A("hq"), A("hs"), A("ht"))
         if r == 2:
             behind.append(len(nodes) - 1)
             quant(A("vq"), A("vs"), A("vt"))
-        send(U8("dq%d" % r, 0, HC), U8("hq", 0, HC), partner(r), "rc%d" % r, "lc%d" % r, CODES)
-        send(A("ds%d" % r), A("hs"), partner(r), "rs%d" % r, "ls%d" % r, PLANE)
+        behind.append(places)
+        behind.append(send(U8("dq%d" % r, 0, HC), U8("hq", 0, HC), partner(r), "rc%d" % r, "lc%d" % r, CODES))
+        plane = send(A("ds%d" % r), A("hs"), partner(r), "rs%d" % r, "ls%d" % r, PLANE)
         if OWN > HC:
             tt(A(xn, 4 * HC, 4 * OWN), IND("h", "min%d" % r, 0, (OWN - HC) // 4), A(x, 4 * HC, 4 * OWN), OP.add)
         if OWN < C:
@@ -487,6 +518,8 @@ def rank_program(g, core, T, topo):
             signs(xn, 1)
         else:
             quant(A("xq", HC, C), A("xs", HC, C), A(xn, 4 * HC, 8 * HC))
+        if LATE:
+            turns()
         wrap("tw", "ts", "w16", 0, HC)
         for i in range(2):
             ts(A("tt", K12 * i, K12 * (i + 1)), W16("tw", 0, HC), 0.5 - BIG, OP.is_gt)
@@ -494,11 +527,12 @@ def rank_program(g, core, T, topo):
         tt(A(Ln, 0, K24), A(L, 0, K24), A("ud"), OP.add)
         tt(A(Ln, 3 * K12, 4 * K12), A(L, 3 * K12, 4 * K12), A("ud", 0, K12), OP.subtract)
         tt(A(Ln, 2 * K12, 3 * K12), A(L, 2 * K12, 3 * K12), A("ud", K12, K24), OP.subtract)
-        vcopy(A("lu%d" % r), A(Ln))
         if r < ROUNDS:
             lists_of(r)
+            behind.append(plane)
             send_children(r + 1)
         else:
+            vcopy(A("lu%d" % r), A(Ln))
             mm("ps4", "vq", "vs", 0, "xq", "xs", HC, C)
             act(A("yo", HC, C), A("ps4", 0, HC))
             act(A("lro"), IND("nat", "lu%d" % r, 0, 2 * K24), AF.Identity, bias=float(HC))

@@ -1,4 +1,4 @@
-from concourse.bass import DstId, RemoteDMATransfer
+import math
 from concourse.mybir import dt, AluOpType, ActivationFunctionType
 
 OP = AluOpType
@@ -6,27 +6,46 @@ AF = ActivationFunctionType
 C, HC, K24, K12 = 384, 192, 24, 12
 MASK = [1, 2, 3]
 ROUNDS = 3
-BIG = 512.0
-LOW = -4096.0
-CYCLE, FACTOR, GATHER, PRODUCT, WAKE, OWNWAKE, ISSUE = 0.00083, 1.1, 1.3, 1.2, 0.22, 0.22, 0.4
-LOCAL, ADDING, SMALL, CODES, PLANE = 1.1, 2.6, 1.3, 0.5, 0.3
-PIECES = ((0, 128, 64), (128, 256, 160), (256, 384, 288))
-MEANS = (0, 352)
-OWN = 384
-LISTS = (0, 128, 384)
-POINT = (("v", 0, 128), ("s", 128, 384))
-COPIES = "svvv" "svvv" "svvv"
-PARTS = (0, 0, 192, 96)
-CLIMB = (("s", 0, 320), ("s", 320, 576), ("v", 576, 768))
+LOW = -64.0
+UNIT = 512.0
+
+FIRST = (("ps4", 128, 384), ("ps5", 0, 128))
+SIGNS = (("ps4", 256, 384), ("ps5", 128, 256), ("ps7", 0, 128))
+SUMS = (("s", 0, 128), ("s", 128, 176), ("v", 176, 256), ("s", 256, 320), ("s", 320, 384))
+PLANES = (("ssss", 0, 256), ("svss", 256, 384))
+OSC = "yyss"
+MEANS = (0, 256, 384)
+RUNS = (0, 256, 384)
 FOLLOW = (("s", 0, 192), ("v", 192, 384))
-READS = (("s", 0, 192), ("s", 192, 384))
-LATE, EARLY, SIDE = True, False, False
-BOOST = 1.0
-PASSES, SWAPS, HEAT = 4, 0, 0.1
+POINT = (("v", 0, 128), ("s", 128, 384))
+PIECES = ((0, 128, 64), (128, 256, 160), (256, 384, 320))
+PRODUCTS = ((0, 0), (0, 1), (0, 2), (0, 3), (1, 0), (1, 1), (1, 2), (2, 0), (2, 1), (2, 2), (1, 3), (2, 3))
+COPIES = "vsvv" "svsv" "vvvv"
+PARTS = (0, 0, 192, 96)
+
+CYCLE = 0.00083
+CLOCKS = ((1.0, 1.4, 1.0, 0.22, 0.8, 1.0, 0.01, 1.0, 0.22), (1.25, 1.9, 1.5, 0.18, 1.0, 1.6, 0.02, 1.0, 0.22),
+          (1.4, 2.6, 1.8, 0.25, 1.2, 2.0, 0.02, 1.2, 0.4), (1.1, 1.3, 1.2, 0.28, 1.4, 2.5, 0.04, 1.3, 0.5))
+ISSUE, LOCAL, REMOTE, NEAR, FAR = 0.4, 1.1, 0.9, 25e3, 14e3
+ONCE = {"g": 1.0, "far": 1.5}
+START, PERIOD = 1.3, 14.0
+FRONT = {"v uq": 1.5, "s w16": 1.55, "v uq2 0": 1.9, "s us2 0": 1.9, "s w4": 2.2, "s us2": 2.4, "v uq2": 3.0, "v la": 2.6, "v lv": 2.9,
+         "v lu": 3.3, "v hd": 3.35, "v dif": 4.1, "v eq": 1.3, "v eq 256": 1.7, "v eq 384": 2.1, "g q16": 0.9, "g vt": 1.0, "g nat": 1.1, "y x": 0.02, "y lk": 0.03}
+WHEN = {"v xq": 1.2, "s pp": 1.25, "v pp": 1.45, "v t0": 1.85,
+        "v g0": 2.3, "s g0": 2.3, "s pp 2": 2.8, "s pp 3": 2.8, "s pp 1024": 2.9, "v t1": 2.9, "s pp 1025": 3.0, "v wm0": 3.2,
+        "s g1": 3.45, "v g1": 3.55, "s pp 1280": 4.0, "s pp 1026": 4.0, "s pp 1027": 4.0, "v ho0": 4.1, "v t2": 4.15, "s ts": 4.4,
+        "v wm1": 4.45, "v d0": 4.6, "v wm1 19": 4.7, "s g2": 4.7, "v g2": 4.85, "s dn": 5.25, "v ho1": 5.4, "v wm2": 5.45,
+        "v d1": 5.75, "v tw": 5.8, "v ho2": 5.95, "v qn": 6.05, "s qn": 6.05, "v d2": 6.3, "v tt": 6.4,
+        "v on": 6.6, "s on": 6.6, "v ud": 6.8, "v ow 0": 7.0, "v ow": 7.15, "s mn 0": 7.15, "v of 0": 7.3, "v lk": 7.35, "v of": 7.5,
+        "v zt": 7.55, "s zt": 7.55, "v zq 0": 8.1, "v zt 1024": 8.25, "v zq 128": 8.65, "v mw 0": 8.75, "v h": 8.85, "s h": 8.95,
+        "v zq": 9.0, "s mn": 9.1, "v h 768": 9.1, "v mu": 9.3, "v mw": 9.6, "v h 896": 9.65, "v mo": 9.9, "s ht": 10.0, "v ht": 10.4,
+        "v lu": 10.8, "v dif": 10.9, "s ln": 11.0, "v hq": 11.2, "v lv": 11.3, "v hd": 11.3, "s lro": 11.3, "v vq": 11.5,
+        "v x 768": 11.6, "v lw": 12.4, "v xq 256": 13.0, "v xq 192": 13.0, "v la": 13.1,
+        "t by eq": 14.0, "t by vq": 14.1, "v x": 14.3, "s yo": 14.5, "v t0 513": 15.05, "v yo": 16.0}
+TRIES, HEAT, COOL, SEED = 30000, 0.005, 0.2, 7
 KEPT = []
 
 BF, F16, F32, I32, U16, COD, PLN = "bfloat16", "float16", "float32", "int32", "uint16", "float8_e4m3fn_x4", "uint8"
-WRAP = F16
 
 
 def _buffers():
@@ -35,12 +54,12 @@ def _buffers():
     def sb(dtype, n, *names):
         for name in names:
             s[name] = ("sbuf", [128, n], dtype)
-    sb(BF, 4 * C, "x0", "x1", "x2", "x3", "xc", "pp", "zt", "h")
+    sb(BF, 4 * C, "x0", "x1", "x2", "x3", "pp", "zt", "h")
     sb(BF, 4 * HC, "ht")
     sb(COD, C, "xq", "zq")
     sb(PLN, C, "xs", "zs")
-    sb(COD, HC, "hq", "dq1", "dq2", "dq3")
-    sb(PLN, HC, "hs", "ds1", "ds2", "ds3")
+    sb(COD, HC, "hq1", "hq2", "hq3", "dq1", "dq2", "dq3")
+    sb(PLN, HC, "hs1", "hs2", "hs3", "ds1", "ds2", "ds3")
     sb(BF, 512, "ut", "vt")
     sb(COD, 128, "uq", "vq")
     sb(PLN, 128, "us", "vs")
@@ -53,32 +72,29 @@ def _buffers():
     sb(I32, 16, "ulist")
     sb(U16, 16, "ulist16")
     sb(I32, K24, "pi", "pm", "q16")
-    sb(I32, 3, "pq")
+    sb(I32, 32, "pos", "pe")
+    sb(I32, 1, "pq")
     sb(U16, K24, "pm16")
-    sb(F32, 32, "pos", "pa", "pb")
+    sb(F32, 32, "pa", "pb")
     sb(BF, 32, "pat")
     sb(BF, C, "w16", "w4", "nat")
     sb(F32, K24, "cw")
-    sb(F32, 8, "col")
+    sb(F32, 2, "col")
     sb(I32, 2 * K24, "lk0")
     sb(F32, 2 * K24, "lk1", "lk2", "lk3")
-    sb(U16, 2 * K24, "lu0", "lu1", "lu2", "lu3")
-    sb(U16, 4 * K24, "la", "of")
-    sb(F32, 3 * K24, "hd", "hm0", "hm1", "hm2", "ho0", "ho1", "ho2")
-    sb(F32, K24, "dif", "tt", "ud", "thr", "ref1", "m2", "ref2", "cl")
-    sb(BF, C, "b", "ga", "gb", "ln", "dn", "qn", "on", "mn")
-    sb(BF, 2 * C, "t0", "gc", "ge")
-    sb(BF, 2 * C + 16, "t1")
-    sb(WRAP, 2 * C, "gew")
-    sb(WRAP, C, "t0w", "t1w", "t2w", "lw", "ow", "mw")
-    sb(F32, 2 * K24, "e2")
-    sb(U16, 2 * K24, "lv")
+    sb(U16, 2 * K24, "lu0", "lu1", "lu2", "lu3", "lv0", "lv1", "lv2")
+    sb(U16, 4 * K24, "la0", "la1", "la2", "of")
+    sb(F32, 3 * K24, "hd0", "hd1", "hd2", "ho0", "ho1", "ho2")
+    sb(F32, K24, "dif0", "dif1", "dif2", "tt", "ud")
+    sb(BF, 2 * C, "t0", "t1", "t2", "g0", "g1", "g2")
+    sb(BF, 3 * C + 32, "wm0", "wm1", "wm2")
+    sb(BF, C, "dn", "qn", "on", "mn", "ln")
+    sb(F16, C, "ow", "mw", "lw")
     sb(U16, K24, "d0", "d1", "d2", "kin1", "kin2", "kin3")
     sb(U16, K12, "mu")
-    sb(U16, 4 * K12, "mo", "min1", "min2", "min3")
+    sb(U16, 4 * K12, "mo1", "mo2", "mo3", "min1", "min2", "min3")
     sb(F32, C, "yo")
-    sb(BF, HC, "ts")
-    sb(WRAP, HC, "tw")
+    sb(BF, HC, "ts", "tw")
     sb(F32, 2 * C, "lro")
     for i in range(8):
         s["ps%d" % i] = ("psum", [128, 512], F32)
@@ -86,12 +102,12 @@ def _buffers():
 
 
 SCRATCH = _buffers()
-SEMAPHORES = ["cv", "cs", "ct", "cg"]
-SEMAPHORES += ["i%d" % i for i in range(9)]
-SEMAPHORES += ["pa%d_%d" % (r, h) for r in (1, 2, 3) for h in range(5)]
-SEMAPHORES += [n + "%d" % r for r in (1, 2, 3) for n in ("rk", "rm", "rc", "rs", "lk", "lm", "lc", "ls")]
-SEMAPHORES += ["o%d" % i for i in range(20)]
+SEMAPHORES = ["cv", "cs", "ct", "cg", "left", "out"]
+SEMAPHORES += ["i%d" % i for i in range(8)]
+SEMAPHORES += ["pa%d_%d" % (r, h) for r in (1, 2, 3) for h in range(len(MEANS) - 1)]
+SEMAPHORES += [n + "%d" % r for r in (1, 2, 3) for n in ("rk", "rm", "rc")]
 
+BY_ROUND = ("x", "hq", "hs", "dq", "ds", "lk", "lu", "lv", "la", "hd", "dif", "kin", "mo", "min")
 COMPUTE = {"v": "cv", "s": "cs", "t": "ct", "g": "cg"}
 
 
@@ -107,7 +123,7 @@ def rank_program(g, core, T, topo):
         n = t.shape[1]
         hi = n if hi is None else hi
         ap = t[:, lo:hi] if step == 1 else t[:, lo:hi:step]
-        return (ap, [(name, lo, hi, step)])
+        return (ap, [(name, lo, lo + (hi - lo - 1) // step * step + 1, step)])
 
     def U8(name, lo, hi):
         return (T[name][:, lo:hi].bitcast(dt.uint8), [(name, lo, hi, 1)])
@@ -117,16 +133,24 @@ def rank_program(g, core, T, topo):
         return (T[win][:, lo:hi].indirect(T[off][:, a:b]), [(win, lo, hi, 1), (off, a, b, 1)])
 
     nodes = []
-    boost = [0.0]
-    early = [True]
+    now = [0]
     behind = []
 
-    def clash(p, q):
-        if p[0] >= q[1] or q[0] >= p[1]:
-            return False
-        return not (p[2] == q[2] > 1 and (p[0] - q[0]) % p[2])
+    def plain(name):
+        return name[:-1] if name[:-1] in BY_ROUND and name[-1].isdigit() else name
 
-    def add(q, call, outs, ins, sem, inc, busy, late, slow, after=()):
+    def hint(q, writes, reads):
+        name, lo = (plain(writes[0][0]), writes[0][1]) if writes else ("", 0)
+        table = WHEN if now[0] else FRONT
+        for key in ("%s %s %d" % (q, name, lo), "%s %s" % (q, name), "%s by %s" % (q, reads[0][0] if reads else "")):
+            if key in table:
+                return table[key] + (START + PERIOD * (now[0] - 1) if now[0] else 0.0)
+        return 0.0
+
+    def clash(p, q):
+        return p[0] < q[1] and q[0] < p[1] and (p[0] - q[0]) % math.gcd(p[2], q[2]) == 0
+
+    def add(q, call, outs, ins, sem, inc, cost, move=None, after=()):
         reads = [r for _, regs in ins for r in regs]
         writes = [r for _, regs in outs for r in regs]
         me = len(nodes)
@@ -141,13 +165,13 @@ def rank_program(g, core, T, topo):
                     if not (w or rw or (bank and other["q"] != q)):
                         continue
                     if bank or clash(reg, (lo, hi, step)):
-                        strong = other["q"] != q or other["slow"] or rw
+                        strong = other["q"] != q or other["move"] is not None or rw
                         deps[n] = deps.get(n, False) or strong
         for w, regs in ((False, reads), (True, writes)):
             for name, lo, hi, step in regs:
                 seen.setdefault(name, []).append(((lo, hi, step), w, me))
-        nodes.append({"q": q, "call": call, "deps": deps, "sem": sem, "inc": inc, "busy": busy, "late": late, "slow": slow,
-                      "boost": boost[0], "early": early[0]})
+        nodes.append({"q": q, "call": call, "deps": deps, "sem": sem, "inc": inc, "cost": cost, "move": move, "when": hint(q, writes, reads),
+                      "kind": (q,) + tuple((plain(name), lo, hi) for name, lo, hi, step in writes + reads)})
         return me
 
     def width(regs):
@@ -160,83 +184,141 @@ def rank_program(g, core, T, topo):
     def op(q, call, outs, ins, pairs=False, flat=False, product=False):
         n = width(outs[0][1])
         if product:
-            busy = (n + 16) * CYCLE * PRODUCT
+            cost = (0.0, n + 16, 2)
         elif flat:
-            busy = 0.012 + 0.00022 * FACTOR * width(ins[0][1])
+            cost = (0.0, (0.012 + 0.00022 * width(ins[0][1])) / CYCLE, 0)
         elif any(len(a[1]) > 1 for a in ins):
-            busy = 0.06 + n * CYCLE * GATHER
+            cost = (0.06, n, 1)
         elif q == "s":
-            busy = 0.06 + n * CYCLE * FACTOR
+            cost = (0.06, n, 0)
         elif q == "g":
-            busy = 0.15 + 2 * n * CYCLE * FACTOR
+            cost = (0.15, 2 * n, 0)
         else:
             both = all(narrow(a[1]) for a in ins + outs if width(a[1]) > 1)
             per = 2.0 if pairs and ins[0][1][0][0][:2] != "ps" else 0.5 if both and not pairs else 1.0
-            busy = max(64, n * per) * CYCLE * FACTOR
-        add(q, lambda: call().then_inc(T.sem[COMPUTE[q]], 1), outs, ins, COMPUTE[q], 1, busy, 0.0, False)
+            cost = (0.0, max(64, n * per), 0)
+        return add(q, lambda: call().then_inc(T.sem[COMPUTE[q]], 1), outs, ins, COMPUTE[q], 1, cost)
 
-    def load(q, out, in_, sem, late=LOCAL, after=(), **kw):
+    def bytes_of(regs):
+        return width(regs) * {PLN: 1, BF: 2, U16: 2}.get(SCRATCH[regs[0][0]][2], 4)
+
+    def load(q, out, in_, sem, after=(), rows=8, **kw):
+        size = bytes_of(out[1] or in_[1]) * (2 if kw else 1)
         return add(q, lambda: queue[q].dma_start(out[0], in_[0], **kw).then_inc(T.sem[sem], 16), [out], [in_], sem, 16,
-                   0.5 if q == "g" else 0.06, late, True, after)
+                   (0.0, ISSUE / CYCLE, 5) if q == "g" else (0.05, 0, 0), (LOCAL, rows, q, size / NEAR), after)
 
     def X(ap):
         return (ap, [])
 
-    def send(out, in_, dst, rsem, lsem, late):
+    def send(out, in_, dst, rsem):
         rid, pid = topo.addr(dst)[:2]
         n = len(topo.engines(core, dst))
-        me = add("g", lambda: g.remote_dma(out_ap=out[0], in_ap=in_[0], remote_sem=T.sem[rsem], local_sem=T.sem[lsem],
+        me = add("g", lambda: g.remote_dma(out_ap=out[0], in_ap=in_[0], remote_sem=T.sem[rsem], local_sem=T.sem["left"],
                                            pid=pid, routing_id=rid, dma_engine_mask=topo.mask(core, dst)),
-                 [], [in_], lsem, n, ISSUE, late, True)
-        add("far", None, [out], [], rsem, len(topo.engines(dst, core)), 0.0, 0.0, True, (me,))
-        return me
+                 [], [in_], "left", n, (0.0, ISSUE / CYCLE, 5), (REMOTE, 128 // n, "far", bytes_of(in_[1]) / FAR))
+        return me, (out, rsem, len(topo.engines(dst, core)))
+
+    def landed(sends):
+        add("far", None, [s[1][0] for s in sends], [], sends[0][1][1], sum(s[1][2] for s in sends), (0.0, 0, 0), None, [s[0] for s in sends])
 
     def plan():
         count = len(nodes)
         if KEPT:
             return KEPT
-        before = [[(d, nodes[d]["late"] + (OWNWAKE if nodes[d]["q"] == n["q"] else WAKE) if strong else 0.0)
-                   for d, strong in n["deps"].items()] for n in nodes]
-        after = [[] for _ in nodes]
-        for i in range(count):
-            for d, wait in before[i]:
-                after[d].append((i, wait))
+        direct, above, ended = [], [], []
+        for n in nodes:
+            over, done = 0, 0
+            for d, strong in n["deps"].items():
+                over |= above[d]
+                done |= ended[d]
+            direct.append([(d, strong) for d, strong in n["deps"].items() if not (done if strong else over) >> d & 1])
+            for d, strong in n["deps"].items():
+                over |= 1 << d
+                done |= strong << d
+            above.append(over)
+            ended.append(done)
+        lane, moves = [n["q"] for n in nodes], [n["move"] for n in nodes]
+        busies = [[n["cost"][0] + n["cost"][1] * CYCLE * k[n["cost"][2]] for n in nodes] for k in CLOCKS]
+        waits = [[[(d, strong, k[8 if lane[d] == "far" else 3] if strong and lane[i] != "far" else 0.0) for d, strong in direct[i]] for i in range(count)] for k in CLOCKS]
 
-        def lay(urgency, needs, feeds, tail):
-            start, left = [0.0] * count, [len(n) for n in needs]
-            ready = list(tail)
-            taken = {q: [] for q in list(queue) + ["far"]}
-            free = [i for i in range(count) if not left[i]]
-            while free:
-                i = min(free, key=lambda i: (urgency[i], i))
-                free.remove(i)
-                busy, at, slots = nodes[i]["busy"], ready[i], taken[nodes[i]["q"]]
-                k = 0
-                while k < len(slots) and slots[k][0] < at + busy - 1e-9:
-                    at = max(at, slots[k][1])
-                    k += 1
-                if busy:
-                    slots.insert(k, (at, at + busy))
-                start[i] = at
-                for j, wait in feeds[i]:
-                    ready[j] = max(ready[j], at + busy + wait)
-                    left[j] -= 1
-                    if not left[j]:
-                        free.append(j)
-            return start
-        way = [0.0] * count
-        for i in range(count - 1, -1, -1):
-            way[i] = nodes[i]["busy"] + max([nodes[i]["late"]] + [wait + way[j] for j, wait in after[i]])
-        urgency, best = [-w - n["boost"] for w, n in zip(way, nodes)], None
-        for _ in range(PASSES):
-            urgency = [i - 1e6 if n["early"] else u for i, (u, n) in enumerate(zip(urgency, nodes))]
-            start = lay(urgency, before, after, [0.0] * count)
-            end = max(t + n["busy"] + n["late"] for t, n in zip(start, nodes))
-            if best is None or end < best[0]:
-                best = (end, start)
-            back = lay([-t - n["busy"] for t, n in zip(start, nodes)], after, before, [n["late"] for n in nodes])
-            urgency = [-t - n["busy"] for t, n in zip(back, nodes)]
-        KEPT.extend(sorted(range(count), key=lambda i: (best[1][i], i)))
+        def ends(order, same=0, old=None):
+            total, held, new = 0.0, [], []
+            last, mover, left = {}, None, dict(ONCE)
+            for i in order[:same]:
+                last[lane[i]] = i
+                if moves[i]:
+                    mover = i
+                    left.pop(moves[i][2], 0.0)
+            last.pop("far", 0)
+            for c, (k, busy, wait_of) in enumerate(zip(CLOCKS, busies, waits)):
+                done, there, why = [list(a) for a in old[c]] if same else ([0.0] * (count + 1), [0.0] * count, [count] * count)
+                new.append((done, there, why))
+                engines, once, free, moving = there[mover] if mover is not None else 0.0, dict(left), dict(last), mover
+                for i in order[same:]:
+                    cause = free.get(lane[i], count)
+                    at = done[cause]
+                    for d, strong, wait in wait_of[i]:
+                        t = there[d] + wait if strong else done[d]
+                        if t > at:
+                            at, cause = t, d
+                    why[i] = cause
+                    if moves[i]:
+                        at += once.pop(moves[i][2], 0.0)
+                        if engines > at + k[4] * moves[i][0]:
+                            why[i] = moving
+                        engines = there[i] = max(engines, at + k[4] * moves[i][0]) + moves[i][1] * (k[6] + k[7] * moves[i][3])
+                        done[i], moving = at + busy[i], i
+                    else:
+                        done[i] = there[i] = at + busy[i]
+                    if busy[i]:
+                        free[lane[i]] = i
+                i = there.index(max(there))
+                total += math.log(there[i])
+                while why[i] < count:
+                    if not above[i] >> why[i] & 1:
+                        held.append((why[i], i))
+                    i = why[i]
+            return total, held, new
+
+        turn, kinds, like = [], {}, []
+        for i, n in enumerate(nodes):
+            turn.append(max([n["when"]] + [turn[d] + (0.02 if strong else 0.001) for d, strong in direct[i]]))
+            kinds.setdefault(n["kind"], []).append(i)
+            like.append((kinds[n["kind"]], len(kinds[n["kind"]]) - 1))
+        order = sorted(range(count), key=lambda i: (turn[i], i))
+        seed, (end, held, clocks) = SEED, ends(order)
+        least = (end, order)
+        for t in range(TRIES):
+            seed = (seed * 1103515245 + 12345) % 2147483648
+            j, i = held[(seed >> 8) % len(held)]
+            ahead = seed >> 20 & 1
+            if not seed >> 22 & 3:
+                a = order.index(j if ahead else i)
+                mates = [k for k in (order[max(0, a - 24):a][::-1] if ahead else order[a + 1:a + 25]) if lane[k] == lane[order[a]]]
+                j, i = ((mates + [j])[0], i) if ahead else (j, (mates + [i])[0])
+            pairs, new, same = [(j, i)], order, count
+            if seed >> 21 & 1:
+                (J, a), (I, e) = like[j], like[i]
+                pairs = [(J[a + s], I[e + s]) for s in range(-min(a, e), min(len(J) - a, len(I) - e))]
+            for j, i in pairs:
+                a, e = new.index(j), new.index(i) + 1
+                if a >= e or above[i] >> j & 1:
+                    continue
+                same = min(same, a)
+                if ahead:
+                    moved = [k for k in new[a:e] if k == i or above[i] >> k & 1]
+                    new = new[:a] + moved + [k for k in new[a:e] if k not in moved] + new[e:]
+                else:
+                    moved = [k for k in new[a:e] if k == j or above[k] >> j & 1]
+                    new = new[:a] + [k for k in new[a:e] if k not in moved] + moved + new[e:]
+            if same == count:
+                continue
+            result = ends(new, same, clocks)
+            if result[0] < end - HEAT * COOL ** (t / TRIES) * math.log(((seed >> 3 & 1023) + 1) / 1024.0):
+                (end, held, clocks), order = result, new
+                if end < least[0]:
+                    least = (end, order)
+        KEPT.extend(least[1])
         return KEPT
 
     def issue(sequence):
@@ -262,30 +344,29 @@ def rank_program(g, core, T, topo):
             total[n["sem"]] = total.get(n["sem"], 0) + n["inc"]
             value[i] = total[n["sem"]]
             clock[i] = dict(known[n["q"]]) if n["call"] is not None else {}
-        for sem in sorted(total):
-            if known["g"].get(sem, 0) < total[sem]:
+        for sem in sorted(total, key=lambda s: s == "out"):
+            if max(k.get(sem, 0) for k in known.values()) < total[sem]:
                 g.wait_ge(T.sem[sem], total[sem])
 
     def ts(out, a, s1, o1, s2=None, o2=None):
         k1, k2 = (s[0] if isinstance(s, tuple) else s for s in (s1, s2))
         ins = [a] + [s for s in (s1, s2) if isinstance(s, tuple)]
         if o2 is None:
-            op("v", lambda: g.vector.tensor_scalar(out[0], a[0], k1, None, o1), [out], ins)
-        else:
-            op("v", lambda: g.vector.tensor_scalar(out[0], a[0], k1, k2, o1, o2), [out], ins)
+            return op("v", lambda: g.vector.tensor_scalar(out[0], a[0], k1, None, o1), [out], ins)
+        return op("v", lambda: g.vector.tensor_scalar(out[0], a[0], k1, k2, o1, o2), [out], ins)
 
     def tt(out, a, b, o):
-        op("v", lambda: g.vector.tensor_tensor(out[0], a[0], b[0], o), [out], [a, b], pairs=True)
+        return op("v", lambda: g.vector.tensor_tensor(out[0], a[0], b[0], o), [out], [a, b], pairs=True)
 
     def vcopy(out, a):
-        op("v", lambda: g.vector.tensor_copy(out[0], a[0]), [out], [a])
+        return op("v", lambda: g.vector.tensor_copy(out[0], a[0]), [out], [a])
 
     def fill(out, value):
-        op("v", lambda: g.vector.memset(out[0], value), [out], [])
+        return op("v", lambda: g.vector.memset(out[0], value), [out], [])
 
     def act(out, a, func=AF.Copy, scale=1.0, bias=0.0):
         more = {k: v for k, v, d in (("bias", bias, 0.0), ("scale", scale, 1.0)) if v != d}
-        op("s", lambda: g.scalar.activation(out[0], a[0], func, **more), [out], [a])
+        return op("s", lambda: g.scalar.activation(out[0], a[0], func, **more), [out], [a])
 
     def times(q, out, a, factor=1.0):
         if q == "s":
@@ -296,18 +377,18 @@ def rank_program(g, core, T, topo):
             ts(out, a, factor, OP.mult)
 
     def scan(out, d0, d1, first, o0, o1):
-        op("v", lambda: g.vector.tensor_tensor_scan(out[0], d0[0], d1[0], first, o0, o1), [out], [d0, d1])
+        return op("v", lambda: g.vector.tensor_tensor_scan(out[0], d0[0], d1[0], first, o0, o1), [out], [d0, d1])
 
-    def wrap(out, data, lift, lo, hi):
-        scan(A(out, lo, hi), A(data, lo, hi), A(lift, lo, hi), LOW, OP.max, OP.add)
+    def wrap(out, data, lift):
+        scan(out, data, A(lift, 0, width(data[1])), LOW, OP.max, OP.add)
 
     def quant(code, plane, a):
-        op("v", lambda: g.vector.quantize_mx(code[0], plane[0], a[0]), [code, plane], [a], flat=True)
+        return op("v", lambda: g.vector.quantize_mx(code[0], plane[0], a[0]), [code, plane], [a], flat=True)
 
     def mm(bank, lhs, lhs_s, a, rhs, rhs_s, lo, hi):
         out, w, ws_ = A(bank, 0, hi - lo), A(lhs, a, a + 128), A(lhs_s, a, a + 128)
         x, xs_ = A(rhs, lo, hi), A(rhs_s, lo, hi)
-        op("t", lambda: g.tensor.matmul_mx(out[0], w[0], ws_[0], x[0], xs_[0], True, True), [out], [w, ws_, x, xs_], product=True)
+        return op("t", lambda: g.tensor.matmul_mx(out[0], w[0], ws_[0], x[0], xs_[0], True, True), [out], [w, ws_, x, xs_], product=True)
 
     def iota(out, pattern, cm, base=0, small=False):
         if small:
@@ -324,233 +405,198 @@ def rank_program(g, core, T, topo):
     def SLOT(name, i):
         return A(name, i, 3 * K24, 3)
 
-    load("y", A("ut"), X(T.u[:]), "i0")
-    load("s", A("lk0", 0, K24), X(T.gl[:]), "i3")
-    load("s", A("lk0", K24, 2 * K24), X(T.gk[:]), "i1")
-    load("y", A("x0", 4 * HC, 4 * C), X(T.x[:, 4 * HC:4 * C]), "i2", late=LOCAL + 0.6)
-    first = load("y", A("x0", 0, 4 * HC), X(T.x[:, 0:4 * HC]), "i7", late=LOCAL + 1.0)
-    if MEANS[-1] < C:
-        load("y", A("xc", 4 * MEANS[-1], 4 * C), X(T.x[:, 4 * MEANS[-1]:4 * C]), "i8", late=LOCAL + 1.5, after=(first,))
-    load("y", U8("wq", 0, 512), X(T.wc[:]), "i4", after=(first,))
-    load("y", A("wp"), X(T.ws[:]), "i5", after=(first,))
+    def runs(bounds):
+        return list(zip(bounds, bounds[1:]))
 
+    load("y", A("ut"), X(T.u[:]), "i0")
+    load("y", A("lk0", 0, K24), X(T.gl[:]), "i3")
+    load("y", A("lk0", K24, 2 * K24), X(T.gk[:]), "i1")
+    for (bank, lo, hi), sem in zip(FIRST, ("i2", "i7")):
+        load("y", A("x0", 4 * lo, 4 * hi), X(T.x[:, 4 * lo:4 * hi]), sem)
+    behind.extend(range(len(nodes)))
+    behind.append(load("y", U8("wq", 0, 512), X(T.wc[:]), "i4"))
+    load("y", A("wp"), X(T.ws[:]), "i5")
+
+    iota(A("pos", 0, 16), [[-1, 16]], 1, base=16)
+    iota(A("pos", 16, 32), [[0, 4], [-4, 4]], 1, base=16)
     iota(A("pi"), [[0, K24]], 1)
-    iota(A("pos", 0, 16), [[1, 16]], 0, small=True)
-    iota(A("pos", 16, 32), [[0, 4], [1, 4]], 0, small=True)
     iota(A("ulist"), [[1, 2], [16, 8]], 0)
+    ts(A("pe", 0, 16), A("pos", 0, 16), 15, OP.bitwise_and)
+    ts(A("pe", 16, 32), A("pos", 16, 32), 2, OP.logical_shift_right, 3, OP.bitwise_and)
+    ts(A("pa"), A("pe"), 0.0, OP.is_equal)
+    ts(A("pb"), A("pe"), 1.0, OP.is_equal)
+    tt(A("pat"), A("pa"), A("pb"), OP.subtract)
+    ts(A("pat", 15, 32, 4), A("pa", 15, 32, 4), -2.0, OP.add)
+    ts(A("pm"), A("pi"), 15, OP.bitwise_and)
+    ts(A("pq"), A("pi", 0, 1), 3, OP.bitwise_and)
+    vcopy(A("pm16"), A("pm"))
+    vcopy(A("ulist16"), A("ulist"))
+    act(A("w16"), IND("pat", "pm16", 0, K24, 0, 16))
+    act(A("w4"), IND("pat", "pm16", 0, K24, 16, 32))
+    ts(A("col", 0, 1), A("pq"), 4 * (UNIT + HC), OP.add)
+    ts(A("col", 1, 2), A("pq"), float(C), OP.mult, UNIT + HC, OP.add)
     fill(A("one"), 1.0)
     fill(A("et"), 0.0)
     eye = A("et", 3, 515, 4)
     op("g", lambda: g.affine_select(eye[0], T.one[:], [[-1, 128]], OP.is_equal, 0.0, 0, 1), [eye], [A("one")])
+    for b in range(4):
+        quant(A("eq", 128 * b, 128 * b + 128), A("es", 128 * b, 128 * b + 128), A("et", 3 - b, 515 - b))
     iota(A("q16"), [[16, K24]], 0)
     iota(A("nat"), [[1, C]], 0, base=-HC, small=True)
-    ts(A("pm"), A("pi"), 15, OP.bitwise_and)
-    ts(A("pq", 0, 1), A("pi", 0, 1), 15, OP.bitwise_and)
-    ts(A("pq", 1, 2), A("pi", 0, 1), 2, OP.logical_shift_right, 3, OP.bitwise_and)
-    ts(A("pq", 2, 3), A("pi", 0, 1), 3, OP.bitwise_and)
-    vcopy(A("col", 0, 3), A("pq"))
-    vcopy(A("pm16"), A("pm"))
-    for i in (1, 0):
-        ts(A("pa", 16 * i, 16 * i + 16), A("pos", 16 * i, 16 * i + 16), A("col", i, i + 1), OP.is_equal, 2 * BIG, OP.mult)
-        ts(A("pb", 16 * i, 16 * i + 16), A("pos", 16 * i, 16 * i + 16), A("col", i, i + 1), OP.is_le, -BIG, OP.mult)
-    tt(A("pat"), A("pa"), A("pb"), OP.add)
-    ts(A("pat", 15, 32, 4), A("pat", 15, 32, 4), -2 * BIG, OP.add)
-    vcopy(A("ulist16"), A("ulist"))
-    early[0] = EARLY
-    act(A("w16"), IND("pat", "pm16", 0, K24, 0, 16))
-    act(A("w4"), IND("pat", "pm16", 0, K24, 16, 32))
-    fill(A("t0", 1, 2 * C, 2), -64.0)
-    ts(A("col", 3, 4), A("pq", 2, 3), 4 * (BIG + HC), OP.add)
-    ts(A("col", 4, 5), A("pq", 2, 3), float(C), OP.mult, BIG + HC, OP.add)
     tt(A("cw"), A("pm"), A("q16"), OP.add)
-    for name in ("hm0", "hm1", "hm2"):
-        fill(A(name), 0.0)
-    early[0] = False
+    fill(A("t0", 0, 2 * C, 2), 0.0)
+    for t in range(3):
+        fill(A("wm%d" % t, 32, None, 48), 0.0)
 
     def partner(r):
         return T.cores[rank ^ MASK[r - 1]]
 
     def send_children(r):
-        send(A("kin%d" % r), A("lu%d" % (r - 1), K24, 2 * K24), partner(r), "rk%d" % r, "lk%d" % r, SMALL)
+        landed([send(A("kin%d" % r), A("lu%d" % (r - 1), K24, 2 * K24), partner(r), "rk%d" % r)])
+
+    def elements(out, data, wrapped, lo, hi):
+        wrap(A(wrapped, lo, hi), A(data, lo, hi), "w4")
+        ts(A(out, lo // 4, hi // 4), W4(wrapped, lo, hi), 4.0 * UNIT, OP.mult, A("col", 0, 1), OP.add)
 
     def lists_of(n):
-        L = "lk%d" % n
-        early[0] = n == 0
+        L, hd, dif = "lk%d" % n, "hd%d" % n, "dif%d" % n
         vcopy(A("lu%d" % n), A(L))
-        for t in range(4):
-            ts(A("la", K24 * t, K24 * (t + 1)), A(L, 0, K24), 4.0, OP.mult, float(t), OP.add)
-        early[0] = False
-        ts(A("lv"), A(L), 2.0, OP.mult)
-        tt(SLOT("hd", 0), A(L, K24, 2 * K24), A("cw"), OP.subtract)
-        tt(SLOT("hd", 1), A("cw"), A(L, 0, K24), OP.subtract)
-        vcopy(SLOT("hd", 2), A(L, 0, K24))
-        tt(A("dif", 0, K12), A(L, 3 * K12, 4 * K12), A(L, 0, K12), OP.subtract)
-        tt(A("dif", K12, K24), A(L, 2 * K12, 3 * K12), A(L, K12, 2 * K12), OP.subtract)
-
-    early[0] = True
-    quant(A("uq"), A("us"), A("ut"))
-    for h in (0, 1):
-        early[0] = h == 0
-        src = (T.uq[:, 0:128].bitcast(dt.uint32).indirect(T.ulist16[:, 8 * h:8 * h + 8]), [("uq", 0, 128, 1), ("ulist16", 0, 16, 1)])
-        vcopy((T.uq2[:, 128 * h:128 * h + 128].bitcast(dt.uint32), [("uq2", 128 * h, 128 * h + 128, 1)]), src)
-        act(A("us2", 128 * h, 128 * h + 128),
-            (T.us[:, 0:128].indirect(T.ulist16[:, 8 * h:8 * h + 8]), [("us", 0, 128, 1), ("ulist16", 0, 16, 1)]))
-    lists_of(0)
-    early[0] = True
-    send_children(1)
-    load("g", A("vt"), X(T.v[:]), "i6", after=(first,))
-    early[0] = False
-
-    def signs(x, h):
-        lo, hi = HC * h, HC * (h + 1)
-        quant(A("xq", lo, hi), A("xs", lo, hi), A(x, 4 * lo, 4 * hi))
-        mm("ps%d" % (5 - h), "uq2", "us2", 0, "xq", "xs", lo, hi)
-        if h == 0 or x == "x0":
-            ts(A("b", lo, hi), A("ps%d" % (5 - h), 0, HC), 0.0, OP.is_gt)
+        if n == 0:
+            for t in range(4):
+                ts(A("la0", K24 * t, K24 * (t + 1)), A(L, 0, K24), 4.0, OP.mult, float(t), OP.add)
         else:
-            act(A("b", lo, hi), A("ps4", 0, HC), AF.Sign)
+            act(A("ln"), IND("nat", "lu%d" % n, 0, K24), scale=1.0 / UNIT)
+            elements("la%d" % n, "ln", "lw", 0, C)
+        ts(A("lv%d" % n), A(L), 2.0, OP.mult, 1.0, OP.add)
+        tt(SLOT(hd, 0), A(L, K24, 2 * K24), A("cw"), OP.subtract)
+        tt(SLOT(hd, 1), A(L, 0, K24), A("cw"), OP.subtract)
+        vcopy(SLOT(hd, 2), A(L, 0, K24))
+        tt(A(dif, 0, K12), A(L, 3 * K12, 4 * K12), A(L, 0, K12), OP.subtract)
+        tt(A(dif, K12, K24), A(L, 2 * K12, 3 * K12), A(L, K12, 2 * K12), OP.subtract)
 
-    def turns():
+    def exchange(r):
+        L, Ln = "lk%d" % (r - 1), "lk%d" % r
         mm("ps6", "uq2", "us2", 128, "xq", "xs", 0, HC)
         act(A("ts"), A("ps6", 0, HC), AF.Sign, scale=-1.0)
-
-    def choose(s):
-        scan(A("ho" + s), A("hm" + s), A("hd"), 0.0, OP.mult, OP.add)
-        vcopy(A("d" + s), SLOT("ho" + s, 2))
-
-    signs("x0", 1)
-    for b in range(4):
-        quant(A("eq", 128 * b, 128 * b + 128), A("es", 128 * b, 128 * b + 128), A("et", 3 - b, 515 - b))
-
-    for r in range(1, ROUNDS + 1):
-        x, xn = "x%d" % (r - 1), "x%d" % r
-        lu, L, Ln = "lu%d" % (r - 1), "lk%d" % (r - 1), "lk%d" % r
-        signs(x, 0)
-        if not LATE:
-            turns()
-        for h, (lo, hi) in enumerate(zip(MEANS, MEANS[1:])):
-            for t in range(4):
-                act(A("pp", 4 * lo + t, 4 * hi, 4), IND(x, "la", K24 * t + lo // 16, K24 * t + hi // 16))
-            load("g", A("pp", 4 * lo, 4 * hi), A(x, 4 * lo, 4 * hi), "pa%d_%d" % (r, h), late=ADDING, accum_op=OP.add)
-        lo = MEANS[-1]
-        if lo < C:
-            if r > 1:
-                act(A("xc", 4 * lo, 4 * C), A(x, 4 * lo, 4 * C))
-            for t in range(4):
-                tt(A("pp", 4 * lo + t, 4 * C, 4), IND(x, "la", K24 * t + lo // 16, K24 * (t + 1)), A("xc", 4 * lo + t, 4 * C, 4), OP.add)
-        act(A("ga"), IND("b", lu, 0, K24), AF.Relu, scale=2.0)
-        ts(A("gb"), IND("b", lu, K24, 2 * K24), 0.5, OP.is_gt, 2.0, OP.add)
-        scan(A("t0", 0, 2 * C, 2), A("ga"), A("gb"), 0.0, OP.max, OP.subtract)
-        ts(A("gc", 0, 2 * C, 2), IND("t0", "lv", K24, 2 * K24), 0.0, OP.is_equal, -6.0, OP.add)
-        act(A("gc", 1, 2 * C, 2), IND("t0", "lv", 0, K24), AF.Relu, scale=2.0, bias=2.0)
-        scan(A("t1", 15, 15 + 2 * C), A("t0"), A("gc"), LOW, OP.max, OP.add)
-        for q, lo, hi in CLIMB:
-            times(q, A("ge", lo, hi), IND("t1", "lv", lo // 16, hi // 16, 16, 15 + 2 * C))
-            scan(A("gew", lo, hi), A("ge", lo, hi), A("w16", 0, hi - lo), LOW, OP.max, OP.add)
-        scan(A("t0w"), A("t0", 0, 2 * C, 2), A("w16"), LOW, OP.max, OP.add)
-        ts(SLOT("hm0", 2), W16("t0w"), -BIG - 1.5, OP.is_lt)
-        ts(SLOT("hm0", 1), W16("t0w"), -BIG - 2.5, OP.is_lt)
-        choose("0")
-        act(A("dn"), IND("nat", "d0", 0, K24))
-        ts(A("m2"), SLOT("hm0", 2), -2.0, OP.mult, -BIG, OP.add)
-        tt(A("ref2"), A("m2"), W16("t0w"), OP.subtract)
-        if SIDE:
-            ts(A("thr"), A("ref2"), -BIG - 6.0, OP.add)
-            ts(A("ref1"), SLOT("hm0", 2), 2.0, OP.mult, -BIG, OP.add)
-            scan(A("t1w"), A("gc", 0, 2 * C, 2), A("w16"), LOW, OP.max, OP.add)
-            scan(A("t2w"), A("gc", 1, 2 * C, 2), A("w16"), LOW, OP.max, OP.add)
-            tt(SLOT("hm1", 1), W16("t1w"), A("thr"), OP.not_equal)
-            tt(SLOT("hm1", 2), W16("t2w"), A("ref1"), OP.not_equal)
-        else:
-            ts(A("thr"), W16("t0w"), -4.5, OP.add)
-            ts(A("ref1"), SLOT("hm0", 2), -4.0, OP.mult, -BIG - 4.0, OP.add)
-            scan(A("t1w"), A("t1", 16, 15 + 2 * C, 2), A("w16"), LOW, OP.max, OP.add)
-            tt(A("cl"), W16("t1w"), A("thr"), OP.is_gt)
-            tt(SLOT("hm1", 1), W16("t1w"), A("ref1"), OP.not_equal)
-            tt(SLOT("hm1", 2), A("cl"), SLOT("hm0", 2), OP.not_equal)
-        choose("1")
-        for q, lo, hi in FOLLOW:
-            times(q, A("qn", lo, hi), IND("dn", "d1", lo // 16, hi // 16))
-        ts(A("e2"), W16("gew", 0, 2 * C), -BIG - 6.0, OP.is_equal)
-        tt(SLOT("hm2", 1), A("e2", K24, 2 * K24), A("ref2"), OP.not_equal)
-        tt(SLOT("hm2", 2), A("e2", 0, K24), SLOT("hm0", 2), OP.not_equal)
-        choose("2")
-        for q, lo, hi in POINT:
-            times(q, A("on", lo, hi), IND("qn", "d2", lo // 16, hi // 16))
-        for lo, hi in zip(LISTS, LISTS[1:]):
-            wrap("ow", "on", "w4", lo, hi)
-            ts(A("of", lo // 4, hi // 4), W4("ow", lo, hi), 4.0, OP.mult, A("col", 3, 4), OP.add)
-        for h, (lo, hi, mid) in enumerate(PIECES):
-            boost[0] = BOOST * (len(PIECES) - 1 - h)
-            for q, a, e in (("v", lo, mid), ("s", mid, hi)):
-                if e > a:
-                    times(q, A("zt", 4 * a, 4 * e), IND("pp", "of", a // 4, e // 4), 0.5)
-            quant(A("zq", lo, hi), A("zs", lo, hi), A("zt", 4 * lo, 4 * hi))
-            for b in range(4):
-                mm("ps%d" % (4 * (h % 2) + b), "wq", "wp", 128 * b, "zq", "zs", lo, hi)
-            boost[0] = 0.0
-            for b in range(4):
-                times(COPIES[4 * h + b], A("h", C * b + lo, C * b + hi), A("ps%d" % (4 * (h % 2) + b), 0, hi - lo), 0.03125)
-        for q, lo, hi in READS:
-            times(q, A("mn", lo, hi), IND("on", "kin%d" % r, lo // 16, hi // 16))
-        wrap("mw", "mn", "w16", 0, HC)
-        ts(A("mu"), W16("mw", 0, HC), BIG + HC, OP.add)
-        wrap("mw", "mn", "w4", HC, C)
-        ts(A("mo"), W4("mw", HC, C), A("col", 4, 5), OP.add)
-        places = send(A("min%d" % r), A("mo"), partner(r), "rm%d" % r, "lm%d" % r, SMALL)
-        for b in range(4):
-            for q, lo, hi in (("v", 0, PARTS[b]), ("s", PARTS[b], HC)):
-                if hi > lo:
-                    times(q, A("ht", 4 * lo + b, 4 * hi, 4), IND("h", "mu", lo // 16, hi // 16, C * b, C * (b + 1)))
-        quant(A("hq"), A("hs"), A("ht"))
-        if r == 2:
-            behind.append(len(nodes) - 1)
-            quant(A("vq"), A("vs"), A("vt"))
-        behind.append(places)
-        behind.append(send(U8("dq%d" % r, 0, HC), U8("hq", 0, HC), partner(r), "rc%d" % r, "lc%d" % r, CODES))
-        plane = send(A("ds%d" % r), A("hs"), partner(r), "rs%d" % r, "ls%d" % r, PLANE)
-        if OWN > HC:
-            tt(A(xn, 4 * HC, 4 * OWN), IND("h", "min%d" % r, 0, (OWN - HC) // 4), A(x, 4 * HC, 4 * OWN), OP.add)
-        if OWN < C:
-            act(A(xn, 4 * OWN, 4 * C), IND("h", "min%d" % r, (OWN - HC) // 4, 4 * K12))
-            load("g", A(xn, 4 * OWN, 4 * C), A(x, 4 * OWN, 4 * C), "pa%d_4" % r, late=ADDING, accum_op=OP.add)
-        if r < ROUNDS:
-            signs(xn, 1)
-        else:
-            quant(A("xq", HC, C), A("xs", HC, C), A(xn, 4 * HC, 8 * HC))
-        if LATE:
-            turns()
-        wrap("tw", "ts", "w16", 0, HC)
+        wrap(A("tw"), A("ts"), "w16")
         for i in range(2):
-            ts(A("tt", K12 * i, K12 * (i + 1)), W16("tw", 0, HC), 0.5 - BIG, OP.is_gt)
-        tt(A("ud"), A("tt"), A("dif"), OP.mult)
+            ts(A("tt", K12 * i, K12 * (i + 1)), W16("tw", 0, HC), -0.5, OP.is_gt)
+        tt(A("ud"), A("tt"), A("dif%d" % (r - 1)), OP.mult)
         tt(A(Ln, 0, K24), A(L, 0, K24), A("ud"), OP.add)
         tt(A(Ln, 3 * K12, 4 * K12), A(L, 3 * K12, 4 * K12), A("ud", 0, K12), OP.subtract)
         tt(A(Ln, 2 * K12, 3 * K12), A(L, 2 * K12, 3 * K12), A("ud", K12, K24), OP.subtract)
         if r < ROUNDS:
             lists_of(r)
-            behind.append(plane)
             send_children(r + 1)
         else:
             vcopy(A("lu%d" % r), A(Ln))
-            mm("ps4", "vq", "vs", 0, "xq", "xs", HC, C)
-            act(A("yo", HC, C), A("ps4", 0, HC))
             act(A("lro"), IND("nat", "lu%d" % r, 0, 2 * K24), AF.Identity, bias=float(HC))
-            load("y", X(T.oc[:, 4 * HC:4 * C]), U8("xq", HC, C), "o0")
-            for k in range(4):
-                load("y", X(T.osc[4 * k:4 * k + 4, HC:C]), (T.xs[32 * k:32 * k + 4, HC:C], [("xs", HC, C, 1)]), "o%d" % (1 + k))
-            load("y", X(T.y[:, HC:C]), A("yo", HC, C), "o5")
-            for k in range(8):
-                load("y", X(T.lr[k:k + 1, :]), (T.lro[16 * k:16 * k + 1, :], [("lro", 0, 2 * C, 1)]), "o%d" % (6 + k))
+            load("y", X(T.lr[:]), (T.lro[0:128:16, :], [("lro", 0, 2 * C, 1)]), "out", rows=1)
+
+    quant(A("uq"), A("us"), A("ut"))
+    for h in (0, 1):
+        src = (T.uq[:, 0:128].bitcast(dt.uint32).indirect(T.ulist16[:, 8 * h:8 * h + 8]), [("uq", 0, 128, 1), ("ulist16", 0, 16, 1)])
+        vcopy((T.uq2[:, 128 * h:128 * h + 128].bitcast(dt.uint32), [("uq2", 128 * h, 128 * h + 128, 1)]), src)
+        act(A("us2", 128 * h, 128 * h + 128),
+            (T.us[:, 0:128].indirect(T.ulist16[:, 8 * h:8 * h + 8]), [("us", 0, 128, 1), ("ulist16", 0, 16, 1)]))
+    lists_of(0)
+    send_children(1)
+    load("g", A("vt"), X(T.v[:]), "i6")
+
+    def signs(x, bank, lo, hi):
+        quant(A("xq", lo, hi), A("xs", lo, hi), A(x, 4 * lo, 4 * hi))
+        mm(bank, "uq2", "us2", 0, "xq", "xs", lo, hi)
+        ts(A("t0", 2 * lo + 1, 2 * hi, 2), A(bank, 0, hi - lo), 0.0, OP.is_le, 1.0, OP.add)
+
+    def result(q, bank, code, plane, lo, hi, end):
+        quant(A(code, lo, hi), A(plane, lo, hi), A("x%d" % ROUNDS, 4 * lo, 4 * hi))
+        mm(bank, "vq", "vs", 0, code, plane, lo, hi)
+        times(q, A("yo", lo, end), A(bank, 0, end - lo))
+
+    def stores(code, plane, lo, hi):
+        load("y", X(T.oc[:, 4 * lo:4 * hi]), U8(code, lo, hi), "out")
+        for k in range(4):
+            load(OSC[k], X(T.osc[4 * k:4 * k + 4, lo:hi]), (T[plane][32 * k:32 * k + 4, lo:hi], [(plane, lo, hi, 1)]), "out", rows=1)
+        load("y", X(T.y[:, lo:hi]), A("yo", lo, hi), "out")
+
+    def step(r, t):
+        table, pair, lv, masks = "t%d" % t, "g%d" % t, "lv%d" % (r - 1), "wm%d" % t
+        for lo, hi in runs(RUNS):
+            act(A(pair, 2 * lo, 2 * hi, 2), IND(table, lv, lo // 16, hi // 16), AF.Abs, bias=-2.0)
+            ts(A(pair, 2 * lo + 1, 2 * hi, 2), IND(table, lv, K24 + lo // 16, K24 + hi // 16), 2.0, OP.is_equal)
+            if t < 2:
+                scan(A("t%d" % (t + 1), 2 * lo, 2 * hi), A(pair, 2 * lo, 2 * hi), A("t0", 2 * lo, 2 * hi), 4.0, OP.min, OP.add)
+        for lo, hi in runs(RUNS if t == 2 else (0, C)):
+            wrap(A(masks, 3 + 3 * lo, 3 + 3 * hi, 3), A(pair, 2 * lo + 1, 2 * hi, 2), "w16")
+            wrap(A(masks, 19 + 3 * lo, 19 + 3 * hi, 3), A(pair, 2 * lo, 2 * hi, 2), "w16")
+        scan(A("ho%d" % t), A(masks, 32, None, 16), A("hd%d" % (r - 1)), 0.0, OP.mult, OP.add)
+        vcopy(A("d%d" % t), SLOT("ho%d" % t, 2))
+
+    for r in range(1, ROUNDS + 1):
+        x, xn = "x%d" % (r - 1), "x%d" % r
+        now[0] = r
+        for bank, lo, hi in (FIRST if r == 1 else SIGNS[1:]):
+            signs(x, bank, lo, hi)
+        exchange(r)
+        for q, lo, hi in (SUMS if r > 1 else ()):
+            times(q, A("pp", 4 * lo, 4 * hi), IND(x, "la%d" % (r - 1), lo // 4, hi // 4))
+        for q, lo, hi in (PLANES if r == 1 else ()):
+            for t in range(4):
+                times(q[t], A("pp", 4 * lo + t, 4 * hi, 4), IND(x, "la0", K24 * t + lo // 16, K24 * t + hi // 16))
+        for h, (lo, hi) in enumerate(runs(MEANS)):
+            load("g", A("pp", 4 * lo, 4 * hi), A(x, 4 * lo, 4 * hi), "pa%d_%d" % (r, h), accum_op=OP.add)
+        for t in range(3):
+            step(r, t)
+        act(A("dn"), IND("nat", "d0", 0, K24), scale=1.0 / UNIT)
+        for q, lo, hi in FOLLOW:
+            times(q, A("qn", lo, hi), IND("dn", "d1", lo // 16, hi // 16))
+        for q, lo, hi in POINT:
+            times(q, A("on", lo, hi), IND("qn", "d2", lo // 16, hi // 16))
+            elements("of", "on", "ow", lo, hi)
+        for h, (lo, hi, mid) in enumerate(PIECES):
+            for q, a, e in (("v", lo, mid), ("s", mid, hi)):
+                times(q, A("zt", 4 * a, 4 * e), IND("pp", "of", a // 4, e // 4), 0.5)
+            quant(A("zq", lo, hi), A("zs", lo, hi), A("zt", 4 * lo, 4 * hi))
+        last = None
+        for i, (h, b) in enumerate(PRODUCTS):
+            lo, hi, mid = PIECES[h]
+            behind.extend([last] if i else [])
+            last = mm("ps%d" % (i % 8), "wq", "wp", 128 * b, "zq", "zs", lo, hi)
+            times(COPIES[i], A("h", C * b + lo, C * b + hi), A("ps%d" % (i % 8), 0, hi - lo), 0.03125)
+        for lo, hi in runs((0, HC, C)):
+            act(A("mn", lo, hi), IND("on", "kin%d" % r, lo // 16, hi // 16))
+        wrap(A("mw", 0, HC), A("mn", 0, HC), "w16")
+        ts(A("mu"), W16("mw", 0, HC), UNIT, OP.mult, UNIT + HC, OP.add)
+        wrap(A("mw", HC, C), A("mn", HC, C), "w4")
+        ts(A("mo%d" % r), W4("mw", HC, C), UNIT, OP.mult, A("col", 1, 2), OP.add)
+        places = send(A("min%d" % r), A("mo%d" % r), partner(r), "rm%d" % r)
+        landed([places])
+        for b in range(4):
+            for q, lo, hi in (("v", 0, PARTS[b]), ("s", PARTS[b], HC)):
+                if hi > lo:
+                    times(q, A("ht", 4 * lo + b, 4 * hi, 4), IND("h", "mu", lo // 16, hi // 16, C * b, C * (b + 1)))
+        quant(A("hq%d" % r), A("hs%d" % r), A("ht"))
+        behind.append(places[0])
+        codes = send(U8("dq%d" % r, 0, HC), U8("hq%d" % r, 0, HC), partner(r), "rc%d" % r)
+        behind.append(codes[0])
+        plane = send(A("ds%d" % r), A("hs%d" % r), partner(r), "rc%d" % r)
+        landed([codes, plane])
+        tt(A(xn, 4 * HC, 4 * C), IND("h", "min%d" % r, 0, 4 * K12), A(x, 4 * HC, 4 * C), OP.add)
+        if r == 2:
+            quant(A("vq"), A("vs"), A("vt"))
+        bank, lo, hi = SIGNS[0]
+        if r < ROUNDS:
+            signs(xn, bank, lo, hi)
+        else:
+            result("s", bank, "xq", "xs", HC, C, C)
+            stores("xq", "xs", HC, C)
         for b in range(4):
             mm("ps%d" % b, "eq", "es", 128 * b, "dq%d" % r, "ds%d" % r, 0, HC)
-            tt(A(xn, b, 4 * HC, 4), A("ps%d" % b, 0, HC), A(x, b, 4 * HC, 4), OP.add)
+            for bank, a, e in SIGNS[1:]:
+                e = min(e, HC)
+                tt(A(xn, 4 * a + b, 4 * e, 4), A("ps%d" % b, a, e), A(x, 4 * a + b, 4 * e, 4), OP.add)
 
-    quant(A("xq", 0, HC), A("xs", 0, HC), A("x3", 0, 4 * HC))
-    mm("ps5", "vq", "vs", 0, "xq", "xs", 0, HC)
-    load("s", X(T.oc[:, 0:4 * HC]), U8("xq", 0, HC), "o14")
-    for k in range(4):
-        load("y" if k < 2 else "s", X(T.osc[4 * k:4 * k + 4, 0:HC]), (T.xs[32 * k:32 * k + 4, 0:HC], [("xs", 0, HC, 1)]), "o%d" % (15 + k))
-    vcopy(A("yo", 0, HC), A("ps5", 0, HC))
-    load("y", X(T.y[:, 0:HC]), A("yo", 0, HC), "o19")
+    for q, (bank, a, e) in zip("sv", SIGNS[1:]):
+        result(q, bank, "zq", "zs", a, e, min(e, HC))
+    stores("zq", "zs", 0, HC)
     issue(plan())

import math
from concourse.mybir import dt, AluOpType, ActivationFunctionType

OP = AluOpType
AF = ActivationFunctionType
C, HC, K24, K12 = 384, 192, 24, 12
MASK = [1, 2, 3]
ROUNDS = 3
LOW = -64.0
UNIT = 512.0

FIRST = (("ps4", 128, 384), ("ps5", 0, 128))
SIGNS = (("ps4", 256, 384), ("ps5", 128, 256), ("ps7", 0, 128))
SUMS = (("s", 0, 128), ("s", 128, 176), ("v", 176, 256), ("s", 256, 320), ("s", 320, 384))
PLANES = (("ssss", 0, 256), ("svss", 256, 384))
OSC = "yyss"
MEANS = (0, 256, 384)
RUNS = (0, 256, 384)
FOLLOW = (("s", 0, 192), ("v", 192, 384))
POINT = (("v", 0, 128), ("s", 128, 384))
PIECES = ((0, 128, 64), (128, 256, 160), (256, 384, 320))
PRODUCTS = ((0, 0), (0, 1), (0, 2), (0, 3), (1, 0), (1, 1), (1, 2), (2, 0), (2, 1), (2, 2), (1, 3), (2, 3))
COPIES = "vsvv" "svsv" "vvvv"
PARTS = (0, 0, 192, 96)

CYCLE = 0.00083
CLOCKS = ((1.0, 1.4, 1.0, 0.22, 0.8, 1.0, 0.01, 1.0, 0.22), (1.25, 1.9, 1.5, 0.18, 1.0, 1.6, 0.02, 1.0, 0.22),
          (1.4, 2.6, 1.8, 0.25, 1.2, 2.0, 0.02, 1.2, 0.4), (1.1, 1.3, 1.2, 0.28, 1.4, 2.5, 0.04, 1.3, 0.5))
ISSUE, LOCAL, REMOTE, NEAR, FAR = 0.4, 1.1, 0.9, 25e3, 14e3
ONCE = {"g": 1.0, "far": 1.5}
START, PERIOD = 1.3, 14.0
FRONT = {"v uq": 1.5, "s w16": 1.55, "v uq2 0": 1.9, "s us2 0": 1.9, "s w4": 2.2, "s us2": 2.4, "v uq2": 3.0, "v la": 2.6, "v lv": 2.9,
         "v lu": 3.3, "v hd": 3.35, "v dif": 4.1, "v eq": 1.3, "v eq 256": 1.7, "v eq 384": 2.1, "g q16": 0.9, "g vt": 1.0, "g nat": 1.1, "y x": 0.02, "y lk": 0.03}
WHEN = {"v xq": 1.2, "s pp": 1.25, "v pp": 1.45, "v t0": 1.85,
        "v g0": 2.3, "s g0": 2.3, "s pp 2": 2.8, "s pp 3": 2.8, "s pp 1024": 2.9, "v t1": 2.9, "s pp 1025": 3.0, "v wm0": 3.2,
        "s g1": 3.45, "v g1": 3.55, "s pp 1280": 4.0, "s pp 1026": 4.0, "s pp 1027": 4.0, "v ho0": 4.1, "v t2": 4.15, "s ts": 4.4,
        "v wm1": 4.45, "v d0": 4.6, "v wm1 19": 4.7, "s g2": 4.7, "v g2": 4.85, "s dn": 5.25, "v ho1": 5.4, "v wm2": 5.45,
        "v d1": 5.75, "v tw": 5.8, "v ho2": 5.95, "v qn": 6.05, "s qn": 6.05, "v d2": 6.3, "v tt": 6.4,
        "v on": 6.6, "s on": 6.6, "v ud": 6.8, "v ow 0": 7.0, "v ow": 7.15, "s mn 0": 7.15, "v of 0": 7.3, "v lk": 7.35, "v of": 7.5,
        "v zt": 7.55, "s zt": 7.55, "v zq 0": 8.1, "v zt 1024": 8.25, "v zq 128": 8.65, "v mw 0": 8.75, "v h": 8.85, "s h": 8.95,
        "v zq": 9.0, "s mn": 9.1, "v h 768": 9.1, "v mu": 9.3, "v mw": 9.6, "v h 896": 9.65, "v mo": 9.9, "s ht": 10.0, "v ht": 10.4,
        "v lu": 10.8, "v dif": 10.9, "s ln": 11.0, "v hq": 11.2, "v lv": 11.3, "v hd": 11.3, "s lro": 11.3, "v vq": 11.5,
        "v x 768": 11.6, "v lw": 12.4, "v xq 256": 13.0, "v xq 192": 13.0, "v la": 13.1,
        "t by eq": 14.0, "t by vq": 14.1, "v x": 14.3, "s yo": 14.5, "v t0 513": 15.05, "v yo": 16.0}
TRIES, HEAT, COOL, SEED = 30000, 0.005, 0.2, 7
KEPT = []

BF, F16, F32, I32, U16, COD, PLN = "bfloat16", "float16", "float32", "int32", "uint16", "float8_e4m3fn_x4", "uint8"


def _buffers():
    s = {}

    def sb(dtype, n, *names):
        for name in names:
            s[name] = ("sbuf", [128, n], dtype)
    sb(BF, 4 * C, "x0", "x1", "x2", "x3", "pp", "zt", "h")
    sb(BF, 4 * HC, "ht")
    sb(COD, C, "xq", "zq")
    sb(PLN, C, "xs", "zs")
    sb(COD, HC, "hq1", "hq2", "hq3", "dq1", "dq2", "dq3")
    sb(PLN, HC, "hs1", "hs2", "hs3", "ds1", "ds2", "ds3")
    sb(BF, 512, "ut", "vt")
    sb(COD, 128, "uq", "vq")
    sb(PLN, 128, "us", "vs")
    sb(COD, 256, "uq2")
    sb(PLN, 256, "us2")
    sb(COD, 512, "wq", "eq")
    sb(PLN, 512, "wp", "es")
    sb(BF, 128, "one")
    sb(BF, 516, "et")
    sb(I32, 16, "ulist")
    sb(U16, 16, "ulist16")
    sb(I32, K24, "pi", "pm", "q16")
    sb(I32, 32, "pos", "pe")
    sb(I32, 1, "pq")
    sb(U16, K24, "pm16")
    sb(F32, 32, "pa", "pb")
    sb(BF, 32, "pat")
    sb(BF, C, "w16", "w4", "nat")
    sb(F32, K24, "cw")
    sb(F32, 2, "col")
    sb(I32, 2 * K24, "lk0")
    sb(F32, 2 * K24, "lk1", "lk2", "lk3")
    sb(U16, 2 * K24, "lu0", "lu1", "lu2", "lu3", "lv0", "lv1", "lv2")
    sb(U16, 4 * K24, "la0", "la1", "la2", "of")
    sb(F32, 3 * K24, "hd0", "hd1", "hd2", "ho0", "ho1", "ho2")
    sb(F32, K24, "dif0", "dif1", "dif2", "tt", "ud")
    sb(BF, 2 * C, "t0", "t1", "t2", "g0", "g1", "g2")
    sb(BF, 3 * C + 32, "wm0", "wm1", "wm2")
    sb(BF, C, "dn", "qn", "on", "mn", "ln")
    sb(F16, C, "ow", "mw", "lw")
    sb(U16, K24, "d0", "d1", "d2", "kin1", "kin2", "kin3")
    sb(U16, K12, "mu")
    sb(U16, 4 * K12, "mo1", "mo2", "mo3", "min1", "min2", "min3")
    sb(F32, C, "yo")
    sb(BF, HC, "ts", "tw")
    sb(F32, 2 * C, "lro")
    for i in range(8):
        s["ps%d" % i] = ("psum", [128, 512], F32)
    return s


SCRATCH = _buffers()
SEMAPHORES = ["cv", "cs", "ct", "cg", "left", "out"]
SEMAPHORES += ["i%d" % i for i in range(8)]
SEMAPHORES += ["pa%d_%d" % (r, h) for r in (1, 2, 3) for h in range(len(MEANS) - 1)]
SEMAPHORES += [n + "%d" % r for r in (1, 2, 3) for n in ("rk", "rm", "rc")]

BY_ROUND = ("x", "hq", "hs", "dq", "ds", "lk", "lu", "lv", "la", "hd", "dif", "kin", "mo", "min")
COMPUTE = {"v": "cv", "s": "cs", "t": "ct", "g": "cg"}


def rank_program(g, core, T, topo):
    rank = T.rank_of(core)
    if rank is None:
        return
    queue = {"v": g.vector, "s": g.scalar, "t": g.tensor, "y": g.sync, "g": g}
    seen = {}

    def A(name, lo=0, hi=None, step=1):
        t = T[name]
        n = t.shape[1]
        hi = n if hi is None else hi
        ap = t[:, lo:hi] if step == 1 else t[:, lo:hi:step]
        return (ap, [(name, lo, lo + (hi - lo - 1) // step * step + 1, step)])

    def U8(name, lo, hi):
        return (T[name][:, lo:hi].bitcast(dt.uint8), [(name, lo, hi, 1)])

    def IND(win, off, a, b, lo=0, hi=None):
        hi = T[win].shape[1] if hi is None else hi
        return (T[win][:, lo:hi].indirect(T[off][:, a:b]), [(win, lo, hi, 1), (off, a, b, 1)])

    nodes = []
    now = [0]
    behind = []

    def plain(name):
        return name[:-1] if name[:-1] in BY_ROUND and name[-1].isdigit() else name

    def hint(q, writes, reads):
        name, lo = (plain(writes[0][0]), writes[0][1]) if writes else ("", 0)
        table = WHEN if now[0] else FRONT
        for key in ("%s %s %d" % (q, name, lo), "%s %s" % (q, name), "%s by %s" % (q, reads[0][0] if reads else "")):
            if key in table:
                return table[key] + (START + PERIOD * (now[0] - 1) if now[0] else 0.0)
        return 0.0

    def clash(p, q):
        return p[0] < q[1] and q[0] < p[1] and (p[0] - q[0]) % math.gcd(p[2], q[2]) == 0

    def add(q, call, outs, ins, sem, inc, cost, move=None, after=()):
        reads = [r for _, regs in ins for r in regs]
        writes = [r for _, regs in outs for r in regs]
        me = len(nodes)
        deps = {n: True for n in after}
        while behind:
            deps[behind.pop()] = False
        for w, regs in ((False, reads), (True, writes)):
            for name, lo, hi, step in regs:
                bank = name[:2] == "ps"
                for (reg, rw, n) in seen.get(name, ()):
                    other = nodes[n]
                    if not (w or rw or (bank and other["q"] != q)):
                        continue
                    if bank or clash(reg, (lo, hi, step)):
                        strong = other["q"] != q or other["move"] is not None or rw
                        deps[n] = deps.get(n, False) or strong
        for w, regs in ((False, reads), (True, writes)):
            for name, lo, hi, step in regs:
                seen.setdefault(name, []).append(((lo, hi, step), w, me))
        nodes.append({"q": q, "call": call, "deps": deps, "sem": sem, "inc": inc, "cost": cost, "move": move, "when": hint(q, writes, reads),
                      "kind": (q,) + tuple((plain(name), lo, hi) for name, lo, hi, step in writes + reads)})
        return me

    def width(regs):
        name, lo, hi, step = regs[0]
        return (hi - lo + step - 1) // step

    def narrow(regs):
        return SCRATCH[regs[0][0]][2] in (BF, F16, U16)

    def op(q, call, outs, ins, pairs=False, flat=False, product=False):
        n = width(outs[0][1])
        if product:
            cost = (0.0, n + 16, 2)
        elif flat:
            cost = (0.0, (0.012 + 0.00022 * width(ins[0][1])) / CYCLE, 0)
        elif any(len(a[1]) > 1 for a in ins):
            cost = (0.06, n, 1)
        elif q == "s":
            cost = (0.06, n, 0)
        elif q == "g":
            cost = (0.15, 2 * n, 0)
        else:
            both = all(narrow(a[1]) for a in ins + outs if width(a[1]) > 1)
            per = 2.0 if pairs and ins[0][1][0][0][:2] != "ps" else 0.5 if both and not pairs else 1.0
            cost = (0.0, max(64, n * per), 0)
        return add(q, lambda: call().then_inc(T.sem[COMPUTE[q]], 1), outs, ins, COMPUTE[q], 1, cost)

    def bytes_of(regs):
        return width(regs) * {PLN: 1, BF: 2, U16: 2}.get(SCRATCH[regs[0][0]][2], 4)

    def load(q, out, in_, sem, after=(), rows=8, **kw):
        size = bytes_of(out[1] or in_[1]) * (2 if kw else 1)
        return add(q, lambda: queue[q].dma_start(out[0], in_[0], **kw).then_inc(T.sem[sem], 16), [out], [in_], sem, 16,
                   (0.0, ISSUE / CYCLE, 5) if q == "g" else (0.05, 0, 0), (LOCAL, rows, q, size / NEAR), after)

    def X(ap):
        return (ap, [])

    def send(out, in_, dst, rsem):
        rid, pid = topo.addr(dst)[:2]
        n = len(topo.engines(core, dst))
        me = add("g", lambda: g.remote_dma(out_ap=out[0], in_ap=in_[0], remote_sem=T.sem[rsem], local_sem=T.sem["left"],
                                           pid=pid, routing_id=rid, dma_engine_mask=topo.mask(core, dst)),
                 [], [in_], "left", n, (0.0, ISSUE / CYCLE, 5), (REMOTE, 128 // n, "far", bytes_of(in_[1]) / FAR))
        return me, (out, rsem, len(topo.engines(dst, core)))

    def landed(sends):
        add("far", None, [s[1][0] for s in sends], [], sends[0][1][1], sum(s[1][2] for s in sends), (0.0, 0, 0), None, [s[0] for s in sends])

    def plan():
        count = len(nodes)
        if KEPT:
            return KEPT
        direct, above, ended = [], [], []
        for n in nodes:
            over, done = 0, 0
            for d, strong in n["deps"].items():
                over |= above[d]
                done |= ended[d]
            direct.append([(d, strong) for d, strong in n["deps"].items() if not (done if strong else over) >> d & 1])
            for d, strong in n["deps"].items():
                over |= 1 << d
                done |= strong << d
            above.append(over)
            ended.append(done)
        lane, moves = [n["q"] for n in nodes], [n["move"] for n in nodes]
        busies = [[n["cost"][0] + n["cost"][1] * CYCLE * k[n["cost"][2]] for n in nodes] for k in CLOCKS]
        waits = [[[(d, strong, k[8 if lane[d] == "far" else 3] if strong and lane[i] != "far" else 0.0) for d, strong in direct[i]] for i in range(count)] for k in CLOCKS]

        def ends(order, same=0, old=None):
            total, held, new = 0.0, [], []
            last, mover, left = {}, None, dict(ONCE)
            for i in order[:same]:
                last[lane[i]] = i
                if moves[i]:
                    mover = i
                    left.pop(moves[i][2], 0.0)
            last.pop("far", 0)
            for c, (k, busy, wait_of) in enumerate(zip(CLOCKS, busies, waits)):
                done, there, why = [list(a) for a in old[c]] if same else ([0.0] * (count + 1), [0.0] * count, [count] * count)
                new.append((done, there, why))
                engines, once, free, moving = there[mover] if mover is not None else 0.0, dict(left), dict(last), mover
                for i in order[same:]:
                    cause = free.get(lane[i], count)
                    at = done[cause]
                    for d, strong, wait in wait_of[i]:
                        t = there[d] + wait if strong else done[d]
                        if t > at:
                            at, cause = t, d
                    why[i] = cause
                    if moves[i]:
                        at += once.pop(moves[i][2], 0.0)
                        if engines > at + k[4] * moves[i][0]:
                            why[i] = moving
                        engines = there[i] = max(engines, at + k[4] * moves[i][0]) + moves[i][1] * (k[6] + k[7] * moves[i][3])
                        done[i], moving = at + busy[i], i
                    else:
                        done[i] = there[i] = at + busy[i]
                    if busy[i]:
                        free[lane[i]] = i
                i = there.index(max(there))
                total += math.log(there[i])
                while why[i] < count:
                    if not above[i] >> why[i] & 1:
                        held.append((why[i], i))
                    i = why[i]
            return total, held, new

        turn, kinds, like = [], {}, []
        for i, n in enumerate(nodes):
            turn.append(max([n["when"]] + [turn[d] + (0.02 if strong else 0.001) for d, strong in direct[i]]))
            kinds.setdefault(n["kind"], []).append(i)
            like.append((kinds[n["kind"]], len(kinds[n["kind"]]) - 1))
        order = sorted(range(count), key=lambda i: (turn[i], i))
        seed, (end, held, clocks) = SEED, ends(order)
        least = (end, order)
        for t in range(TRIES):
            seed = (seed * 1103515245 + 12345) % 2147483648
            j, i = held[(seed >> 8) % len(held)]
            ahead = seed >> 20 & 1
            if not seed >> 22 & 3:
                a = order.index(j if ahead else i)
                mates = [k for k in (order[max(0, a - 24):a][::-1] if ahead else order[a + 1:a + 25]) if lane[k] == lane[order[a]]]
                j, i = ((mates + [j])[0], i) if ahead else (j, (mates + [i])[0])
            pairs, new, same = [(j, i)], order, count
            if seed >> 21 & 1:
                (J, a), (I, e) = like[j], like[i]
                pairs = [(J[a + s], I[e + s]) for s in range(-min(a, e), min(len(J) - a, len(I) - e))]
            for j, i in pairs:
                a, e = new.index(j), new.index(i) + 1
                if a >= e or above[i] >> j & 1:
                    continue
                same = min(same, a)
                if ahead:
                    moved = [k for k in new[a:e] if k == i or above[i] >> k & 1]
                    new = new[:a] + moved + [k for k in new[a:e] if k not in moved] + new[e:]
                else:
                    moved = [k for k in new[a:e] if k == j or above[k] >> j & 1]
                    new = new[:a] + [k for k in new[a:e] if k not in moved] + moved + new[e:]
            if same == count:
                continue
            result = ends(new, same, clocks)
            if result[0] < end - HEAT * COOL ** (t / TRIES) * math.log(((seed >> 3 & 1023) + 1) / 1024.0):
                (end, held, clocks), order = result, new
                if end < least[0]:
                    least = (end, order)
        KEPT.extend(least[1])
        return KEPT

    def issue(sequence):
        known = {q: {} for q in list(queue) + ["far"]}
        total, value, clock = {}, {}, {}
        for i in sequence:
            n = nodes[i]
            best = {}
            for d, strong in n["deps"].items():
                sem = nodes[d]["sem"]
                if strong and known[n["q"]].get(sem, 0) < value[d] and (sem not in best or value[best[sem]] < value[d]):
                    best[sem] = d
            if n["call"] is not None:
                for sem, d in best.items():
                    if any(s2 != sem and clock[d2].get(sem, 0) >= value[d] for s2, d2 in best.items()):
                        continue
                    queue[n["q"]].wait_ge(T.sem[sem], value[d])
                    k = known[n["q"]]
                    for s, v in list(clock[d].items()) + [(sem, value[d])]:
                        if v > k.get(s, 0):
                            k[s] = v
                n["call"]()
            total[n["sem"]] = total.get(n["sem"], 0) + n["inc"]
            value[i] = total[n["sem"]]
            clock[i] = dict(known[n["q"]]) if n["call"] is not None else {}
        for sem in sorted(total, key=lambda s: s == "out"):
            if max(k.get(sem, 0) for k in known.values()) < total[sem]:
                g.wait_ge(T.sem[sem], total[sem])

    def ts(out, a, s1, o1, s2=None, o2=None):
        k1, k2 = (s[0] if isinstance(s, tuple) else s for s in (s1, s2))
        ins = [a] + [s for s in (s1, s2) if isinstance(s, tuple)]
        if o2 is None:
            return op("v", lambda: g.vector.tensor_scalar(out[0], a[0], k1, None, o1), [out], ins)
        return op("v", lambda: g.vector.tensor_scalar(out[0], a[0], k1, k2, o1, o2), [out], ins)

    def tt(out, a, b, o):
        return op("v", lambda: g.vector.tensor_tensor(out[0], a[0], b[0], o), [out], [a, b], pairs=True)

    def vcopy(out, a):
        return op("v", lambda: g.vector.tensor_copy(out[0], a[0]), [out], [a])

    def fill(out, value):
        return op("v", lambda: g.vector.memset(out[0], value), [out], [])

    def act(out, a, func=AF.Copy, scale=1.0, bias=0.0):
        more = {k: v for k, v, d in (("bias", bias, 0.0), ("scale", scale, 1.0)) if v != d}
        return op("s", lambda: g.scalar.activation(out[0], a[0], func, **more), [out], [a])

    def times(q, out, a, factor=1.0):
        if q == "s":
            act(out, a, scale=factor)
        elif factor == 1.0:
            vcopy(out, a)
        else:
            ts(out, a, factor, OP.mult)

    def scan(out, d0, d1, first, o0, o1):
        return op("v", lambda: g.vector.tensor_tensor_scan(out[0], d0[0], d1[0], first, o0, o1), [out], [d0, d1])

    def wrap(out, data, lift):
        scan(out, data, A(lift, 0, width(data[1])), LOW, OP.max, OP.add)

    def quant(code, plane, a):
        return op("v", lambda: g.vector.quantize_mx(code[0], plane[0], a[0]), [code, plane], [a], flat=True)

    def mm(bank, lhs, lhs_s, a, rhs, rhs_s, lo, hi):
        out, w, ws_ = A(bank, 0, hi - lo), A(lhs, a, a + 128), A(lhs_s, a, a + 128)
        x, xs_ = A(rhs, lo, hi), A(rhs_s, lo, hi)
        return op("t", lambda: g.tensor.matmul_mx(out[0], w[0], ws_[0], x[0], xs_[0], True, True), [out], [w, ws_, x, xs_], product=True)

    def iota(out, pattern, cm, base=0, small=False):
        if small:
            op("g", lambda: g.iota(out[0], pattern, base, cm, allow_small_or_imprecise_dtypes=True), [out], [])
        else:
            op("g", lambda: g.iota(out[0], pattern, base, cm), [out], [])

    def W16(name, lo=0, hi=C):
        return A(name, lo + 15, hi, 16)

    def W4(name, lo=0, hi=C):
        return A(name, lo + 3, hi, 4)

    def SLOT(name, i):
        return A(name, i, 3 * K24, 3)

    def runs(bounds):
        return list(zip(bounds, bounds[1:]))

    load("y", A("ut"), X(T.u[:]), "i0")
    load("y", A("lk0", 0, K24), X(T.gl[:]), "i3")
    load("y", A("lk0", K24, 2 * K24), X(T.gk[:]), "i1")
    for (bank, lo, hi), sem in zip(FIRST, ("i2", "i7")):
        load("y", A("x0", 4 * lo, 4 * hi), X(T.x[:, 4 * lo:4 * hi]), sem)
    behind.extend(range(len(nodes)))
    behind.append(load("y", U8("wq", 0, 512), X(T.wc[:]), "i4"))
    load("y", A("wp"), X(T.ws[:]), "i5")

    iota(A("pos", 0, 16), [[-1, 16]], 1, base=16)
    iota(A("pos", 16, 32), [[0, 4], [-4, 4]], 1, base=16)
    iota(A("pi"), [[0, K24]], 1)
    iota(A("ulist"), [[1, 2], [16, 8]], 0)
    ts(A("pe", 0, 16), A("pos", 0, 16), 15, OP.bitwise_and)
    ts(A("pe", 16, 32), A("pos", 16, 32), 2, OP.logical_shift_right, 3, OP.bitwise_and)
    ts(A("pa"), A("pe"), 0.0, OP.is_equal)
    ts(A("pb"), A("pe"), 1.0, OP.is_equal)
    tt(A("pat"), A("pa"), A("pb"), OP.subtract)
    ts(A("pat", 15, 32, 4), A("pa", 15, 32, 4), -2.0, OP.add)
    ts(A("pm"), A("pi"), 15, OP.bitwise_and)
    ts(A("pq"), A("pi", 0, 1), 3, OP.bitwise_and)
    vcopy(A("pm16"), A("pm"))
    vcopy(A("ulist16"), A("ulist"))
    act(A("w16"), IND("pat", "pm16", 0, K24, 0, 16))
    act(A("w4"), IND("pat", "pm16", 0, K24, 16, 32))
    ts(A("col", 0, 1), A("pq"), 4 * (UNIT + HC), OP.add)
    ts(A("col", 1, 2), A("pq"), float(C), OP.mult, UNIT + HC, OP.add)
    fill(A("one"), 1.0)
    fill(A("et"), 0.0)
    eye = A("et", 3, 515, 4)
    op("g", lambda: g.affine_select(eye[0], T.one[:], [[-1, 128]], OP.is_equal, 0.0, 0, 1), [eye], [A("one")])
    for b in range(4):
        quant(A("eq", 128 * b, 128 * b + 128), A("es", 128 * b, 128 * b + 128), A("et", 3 - b, 515 - b))
    iota(A("q16"), [[16, K24]], 0)
    iota(A("nat"), [[1, C]], 0, base=-HC, small=True)
    tt(A("cw"), A("pm"), A("q16"), OP.add)
    fill(A("t0", 0, 2 * C, 2), 0.0)
    for t in range(3):
        fill(A("wm%d" % t, 32, None, 48), 0.0)

    def partner(r):
        return T.cores[rank ^ MASK[r - 1]]

    def send_children(r):
        landed([send(A("kin%d" % r), A("lu%d" % (r - 1), K24, 2 * K24), partner(r), "rk%d" % r)])

    def elements(out, data, wrapped, lo, hi):
        wrap(A(wrapped, lo, hi), A(data, lo, hi), "w4")
        ts(A(out, lo // 4, hi // 4), W4(wrapped, lo, hi), 4.0 * UNIT, OP.mult, A("col", 0, 1), OP.add)

    def lists_of(n):
        L, hd, dif = "lk%d" % n, "hd%d" % n, "dif%d" % n
        vcopy(A("lu%d" % n), A(L))
        if n == 0:
            for t in range(4):
                ts(A("la0", K24 * t, K24 * (t + 1)), A(L, 0, K24), 4.0, OP.mult, float(t), OP.add)
        else:
            act(A("ln"), IND("nat", "lu%d" % n, 0, K24), scale=1.0 / UNIT)
            elements("la%d" % n, "ln", "lw", 0, C)
        ts(A("lv%d" % n), A(L), 2.0, OP.mult, 1.0, OP.add)
        tt(SLOT(hd, 0), A(L, K24, 2 * K24), A("cw"), OP.subtract)
        tt(SLOT(hd, 1), A(L, 0, K24), A("cw"), OP.subtract)
        vcopy(SLOT(hd, 2), A(L, 0, K24))
        tt(A(dif, 0, K12), A(L, 3 * K12, 4 * K12), A(L, 0, K12), OP.subtract)
        tt(A(dif, K12, K24), A(L, 2 * K12, 3 * K12), A(L, K12, 2 * K12), OP.subtract)

    def exchange(r):
        L, Ln = "lk%d" % (r - 1), "lk%d" % r
        mm("ps6", "uq2", "us2", 128, "xq", "xs", 0, HC)
        act(A("ts"), A("ps6", 0, HC), AF.Sign, scale=-1.0)
        wrap(A("tw"), A("ts"), "w16")
        for i in range(2):
            ts(A("tt", K12 * i, K12 * (i + 1)), W16("tw", 0, HC), -0.5, OP.is_gt)
        tt(A("ud"), A("tt"), A("dif%d" % (r - 1)), OP.mult)
        tt(A(Ln, 0, K24), A(L, 0, K24), A("ud"), OP.add)
        tt(A(Ln, 3 * K12, 4 * K12), A(L, 3 * K12, 4 * K12), A("ud", 0, K12), OP.subtract)
        tt(A(Ln, 2 * K12, 3 * K12), A(L, 2 * K12, 3 * K12), A("ud", K12, K24), OP.subtract)
        if r < ROUNDS:
            lists_of(r)
            send_children(r + 1)
        else:
            vcopy(A("lu%d" % r), A(Ln))
            act(A("lro"), IND("nat", "lu%d" % r, 0, 2 * K24), AF.Identity, bias=float(HC))
            load("y", X(T.lr[:]), (T.lro[0:128:16, :], [("lro", 0, 2 * C, 1)]), "out", rows=1)

    quant(A("uq"), A("us"), A("ut"))
    for h in (0, 1):
        src = (T.uq[:, 0:128].bitcast(dt.uint32).indirect(T.ulist16[:, 8 * h:8 * h + 8]), [("uq", 0, 128, 1), ("ulist16", 0, 16, 1)])
        vcopy((T.uq2[:, 128 * h:128 * h + 128].bitcast(dt.uint32), [("uq2", 128 * h, 128 * h + 128, 1)]), src)
        act(A("us2", 128 * h, 128 * h + 128),
            (T.us[:, 0:128].indirect(T.ulist16[:, 8 * h:8 * h + 8]), [("us", 0, 128, 1), ("ulist16", 0, 16, 1)]))
    lists_of(0)
    send_children(1)
    load("g", A("vt"), X(T.v[:]), "i6")

    def signs(x, bank, lo, hi):
        quant(A("xq", lo, hi), A("xs", lo, hi), A(x, 4 * lo, 4 * hi))
        mm(bank, "uq2", "us2", 0, "xq", "xs", lo, hi)
        ts(A("t0", 2 * lo + 1, 2 * hi, 2), A(bank, 0, hi - lo), 0.0, OP.is_le, 1.0, OP.add)

    def result(q, bank, code, plane, lo, hi, end):
        quant(A(code, lo, hi), A(plane, lo, hi), A("x%d" % ROUNDS, 4 * lo, 4 * hi))
        mm(bank, "vq", "vs", 0, code, plane, lo, hi)
        times(q, A("yo", lo, end), A(bank, 0, end - lo))

    def stores(code, plane, lo, hi):
        load("y", X(T.oc[:, 4 * lo:4 * hi]), U8(code, lo, hi), "out")
        for k in range(4):
            load(OSC[k], X(T.osc[4 * k:4 * k + 4, lo:hi]), (T[plane][32 * k:32 * k + 4, lo:hi], [(plane, lo, hi, 1)]), "out", rows=1)
        load("y", X(T.y[:, lo:hi]), A("yo", lo, hi), "out")

    def step(r, t):
        table, pair, lv, masks = "t%d" % t, "g%d" % t, "lv%d" % (r - 1), "wm%d" % t
        for lo, hi in runs(RUNS):
            act(A(pair, 2 * lo, 2 * hi, 2), IND(table, lv, lo // 16, hi // 16), AF.Abs, bias=-2.0)
            ts(A(pair, 2 * lo + 1, 2 * hi, 2), IND(table, lv, K24 + lo // 16, K24 + hi // 16), 2.0, OP.is_equal)
            if t < 2:
                scan(A("t%d" % (t + 1), 2 * lo, 2 * hi), A(pair, 2 * lo, 2 * hi), A("t0", 2 * lo, 2 * hi), 4.0, OP.min, OP.add)
        for lo, hi in runs(RUNS if t == 2 else (0, C)):
            wrap(A(masks, 3 + 3 * lo, 3 + 3 * hi, 3), A(pair, 2 * lo + 1, 2 * hi, 2), "w16")
            wrap(A(masks, 19 + 3 * lo, 19 + 3 * hi, 3), A(pair, 2 * lo, 2 * hi, 2), "w16")
        scan(A("ho%d" % t), A(masks, 32, None, 16), A("hd%d" % (r - 1)), 0.0, OP.mult, OP.add)
        vcopy(A("d%d" % t), SLOT("ho%d" % t, 2))

    for r in range(1, ROUNDS + 1):
        x, xn = "x%d" % (r - 1), "x%d" % r
        now[0] = r
        for bank, lo, hi in (FIRST if r == 1 else SIGNS[1:]):
            signs(x, bank, lo, hi)
        exchange(r)
        for q, lo, hi in (SUMS if r > 1 else ()):
            times(q, A("pp", 4 * lo, 4 * hi), IND(x, "la%d" % (r - 1), lo // 4, hi // 4))
        for q, lo, hi in (PLANES if r == 1 else ()):
            for t in range(4):
                times(q[t], A("pp", 4 * lo + t, 4 * hi, 4), IND(x, "la0", K24 * t + lo // 16, K24 * t + hi // 16))
        for h, (lo, hi) in enumerate(runs(MEANS)):
            load("g", A("pp", 4 * lo, 4 * hi), A(x, 4 * lo, 4 * hi), "pa%d_%d" % (r, h), accum_op=OP.add)
        for t in range(3):
            step(r, t)
        act(A("dn"), IND("nat", "d0", 0, K24), scale=1.0 / UNIT)
        for q, lo, hi in FOLLOW:
            times(q, A("qn", lo, hi), IND("dn", "d1", lo // 16, hi // 16))
        for q, lo, hi in POINT:
            times(q, A("on", lo, hi), IND("qn", "d2", lo // 16, hi // 16))
            elements("of", "on", "ow", lo, hi)
        for h, (lo, hi, mid) in enumerate(PIECES):
            for q, a, e in (("v", lo, mid), ("s", mid, hi)):
                times(q, A("zt", 4 * a, 4 * e), IND("pp", "of", a // 4, e // 4), 0.5)
            quant(A("zq", lo, hi), A("zs", lo, hi), A("zt", 4 * lo, 4 * hi))
        last = None
        for i, (h, b) in enumerate(PRODUCTS):
            lo, hi, mid = PIECES[h]
            behind.extend([last] if i else [])
            last = mm("ps%d" % (i % 8), "wq", "wp", 128 * b, "zq", "zs", lo, hi)
            times(COPIES[i], A("h", C * b + lo, C * b + hi), A("ps%d" % (i % 8), 0, hi - lo), 0.03125)
        for lo, hi in runs((0, HC, C)):
            act(A("mn", lo, hi), IND("on", "kin%d" % r, lo // 16, hi // 16))
        wrap(A("mw", 0, HC), A("mn", 0, HC), "w16")
        ts(A("mu"), W16("mw", 0, HC), UNIT, OP.mult, UNIT + HC, OP.add)
        wrap(A("mw", HC, C), A("mn", HC, C), "w4")
        ts(A("mo%d" % r), W4("mw", HC, C), UNIT, OP.mult, A("col", 1, 2), OP.add)
        places = send(A("min%d" % r), A("mo%d" % r), partner(r), "rm%d" % r)
        landed([places])
        for b in range(4):
            for q, lo, hi in (("v", 0, PARTS[b]), ("s", PARTS[b], HC)):
                if hi > lo:
                    times(q, A("ht", 4 * lo + b, 4 * hi, 4), IND("h", "mu", lo // 16, hi // 16, C * b, C * (b + 1)))
        quant(A("hq%d" % r), A("hs%d" % r), A("ht"))
        behind.append(places[0])
        codes = send(U8("dq%d" % r, 0, HC), U8("hq%d" % r, 0, HC), partner(r), "rc%d" % r)
        behind.append(codes[0])
        plane = send(A("ds%d" % r), A("hs%d" % r), partner(r), "rc%d" % r)
        landed([codes, plane])
        tt(A(xn, 4 * HC, 4 * C), IND("h", "min%d" % r, 0, 4 * K12), A(x, 4 * HC, 4 * C), OP.add)
        if r == 2:
            quant(A("vq"), A("vs"), A("vt"))
        bank, lo, hi = SIGNS[0]
        if r < ROUNDS:
            signs(xn, bank, lo, hi)
        else:
            result("s", bank, "xq", "xs", HC, C, C)
            stores("xq", "xs", HC, C)
        for b in range(4):
            mm("ps%d" % b, "eq", "es", 128 * b, "dq%d" % r, "ds%d" % r, 0, HC)
            for bank, a, e in SIGNS[1:]:
                e = min(e, HC)
                tt(A(xn, 4 * a + b, 4 * e, 4), A("ps%d" % b, a, e), A(x, 4 * a + b, 4 * e, 4), OP.add)

    for q, (bank, a, e) in zip("sv", SIGNS[1:]):
        result(q, bank, "zq", "zs", a, e, min(e, HC))
    stores("zq", "zs", 0, HC)
    issue(plan())
